import numpy as np
import ml_dtypes


def mxq(x, axis, fmt="e4m3"):
    dtype, down = {"e4m3": (ml_dtypes.float8_e4m3fn, 7), "e5m2": (ml_dtypes.float8_e5m2, 14)}[fmt]
    v = np.moveaxis(np.asarray(x, np.float32).astype(ml_dtypes.bfloat16).astype(np.float64), axis, -1)
    blocks = v.reshape(v.shape[:-1] + (-1, 32))
    amax = np.abs(blocks).max(-1, keepdims=True)
    byte = np.maximum(np.where(amax > 0, np.frexp(amax)[1] - 1 + 127, 0) - down, 1)
    scale = np.exp2(byte - 127.0)
    codes = (blocks / scale).astype(np.float32).astype(dtype).astype(np.float64)
    return np.moveaxis((codes * scale).reshape(v.shape), -1, axis)


WIDE = False


def mx_kscale(k):
    if not WIDE:
        return np.ones(k)
    levels = np.array([10, -10, 5, -5, 0])
    if k % 512:
        return np.exp2(np.random.permutation(np.resize(levels, k // 32))).repeat(32)
    a = np.empty((k // 512, 16))
    for p in range(k // 512):
        a[p, :8] = np.random.permutation(np.resize(levels, 8))
        for g in range(8):
            far = levels[np.abs(levels - a[p, g]) >= 10]
            a[p, g + 8] = far[np.random.randint(len(far))]
    return np.exp2(a.ravel()).repeat(32)


BF16 = ml_dtypes.bfloat16


def bf(x):
    return np.asarray(x, np.float32).astype(BF16)


def f64(x):
    return np.asarray(x).astype(np.float64)


N, Q, R = 1024, 1024, 512


def draw0():
    t = mx_kscale(Q)
    u = mx_kscale(R)
    r = mx_kscale(N)
    return {
        "x1": bf(np.random.standard_normal((N, Q))),
        "x2": bf(np.random.standard_normal((N, R))),
        "w1": bf(np.random.standard_normal((Q, R)) / np.sqrt(Q) / t[:, None]),
        "v1": bf(np.random.standard_normal((R, Q)) / np.sqrt(R) / u[:, None]),
        "g": bf((1.0 + 0.1 * np.random.standard_normal(Q)) * t),
        "pi2": bf(np.random.uniform(0.5, 1.5, R) * u),
        "a": bf((1.0 + 0.1 * np.random.standard_normal(N)) * r),
        "c": bf((1.0 + 0.1 * np.random.standard_normal(N)) / r),
    }


def core(x1, x2, w1, v1, g, pi2, a, c):
    x1, x2, w1, v1 = f64(x1), f64(x2), f64(w1), f64(v1)
    g, pi2, a, c = f64(g), f64(pi2), f64(a), f64(c)
    n = x1.shape[0]
    f = np.tanh(x1)
    mu = mxq(f * g[None, :], 1, "e4m3") @ mxq(w1, 0, "e4m3")
    eps = x2 - mu
    back = mxq(eps * pi2[None, :], 1, "e4m3") @ mxq(v1, 0, "e4m3")
    x1_new = x1 + 0.5 * (-x1 + (1.0 - f * f) * back)
    dw1 = (mxq(f * a[:, None], 0, "e4m3").T @ mxq(eps * c[:, None], 0, "e4m3")) / np.sqrt(n)
    return x1_new, dw1


def e4m3fn_bytes(y):
    return np.clip(np.asarray(y, np.float64), -448.0, 448.0).astype(np.float32).astype(ml_dtypes.float8_e4m3fn).view(np.uint8)


def e4m3fn_values(b):
    return np.asarray(b, np.uint8).view(ml_dtypes.float8_e4m3fn).astype(np.float64)


def setup_inputs():
    d = draw0()
    x0 = np.asarray(d['w1']).astype(np.float64)
    s = (np.max(np.abs(x0), axis=(1,), keepdims=True) / 448.0).astype(np.float32)
    out = {}
    for k, v in d.items():
        if k == 'w1':
            out['w1_bytes'] = e4m3fn_bytes(x0 / s.astype(np.float64))
            out['w1_scale'] = s
        else:
            out[k] = v
    return out


def reference(x1, x2, w1_bytes, w1_scale, v1, g, pi2, a, c):
    return core(x1, x2, e4m3fn_values(w1_bytes) * w1_scale.astype(np.float64), v1, g, pi2, a, c)

@@ -1,0 +1,410 @@
+from contextlib import ExitStack
+
+import concourse.mybir as mybir
+from concourse.masks import make_identity
+
+N, Q, R = 1024, 1024, 512
+P = 128
+FLOPS = 3 * 2 * N * Q * R
+
+F32 = mybir.dt.float32
+BF16 = mybir.dt.bfloat16
+U32 = mybir.dt.uint32
+U8 = mybir.dt.uint8
+FP8 = mybir.dt.float8_e4m3fn
+FP8X4 = mybir.dt.float8_e4m3fn_x4
+ALU = mybir.AluOpType
+ACT = mybir.ActivationFunctionType
+
+HALF_ROOT = 0.5 ** 0.5
+GC = 704
+ON_G = (0, 1, 2, 3)
+
+
+def tile_incrementalpredictivecodingupdate_kernel(tc, x1, x2, w1_bytes, w1_scale, v1, g, pi2, a, c, out_0, out_1):
+    nc = tc.nc
+    x1v = x1.rearrange("(g p t) q -> g p t q", p=P, t=4)
+    x2v = x2.rearrange("(g p t) r -> g p t r", p=P, t=4)
+    w1v = w1_bytes.rearrange("(g p t) r -> g p t r", p=P, t=4)
+    v1v = v1.rearrange("(p t) q -> p t q", t=4)
+    dwv = out_1.rearrange("(k p u) r -> k u p r", k=2, u=4)
+    xov = out_0.rearrange("(g p t) q -> g p t q", p=P, t=4)
+
+    with ExitStack() as ctx:
+        keep = ctx.enter_context(tc.tile_pool(name="keep", bufs=1))
+        work = ctx.enter_context(tc.tile_pool(name="work", bufs=2))
+        psum = ctx.enter_context(tc.psum_pool(name="psum", bufs=1))
+
+        x1s = keep.tile([P, 2, 4, Q], BF16, name="x1s")
+        x2s = keep.tile([P, 2, 4, R], BF16, name="x2s")
+        w1b = keep.tile([P, 2, 4, R], U8, name="w1b")
+        w1s = keep.tile([P, 2, 4], F32, name="w1s")
+        v1s = keep.tile([P, 4, Q], BF16, name="v1s")
+        gs = keep.tile([P, 2, 4], BF16, name="gs")
+        as_ = keep.tile([P, 2, 4], BF16, name="as_")
+        cs = keep.tile([P, 2, 4], BF16, name="cs")
+        ps = keep.tile([P, 4], BF16, name="ps")
+        ident = keep.tile([P, P], F32, name="ident")
+
+        f = keep.tile([P, 2, 4, Q], F32, name="f")
+        eps = keep.tile([P, 2, 4, R], F32, name="eps")
+        w1p = keep.tile([P, 2, 4, R], BF16, name="w1p")
+        w1i = keep.tile([P, 2, R, 4], BF16, name="w1i", tag="inter", bufs=3, align_bytes=64)
+        v1i = keep.tile([P, Q, 4], BF16, name="v1i", tag="inter", bufs=3, align_bytes=64)
+        fai = []
+        fap = []
+        for k in (0, 1):
+            fai_k = keep.tile([P, Q, 4], BF16, name="fai%d" % k, tag="inter", bufs=3, align_bytes=64)
+            fai.append(fai_k)
+            fap_k = keep.tile([P, 4, Q], BF16, name="fap%d" % k)
+            fap.append(fap_k)
+        w1c = keep.tile([P, 2 * R], U32, name="w1c", align_bytes=64)
+        w1e = keep.tile([P, 2 * R], U8, name="w1e", align_bytes=64)
+        v1c = keep.tile([P, Q], U32, name="v1c", align_bytes=64)
+        v1e = keep.tile([P, Q], U8, name="v1e", align_bytes=64)
+        fac = keep.tile([P, 2 * Q], U32, name="fac", align_bytes=64)
+        fae = keep.tile([P, 2 * Q], U8, name="fae", align_bytes=64)
+        ecc = keep.tile([P, 2 * R], U32, name="ecc", align_bytes=64)
+        ece = keep.tile([P, 2 * R], U8, name="ece", align_bytes=64)
+
+        with tc.manual_schedule():
+            nc.scalar.dma_start(out=w1s[:], in_=w1_scale.rearrange("(g p t) o -> p g (t o)", p=P, t=4))
+            nc.scalar.dma_start(out=gs[:], in_=g.rearrange("(g p t) -> p g t", p=P, t=4))
+            nc.sync.dma_start(out=w1b[:, 0], in_=w1v[0])
+            nc.scalar.dma_start(out=as_[:], in_=a.rearrange("(g p t) -> p g t", p=P, t=4))
+            nc.sync.dma_start(out=w1b[:, 1], in_=w1v[1])
+            nc.sync.dma_start(out=x1s[:, 0, 0, :], in_=x1v[0][:, 0, :])
+            for t in (1, 2, 3):
+                nc.sync.dma_start(out=x1s[:, 0, t, :], in_=x1v[0][:, t, :])
+            nc.sync.dma_start(out=v1s[:, :, 0:512], in_=v1v[:, :, 0:512])
+            nc.sync.dma_start(out=x2s[:, 0], in_=x2v[0])
+            nc.sync.dma_start(out=v1s[:, :, 512:1024], in_=v1v[:, :, 512:1024])
+            for t in (0, 2):
+                nc.sync.dma_start(out=x1s[:, 1, t:t + 2, :], in_=x1v[1][:, t:t + 2, :])
+            nc.sync.dma_start(out=x2s[:, 1], in_=x2v[1])
+            make_identity(nc, ident[:])
+            nc.gpsimd.dma_start(out=ps[:], in_=pi2.rearrange("(p t) -> p t", t=4))
+            nc.gpsimd.dma_start(out=cs[:], in_=c.rearrange("(g p t) -> p g t", p=P, t=4))
+
+            warm = keep.tile([P, 1], F32, name="warm")
+            warm2 = keep.tile([P, 1], F32, name="warm2")
+            nc.vector.memset(warm[:], 0.0)
+            nc.scalar.activation(out=warm2[:], in_=warm[:], func=ACT.Tanh)
+
+            af = keep.tile([P, 2, 4], F32, name="af")
+            nc.gpsimd.tensor_copy(out=af[:], in_=as_[:])
+
+            def tanh(i):
+                nc.scalar.activation(out=f[:, i // 4, i % 4, :].rearrange("p (k u m) -> p k u m", k=2, u=4),
+                                     in_=x1s[:, i // 4, i % 4, :].rearrange("p (k m u) -> p k u m", k=2, u=4), func=ACT.Tanh)
+
+            hs = {}
+
+            def square(i):
+                h = work.tile([P, Q], F32, name="h", bufs=3)
+                for k in (0, 1):
+                    s = slice(k * 512, (k + 1) * 512)
+                    nc.scalar.activation(out=h[:, s].rearrange("p (b j u) -> p b u j", j=4, u=4),
+                                         in_=f[:, i // 4, i % 4, s].rearrange("p (u b j) -> p b u j", u=4, j=4), func=ACT.Square, scale=HALF_ROOT)
+                hs[i] = h
+
+            def warm_up(n):
+                for e in range(n):
+                    idle = psum.tile([P, 512], F32, name="idle", tag="ft", bufs=4)
+                    nc.tensor.matmul(idle[:], lhsT=ecs[1][:, 256:288, :].rearrange("p r t -> p (r t)"), rhs=ecs[1][:, 256:384, :].rearrange("p r t -> p (r t)"), start=True, stop=True)
+
+            fts = {}
+
+            def trans_f(i):
+                for k in (0, 1):
+                    ft = psum.tile([P, 4, P], F32, name="ft", tag="ft", bufs=4)
+                    for t in range(4):
+                        nc.tensor.transpose(ft[:, t, :], f[:, i // 4, i % 4, k * 512 + t * P:k * 512 + (t + 1) * P], ident[:])
+                    fts[i, k] = ft
+
+            fgs = {}
+
+            def mul_g(i):
+                fg = work.tile([P, 2, P, 4], BF16, name="fg", align_bytes=64)
+                for k in (0, 1):
+                    nc.vector.tensor_tensor(out=fg[:, k], in0=fts[i, k][:].rearrange("p t n -> p n t"),
+                                            in1=gs[:, k, :].unsqueeze(1).to_broadcast([P, P, 4]), op=ALU.mult)
+                fgs[i] = fg
+
+            fgq = {}
+
+            def quant_fg(i):
+                cd = work.tile([P, 2 * P], U32, name="fgc", align_bytes=64)
+                sc = work.tile([P, 2 * P], U8, name="fge", align_bytes=64)
+                nc.vector.quantize_mx(out=cd[:].bitcast(FP8X4), scales=sc[:], in_=fgs[i][:].rearrange("p k n t -> p (k n t)"))
+                fgq[i] = (cd, sc)
+
+            mus = {}
+
+            def mm1(i):
+                mu = psum.tile([P, R], F32, name="mu", tag="mu")
+                cd, sc = fgq[i]
+                for k in (0, 1):
+                    nc.tensor.matmul_mx(out=mu[:], lhsT=cd[:, k * P:(k + 1) * P].bitcast(FP8X4), lhsT_scale=sc[:, k * P:(k + 1) * P],
+                                        rhs=w1c[:, k * R:(k + 1) * R].bitcast(FP8X4), rhs_scale=w1e[:, k * R:(k + 1) * R],
+                                        start=(k == 0), stop=(k == 1))
+                mus[i] = mu
+
+            def error(i):
+                nc.vector.tensor_tensor(out=eps[:, i // 4, i % 4, :].rearrange("p (u m) -> p u m", u=4),
+                                        in0=x2s[:, i // 4, i % 4, :].rearrange("p (m u) -> p u m", u=4),
+                                        in1=mus[i][:].rearrange("p (m u) -> p u m", u=4), op=ALU.subtract)
+
+            ets = {}
+
+            def trans_e(i):
+                et = psum.tile([P, 4, P], F32, name="et", tag="et")
+                for t in range(4):
+                    nc.tensor.transpose(et[:, t, :], eps[:, i // 4, i % 4, t * P:(t + 1) * P], ident[:])
+                ets[i] = et
+
+            eps_ = {}
+
+            def mul_p(i):
+                ep = work.tile([P, P, 4], BF16, name="ep", align_bytes=64)
+                nc.vector.tensor_tensor(out=ep[:], in0=ets[i][:].rearrange("p t n -> p n t"),
+                                        in1=ps[:].unsqueeze(1).to_broadcast([P, P, 4]), op=ALU.mult)
+                eps_[i] = ep
+
+            epq = {}
+
+            def quant_ep(i):
+                cd = work.tile([P, P], U32, name="epc", align_bytes=64)
+                sc = work.tile([P, P], U8, name="epe", align_bytes=64)
+                nc.vector.quantize_mx(out=cd[:].bitcast(FP8X4), scales=sc[:], in_=eps_[i][:].rearrange("p n t -> p (n t)"))
+                epq[i] = (cd, sc)
+
+            bks = {}
+
+            def mm2(i):
+                cd, sc = epq[i]
+                for h in (0, 1):
+                    bk = psum.tile([P, 512], F32, name="bk", tag="bk", bufs=2)
+                    nc.tensor.matmul_mx(out=bk[:], lhsT=cd[:].bitcast(FP8X4), lhsT_scale=sc[:],
+                                        rhs=v1c[:, h * 512:(h + 1) * 512].bitcast(FP8X4), rhs_scale=v1e[:, h * 512:(h + 1) * 512],
+                                        start=True, stop=True)
+                    bks[i, h] = bk
+
+            us = {}
+            xh = {}
+
+            def half_x(i):
+                if i in ON_G:
+                    y = work.tile([P, Q], BF16, name="y", bufs=3)
+                    nc.vector.tensor_scalar(out=y[:, :GC], in0=x1s[:, i // 4, i % 4, :GC], scalar1=0.5, scalar2=None, op0=ALU.mult)
+                    xh[i] = y
+
+            def delta(i):
+                u = work.tile([P, Q], F32, name="u", bufs=2)
+                for h in (0, 1):
+                    s = slice(h * 512, (h + 1) * 512)
+                    nc.vector.scalar_tensor_tensor(out=u[:, s], in0=hs[i][:, s], scalar=0.5, in1=bks[i, h][:], op0=ALU.subtract, op1=ALU.mult)
+                us[i] = u
+
+            outs = {}
+
+            def state_rest(i):
+                o = outs[i]
+                if GC < Q:
+                    nc.vector.scalar_tensor_tensor(out=o[:, GC:], in0=x1s[:, i // 4, i % 4, GC:], scalar=0.5, in1=us[i][:, GC:], op0=ALU.mult, op1=ALU.subtract)
+                nc.sync.dma_start(out=xov[i // 4][:, i % 4, :], in_=o[:])
+
+            def state(i):
+                o = work.tile([P, Q], F32, name="o", bufs=3)
+                if i in ON_G:
+                    nc.gpsimd.tensor_tensor(out=o[:, :GC], in0=xh[i][:, :GC], in1=us[i][:, :GC], op=ALU.subtract)
+                    outs[i] = o
+                    return
+                else:
+                    for h in (0, 1):
+                        s = slice(h * 512, (h + 1) * 512)
+                        nc.vector.scalar_tensor_tensor(out=o[:, s], in0=x1s[:, i // 4, i % 4, s], scalar=0.5, in1=us[i][:, s], op0=ALU.mult, op1=ALU.subtract)
+                        nc.sync.dma_start(out=xov[i // 4][:, i % 4, s], in_=o[:, s])
+                    return
+                nc.sync.dma_start(out=xov[i // 4][:, i % 4, :], in_=o[:])
+
+            def scale_fa(i):
+                s = slice(512 if i < 4 else 0, Q)
+                nc.scalar.activation(out=fap[i // 4][:, i % 4, s], in_=f[:, i // 4, i % 4, s], func=ACT.Copy, scale=af[:, i // 4, i % 4:i % 4 + 1])
+
+            def inter(eng_copy, out, in_):
+                eng_copy(out=out.rearrange("p (c i) t -> p c t i", i=4), in_=in_.rearrange("p t (c i) -> p c t i", i=4))
+
+            def inter_fa(k, h):
+                inter(nc.scalar.copy, fai[k][:, h * 256:(h + 1) * 256, :], fap[k][:, :, h * 256:(h + 1) * 256])
+
+            def quant_fa(k, h):
+                o = k * Q + h * 512
+                nc.vector.quantize_mx(out=fac[:, o:o + 512].bitcast(FP8X4), scales=fae[:, o:o + 512],
+                                      in_=fai[k][:, h * 512:(h + 1) * 512, :].rearrange("p q t -> p (q t)"))
+
+            gaps = []
+
+            def gap_piece(k, b, kind):
+                z = work.tile([P, P, 4], BF16, name="z", bufs=1, align_bytes=64)
+                src, gain, codes, scales, width = (eps, cs, ecc, ece, R) if kind == 0 else (f, as_, fac, fae, Q)
+                s = slice(b * P, (b + 1) * P)
+                nc.gpsimd.tensor_tensor(out=z[:], in0=src[:, k, :, s].rearrange("p t q -> p q t"),
+                                        in1=gain[:, k, :].unsqueeze(1).to_broadcast([P, P, 4]), op=ALU.mult)
+                o = k * width + b * P
+                gaps.append((codes[:, o:o + P], scales[:, o:o + P], z))
+
+            def gap_quant():
+                if gaps:
+                    cd, sc, z = gaps.pop(0)
+                    nc.vector.quantize_mx(out=cd.bitcast(FP8X4), scales=sc, in_=z[:].rearrange("p q t -> p (q t)"))
+
+            ecs = {}
+
+            def mul_c(k, h):
+                if h == 0:
+                    ec = work.tile([P, R, 4], BF16, name="ec", align_bytes=64)
+                    ecs[k] = ec
+                s = slice(h * 256, (h + 1) * 256)
+                nc.vector.tensor_tensor(out=ecs[k][:, s, :].rearrange("p (c i) t -> p c t i", i=4),
+                                        in0=eps[:, k, :, s].rearrange("p t (c i) -> p c t i", i=4),
+                                        in1=cs[:, k, :].unsqueeze(1).unsqueeze(3).to_broadcast([P, 64, 4, 4]), op=ALU.mult)
+
+            def quant_ec(k):
+                nc.vector.quantize_mx(out=ecc[:, k * R:(k + 1) * R].bitcast(FP8X4), scales=ece[:, k * R:(k + 1) * R],
+                                      in_=ecs[k][:].rearrange("p r t -> p (r t)"))
+
+            def mm3(m):
+                dw = psum.tile([P, R], F32, name="dw", tag="ft", bufs=4)
+                for k in (0, 1):
+                    o = k * Q + m * P
+                    nc.tensor.matmul_mx(out=dw[:], lhsT=fac[:, o:o + P].bitcast(FP8X4), lhsT_scale=fae[:, o:o + P],
+                                        rhs=ecc[:, k * R:(k + 1) * R].bitcast(FP8X4), rhs_scale=ece[:, k * R:(k + 1) * R],
+                                        start=(k == 0), stop=(k == 1))
+                d = work.tile([P, R], F32, name="d", bufs=8)
+                nc.scalar.activation(out=d[:].rearrange("p (m u) -> p m u", u=4), in_=dw[:].rearrange("p (u m) -> p m u", u=4), func=ACT.Copy, scale=0.03125)
+                nc.sync.dma_start(out=dwv[m // 4, m % 4], in_=d[:])
+
+            def widen_s(k, t):
+                nc.scalar.activation(out=w1p[:, k, t, :], in_=w1b[:, k, t, :].bitcast(FP8), func=ACT.Copy, scale=w1s[:, k, t:t + 1])
+
+            def widen(k, t):
+                nc.vector.tensor_scalar(out=w1p[:, k, t, :], in0=w1b[:, k, t, :].bitcast(FP8), scalar1=w1s[:, k, t:t + 1], scalar2=None, op0=ALU.mult)
+
+            def quant_w1(k):
+                nc.vector.quantize_mx(out=w1c[:, k * R:(k + 1) * R].bitcast(FP8X4), scales=w1e[:, k * R:(k + 1) * R],
+                                      in_=w1i[:, k].rearrange("p r t -> p (r t)"))
+
+            def inter_v1(h):
+                inter(nc.scalar.copy, v1i[:, h * 256:(h + 1) * 256, :], v1s[:, :, h * 256:(h + 1) * 256])
+
+            def quant_v1(h):
+                nc.vector.quantize_mx(out=v1c[:, h * 512:(h + 1) * 512].bitcast(FP8X4), scales=v1e[:, h * 512:(h + 1) * 512],
+                                      in_=v1i[:, h * 512:(h + 1) * 512, :].rearrange("p q t -> p (q t)"))
+
+            widen_s(0, 0)
+            widen_s(0, 1)
+            for i in range(2):
+                tanh(i)
+            for k in (0, 1):
+                for t in range(4):
+                    if (k, t) not in ((0, 0), (0, 1)):
+                        widen(k, t)
+            trans_f(0)
+            inter(nc.vector.tensor_copy, w1i[:, 0], w1p[:, 0])
+            inter(nc.scalar.copy, w1i[:, 1, :256], w1p[:, 1, :, :256])
+            quant_w1(0)
+            inter(nc.vector.tensor_copy, w1i[:, 1, 256:], w1p[:, 1, :, 256:])
+            tanh(2)
+            tanh(3)
+            for q in range(4):
+                inter_v1(q)
+            for i in range(4, 8):
+                tanh(i)
+            side = [(scale_fa, t) for t in range(4)] + [(inter_fa, 0, 2), (inter_fa, 0, 3)] + [(scale_fa, 4 + t) for t in range(4)] + [(inter_fa, 1, h) for h in range(4)]
+            nside = 0
+
+            for s in range(8):
+                j = s - 3
+                if s == 1:
+                    z0 = work.tile([P, P, 4], BF16, name="z", bufs=1, align_bytes=64)
+                    nc.vector.memset(z0[:, 0:1, 0:2], 0.0)
+                if s in (1, 2, 3, 4):
+                    gap_quant()
+                    gap_piece(0, s - 1, 1)
+                mul_g(s)
+                if s < 7:
+                    trans_f(s + 1)
+                if s == 0:
+                    quant_w1(1)
+                if s >= 1:
+                    error(s - 1)
+                if j >= 0:
+                    mul_p(j)
+                if s == 2:
+                    half_x(0)
+                quant_fg(s)
+                mm1(s)
+                if s == 3:
+                    quant_v1(0)
+                    quant_v1(1)
+                if j >= 0:
+                    quant_ep(j)
+                if j >= 2:
+                    state_rest(j - 2)
+                if j + 1 >= 0:
+                    trans_e(j + 1)
+                if j >= 0:
+                    half_x(j + 1)
+                    square(j)
+                while nside < (0, 0, 0, 3, 6, 9, 11, 14)[s]:
+                    side[nside][0](*side[nside][1:])
+                    nside += 1
+                if s >= 4:
+                    gap_quant()
+                    gap_piece(0, s - 4, 0)
+                if j >= 1:
+                    delta(j - 1)
+                    state(j - 1)
+                if j >= 0:
+                    mm2(j)
+            error(7)
+            mul_p(5)
+            square(5)
+            delta(4)
+            gap_quant()
+            quant_ep(5)
+            state_rest(3)
+            trans_e(6)
+            mm2(5)
+            mul_c(1, 0)
+            mul_c(1, 1)
+            warm_up(4)
+            quant_fa(0, 1)
+            quant_fa(1, 0)
+            quant_fa(1, 1)
+            quant_ec(1)
+            square(6)
+            square(7)
+            mul_p(6)
+            state(4)
+            for m in range(2):
+                mm3(m)
+            trans_e(7)
+            for m in range(2, 4):
+                mm3(m)
+            quant_ep(6)
+            delta(5)
+            mm2(6)
+            mul_p(7)
+            state(5)
+            for m in range(4, 6):
+                mm3(m)
+            quant_ep(7)
+            delta(6)
+            mm2(7)
+            state(6)
+            for m in range(6, 8):
+                mm3(m)
+            delta(7)
+            state(7)

@@ -17,8 +17,7 @@ ALU = mybir.AluOpType
 ACT = mybir.ActivationFunctionType
 
 HALF_ROOT = 0.5 ** 0.5
-GC = 704
-ON_G = (0, 1, 2, 3)
+GC = 640
 
 
 def tile_incrementalpredictivecodingupdate_kernel(tc, x1, x2, w1_bytes, w1_scale, v1, g, pi2, a, c, out_0, out_1):
@@ -35,29 +34,23 @@ def tile_incrementalpredictivecodingupdate_kernel(tc, x1, x2, w1_bytes, w1_scale
         work = ctx.enter_context(tc.tile_pool(name="work", bufs=2))
         psum = ctx.enter_context(tc.psum_pool(name="psum", bufs=1))
 
-        x1s = keep.tile([P, 2, 4, Q], BF16, name="x1s")
-        x2s = keep.tile([P, 2, 4, R], BF16, name="x2s")
-        w1b = keep.tile([P, 2, 4, R], U8, name="w1b")
+        x1s = [keep.tile([P, Q], BF16, name="x1s%d" % i) for i in range(8)]
+        x2s = [keep.tile([P, 4, R], BF16, name="x2s%d" % k) for k in (0, 1)]
+        w1b = [keep.tile([P, 4, R], U8, name="w1b%d" % k) for k in (0, 1)]
+        v1s = [keep.tile([P, 4, 512], BF16, name="v1s%d" % h) for h in (0, 1)]
         w1s = keep.tile([P, 2, 4], F32, name="w1s")
-        v1s = keep.tile([P, 4, Q], BF16, name="v1s")
         gs = keep.tile([P, 2, 4], BF16, name="gs")
         as_ = keep.tile([P, 2, 4], BF16, name="as_")
         cs = keep.tile([P, 2, 4], BF16, name="cs")
         ps = keep.tile([P, 4], BF16, name="ps")
+        af = keep.tile([P, 2, 4], F32, name="af")
+        cf = keep.tile([P, 2, 4], F32, name="cf")
         ident = keep.tile([P, P], F32, name="ident")
+        mhalf = keep.tile([P, P], BF16, name="mhalf")
 
-        f = keep.tile([P, 2, 4, Q], F32, name="f")
-        eps = keep.tile([P, 2, 4, R], F32, name="eps")
-        w1p = keep.tile([P, 2, 4, R], BF16, name="w1p")
-        w1i = keep.tile([P, 2, R, 4], BF16, name="w1i", tag="inter", bufs=3, align_bytes=64)
-        v1i = keep.tile([P, Q, 4], BF16, name="v1i", tag="inter", bufs=3, align_bytes=64)
-        fai = []
-        fap = []
-        for k in (0, 1):
-            fai_k = keep.tile([P, Q, 4], BF16, name="fai%d" % k, tag="inter", bufs=3, align_bytes=64)
-            fai.append(fai_k)
-            fap_k = keep.tile([P, 4, Q], BF16, name="fap%d" % k)
-            fap.append(fap_k)
+        f = [keep.tile([P, 4, Q], F32, name="f%d" % k) for k in (0, 1)]
+        eps = [keep.tile([P, 4, R], F32, name="eps%d" % k) for k in (0, 1)]
+        w1p = [keep.tile([P, 4, R], BF16, name="w1p%d" % k) for k in (0, 1)]
         w1c = keep.tile([P, 2 * R], U32, name="w1c", align_bytes=64)
         w1e = keep.tile([P, 2 * R], U8, name="w1e", align_bytes=64)
         v1c = keep.tile([P, Q], U32, name="v1c", align_bytes=64)
@@ -67,82 +60,55 @@ def tile_incrementalpredictivecodingupdate_kernel(tc, x1, x2, w1_bytes, w1_scale
         ecc = keep.tile([P, 2 * R], U32, name="ecc", align_bytes=64)
         ece = keep.tile([P, 2 * R], U8, name="ece", align_bytes=64)
 
+        def bank(b, shape):
+            return psum.tile(shape, F32, name="bank%d" % b)
+
         with tc.manual_schedule():
-            nc.scalar.dma_start(out=w1s[:], in_=w1_scale.rearrange("(g p t) o -> p g (t o)", p=P, t=4))
-            nc.scalar.dma_start(out=gs[:], in_=g.rearrange("(g p t) -> p g t", p=P, t=4))
-            nc.sync.dma_start(out=w1b[:, 0], in_=w1v[0])
-            nc.scalar.dma_start(out=as_[:], in_=a.rearrange("(g p t) -> p g t", p=P, t=4))
-            nc.sync.dma_start(out=w1b[:, 1], in_=w1v[1])
-            nc.sync.dma_start(out=x1s[:, 0, 0, :], in_=x1v[0][:, 0, :])
-            for t in (1, 2, 3):
-                nc.sync.dma_start(out=x1s[:, 0, t, :], in_=x1v[0][:, t, :])
-            nc.sync.dma_start(out=v1s[:, :, 0:512], in_=v1v[:, :, 0:512])
-            nc.sync.dma_start(out=x2s[:, 0], in_=x2v[0])
-            nc.sync.dma_start(out=v1s[:, :, 512:1024], in_=v1v[:, :, 512:1024])
-            for t in (0, 2):
-                nc.sync.dma_start(out=x1s[:, 1, t:t + 2, :], in_=x1v[1][:, t:t + 2, :])
-            nc.sync.dma_start(out=x2s[:, 1], in_=x2v[1])
-            make_identity(nc, ident[:])
-            nc.gpsimd.dma_start(out=ps[:], in_=pi2.rearrange("(p t) -> p t", t=4))
-            nc.gpsimd.dma_start(out=cs[:], in_=c.rearrange("(g p t) -> p g t", p=P, t=4))
-
-            warm = keep.tile([P, 1], F32, name="warm")
-            warm2 = keep.tile([P, 1], F32, name="warm2")
-            nc.vector.memset(warm[:], 0.0)
-            nc.scalar.activation(out=warm2[:], in_=warm[:], func=ACT.Tanh)
-
-            af = keep.tile([P, 2, 4], F32, name="af")
-            nc.gpsimd.tensor_copy(out=af[:], in_=as_[:])
+            def load_x1(i):
+                nc.sync.dma_start(out=x1s[i][:], in_=x1v[i // 4][:, i % 4, :])
 
             def tanh(i):
-                nc.scalar.activation(out=f[:, i // 4, i % 4, :].rearrange("p (k u m) -> p k u m", k=2, u=4),
-                                     in_=x1s[:, i // 4, i % 4, :].rearrange("p (k m u) -> p k u m", k=2, u=4), func=ACT.Tanh)
+                nc.scalar.activation(out=f[i // 4][:, i % 4, :].rearrange("p (k u m) -> p k u m", k=2, u=4),
+                                     in_=x1s[i][:].rearrange("p (k m u) -> p k u m", k=2, u=4), func=ACT.Tanh)
 
             hs = {}
 
             def square(i):
-                h = work.tile([P, Q], F32, name="h", bufs=3)
+                h = work.tile([P, Q], F32, name="h", bufs=4)
                 for k in (0, 1):
                     s = slice(k * 512, (k + 1) * 512)
                     nc.scalar.activation(out=h[:, s].rearrange("p (b j u) -> p b u j", j=4, u=4),
-                                         in_=f[:, i // 4, i % 4, s].rearrange("p (u b j) -> p b u j", u=4, j=4), func=ACT.Square, scale=HALF_ROOT)
+                                         in_=f[i // 4][:, i % 4, s].rearrange("p (u b j) -> p b u j", u=4, j=4), func=ACT.Square, scale=HALF_ROOT)
                 hs[i] = h
-
-            def warm_up(n):
-                for e in range(n):
-                    idle = psum.tile([P, 512], F32, name="idle", tag="ft", bufs=4)
-                    nc.tensor.matmul(idle[:], lhsT=ecs[1][:, 256:288, :].rearrange("p r t -> p (r t)"), rhs=ecs[1][:, 256:384, :].rearrange("p r t -> p (r t)"), start=True, stop=True)
 
             fts = {}
 
-            def trans_f(i):
-                for k in (0, 1):
-                    ft = psum.tile([P, 4, P], F32, name="ft", tag="ft", bufs=4)
-                    for t in range(4):
-                        nc.tensor.transpose(ft[:, t, :], f[:, i // 4, i % 4, k * 512 + t * P:k * 512 + (t + 1) * P], ident[:])
-                    fts[i, k] = ft
+            def trans_f(i, k, b):
+                ft = bank(b, [P, 4, P])
+                for t in range(4):
+                    nc.tensor.transpose(ft[:, t, :], f[i // 4][:, i % 4, k * 512 + t * P:k * 512 + (t + 1) * P], ident[:])
+                fts[i, k] = ft
 
             fgs = {}
 
-            def mul_g(i):
-                fg = work.tile([P, 2, P, 4], BF16, name="fg", align_bytes=64)
-                for k in (0, 1):
-                    nc.vector.tensor_tensor(out=fg[:, k], in0=fts[i, k][:].rearrange("p t n -> p n t"),
-                                            in1=gs[:, k, :].unsqueeze(1).to_broadcast([P, P, 4]), op=ALU.mult)
-                fgs[i] = fg
+            def mul_g(i, k):
+                if k == 0:
+                    fgs[i] = work.tile([P, 2, P, 4], BF16, name="fg", align_bytes=64, bufs=4)
+                nc.vector.tensor_tensor(out=fgs[i][:, k], in0=fts[i, k][:].rearrange("p t n -> p n t"),
+                                        in1=gs[:, k, :].unsqueeze(1).to_broadcast([P, P, 4]), op=ALU.mult)
 
             fgq = {}
 
             def quant_fg(i):
-                cd = work.tile([P, 2 * P], U32, name="fgc", align_bytes=64)
-                sc = work.tile([P, 2 * P], U8, name="fge", align_bytes=64)
+                cd = work.tile([P, 2 * P], U32, name="fgc", align_bytes=64, bufs=4)
+                sc = work.tile([P, 2 * P], U8, name="fge", align_bytes=64, bufs=4)
                 nc.vector.quantize_mx(out=cd[:].bitcast(FP8X4), scales=sc[:], in_=fgs[i][:].rearrange("p k n t -> p (k n t)"))
                 fgq[i] = (cd, sc)
 
             mus = {}
 
-            def mm1(i):
-                mu = psum.tile([P, R], F32, name="mu", tag="mu")
+            def mm1(i, b):
+                mu = bank(b, [P, R])
                 cd, sc = fgq[i]
                 for k in (0, 1):
                     nc.tensor.matmul_mx(out=mu[:], lhsT=cd[:, k * P:(k + 1) * P].bitcast(FP8X4), lhsT_scale=sc[:, k * P:(k + 1) * P],
@@ -151,40 +117,40 @@ def tile_incrementalpredictivecodingupdate_kernel(tc, x1, x2, w1_bytes, w1_scale
                 mus[i] = mu
 
             def error(i):
-                nc.vector.tensor_tensor(out=eps[:, i // 4, i % 4, :].rearrange("p (u m) -> p u m", u=4),
-                                        in0=x2s[:, i // 4, i % 4, :].rearrange("p (m u) -> p u m", u=4),
+                nc.vector.tensor_tensor(out=eps[i // 4][:, i % 4, :].rearrange("p (u m) -> p u m", u=4),
+                                        in0=x2s[i // 4][:, i % 4, :].rearrange("p (m u) -> p u m", u=4),
                                         in1=mus[i][:].rearrange("p (m u) -> p u m", u=4), op=ALU.subtract)
 
             ets = {}
 
-            def trans_e(i):
-                et = psum.tile([P, 4, P], F32, name="et", tag="et")
+            def trans_e(i, b):
+                et = bank(b, [P, 4, P])
                 for t in range(4):
-                    nc.tensor.transpose(et[:, t, :], eps[:, i // 4, i % 4, t * P:(t + 1) * P], ident[:])
+                    nc.tensor.transpose(et[:, t, :], eps[i // 4][:, i % 4, t * P:(t + 1) * P], ident[:])
                 ets[i] = et
 
-            eps_ = {}
+            epb = {}
 
             def mul_p(i):
-                ep = work.tile([P, P, 4], BF16, name="ep", align_bytes=64)
+                ep = work.tile([P, P, 4], BF16, name="ep", align_bytes=64, bufs=4)
                 nc.vector.tensor_tensor(out=ep[:], in0=ets[i][:].rearrange("p t n -> p n t"),
                                         in1=ps[:].unsqueeze(1).to_broadcast([P, P, 4]), op=ALU.mult)
-                eps_[i] = ep
+                epb[i] = ep
 
             epq = {}
 
             def quant_ep(i):
-                cd = work.tile([P, P], U32, name="epc", align_bytes=64)
-                sc = work.tile([P, P], U8, name="epe", align_bytes=64)
-                nc.vector.quantize_mx(out=cd[:].bitcast(FP8X4), scales=sc[:], in_=eps_[i][:].rearrange("p n t -> p (n t)"))
+                cd = work.tile([P, P], U32, name="epc", align_bytes=64, bufs=4)
+                sc = work.tile([P, P], U8, name="epe", align_bytes=64, bufs=4)
+                nc.vector.quantize_mx(out=cd[:].bitcast(FP8X4), scales=sc[:], in_=epb[i][:].rearrange("p n t -> p (n t)"))
                 epq[i] = (cd, sc)
 
             bks = {}
 
-            def mm2(i):
+            def mm2(i, b):
                 cd, sc = epq[i]
                 for h in (0, 1):
-                    bk = psum.tile([P, 512], F32, name="bk", tag="bk", bufs=2)
+                    bk = bank(b + h, [P, 512])
                     nc.tensor.matmul_mx(out=bk[:], lhsT=cd[:].bitcast(FP8X4), lhsT_scale=sc[:],
                                         rhs=v1c[:, h * 512:(h + 1) * 512].bitcast(FP8X4), rhs_scale=v1e[:, h * 512:(h + 1) * 512],
                                         start=True, stop=True)
@@ -194,217 +160,327 @@ def tile_incrementalpredictivecodingupdate_kernel(tc, x1, x2, w1_bytes, w1_scale
             xh = {}
 
             def half_x(i):
-                if i in ON_G:
-                    y = work.tile([P, Q], BF16, name="y", bufs=3)
-                    nc.vector.tensor_scalar(out=y[:, :GC], in0=x1s[:, i // 4, i % 4, :GC], scalar1=0.5, scalar2=None, op0=ALU.mult)
-                    xh[i] = y
+                y = work.tile([P, GC], BF16, name="y", bufs=2)
+                nc.vector.tensor_scalar(out=y[:], in0=x1s[i][:, :GC], scalar1=0.5, scalar2=None, op0=ALU.mult)
+                xh[i] = y
 
-            def delta(i):
-                u = work.tile([P, Q], F32, name="u", bufs=2)
-                for h in (0, 1):
-                    s = slice(h * 512, (h + 1) * 512)
-                    nc.vector.scalar_tensor_tensor(out=u[:, s], in0=hs[i][:, s], scalar=0.5, in1=bks[i, h][:], op0=ALU.subtract, op1=ALU.mult)
-                us[i] = u
+            def delta(i, h):
+                if h == 0:
+                    us[i] = work.tile([P, Q], F32, name="u", bufs=4)
+                s = slice(h * 512, (h + 1) * 512)
+                nc.vector.scalar_tensor_tensor(out=us[i][:, s], in0=hs[i][:, s], scalar=0.5, in1=bks[i, h][:], op0=ALU.subtract, op1=ALU.mult)
 
             outs = {}
 
-            def state_rest(i):
-                o = outs[i]
-                if GC < Q:
-                    nc.vector.scalar_tensor_tensor(out=o[:, GC:], in0=x1s[:, i // 4, i % 4, GC:], scalar=0.5, in1=us[i][:, GC:], op0=ALU.mult, op1=ALU.subtract)
-                nc.sync.dma_start(out=xov[i // 4][:, i % 4, :], in_=o[:])
+            def state_g(i):
+                o = work.tile([P, GC], F32, name="o", bufs=3)
+                nc.gpsimd.tensor_tensor(out=o[:], in0=xh[i][:], in1=us[i][:, :GC], op=ALU.subtract)
+                outs[i] = o
 
-            def state(i):
-                o = work.tile([P, Q], F32, name="o", bufs=3)
-                if i in ON_G:
-                    nc.gpsimd.tensor_tensor(out=o[:, :GC], in0=xh[i][:, :GC], in1=us[i][:, :GC], op=ALU.subtract)
-                    outs[i] = o
-                    return
-                else:
-                    for h in (0, 1):
-                        s = slice(h * 512, (h + 1) * 512)
-                        nc.vector.scalar_tensor_tensor(out=o[:, s], in0=x1s[:, i // 4, i % 4, s], scalar=0.5, in1=us[i][:, s], op0=ALU.mult, op1=ALU.subtract)
-                        nc.sync.dma_start(out=xov[i // 4][:, i % 4, s], in_=o[:, s])
-                    return
-                nc.sync.dma_start(out=xov[i // 4][:, i % 4, :], in_=o[:])
+            def store_g(i):
+                nc.sync.dma_start(out=xov[i // 4][:, i % 4, :GC], in_=outs[i][:])
 
-            def scale_fa(i):
-                s = slice(512 if i < 4 else 0, Q)
-                nc.scalar.activation(out=fap[i // 4][:, i % 4, s], in_=f[:, i // 4, i % 4, s], func=ACT.Copy, scale=af[:, i // 4, i % 4:i % 4 + 1])
+            def state_v(i, lo, hi):
+                o = work.tile([P, hi - lo], F32, name="ov", bufs=4)
+                nc.vector.scalar_tensor_tensor(out=o[:], in0=x1s[i][:, lo:hi], scalar=0.5, in1=us[i][:, lo:hi], op0=ALU.mult, op1=ALU.subtract)
+                nc.sync.dma_start(out=xov[i // 4][:, i % 4, lo:hi], in_=o[:])
+
+            sums = {}
+
+            def state_pe(i, b):
+                acc = bank(b, [P, Q - GC])
+                nc.tensor.matmul(acc[:], lhsT=mhalf[:], rhs=x1s[i][:, GC:], start=True, stop=False)
+                nc.tensor.matmul(acc[:], lhsT=ident[:], rhs=us[i][:, GC:], start=False, stop=True)
+                sums[i] = acc
+
+            def state_out(i):
+                o = work.tile([P, Q - GC], F32, name="op", bufs=4)
+                nc.scalar.activation(out=o[:], in_=sums[i][:], func=ACT.Copy, scale=-1.0)
+                nc.sync.dma_start(out=xov[i // 4][:, i % 4, GC:], in_=o[:])
 
             def inter(eng_copy, out, in_):
                 eng_copy(out=out.rearrange("p (c i) t -> p c t i", i=4), in_=in_.rearrange("p t (c i) -> p c t i", i=4))
 
-            def inter_fa(k, h):
-                inter(nc.scalar.copy, fai[k][:, h * 256:(h + 1) * 256, :], fap[k][:, :, h * 256:(h + 1) * 256])
+            third = {"fa": (f, as_, af, fac, fae, Q), "ec": (eps, cs, cf, ecc, ece, R)}
+            ready = {}
 
-            def quant_fa(k, h):
-                o = k * Q + h * 512
-                nc.vector.quantize_mx(out=fac[:, o:o + 512].bitcast(FP8X4), scales=fae[:, o:o + 512],
-                                      in_=fai[k][:, h * 512:(h + 1) * 512, :].rearrange("p q t -> p (q t)"))
+            def quant3(kind, k, lo, hi):
+                src, gain, gainf, codes, scales, width = third[kind]
+                o = k * width
+                nc.vector.quantize_mx(out=codes[:, o + lo:o + hi].bitcast(FP8X4), scales=scales[:, o + lo:o + hi],
+                                      in_=ready[kind, k, lo][:].rearrange("p q t -> p (q t)"))
 
-            gaps = []
+            def gain_tt(eng, tag, bufs, kind, k, lo, hi):
+                src, gain, gainf, codes, scales, width = third[kind]
+                z = work.tile([P, hi - lo, 4], BF16, name="z" + tag, tag=tag, bufs=bufs, align_bytes=64)
+                eng.tensor_tensor(out=z[:].rearrange("p (c i) t -> p c t i", i=2),
+                                  in0=src[k][:, :, lo:hi].rearrange("p t (c i) -> p c t i", i=2),
+                                  in1=gain[:, k, :].unsqueeze(1).unsqueeze(3).to_broadcast([P, (hi - lo) // 2, 4, 2]), op=ALU.mult)
+                ready[kind, k, lo] = z
 
-            def gap_piece(k, b, kind):
-                z = work.tile([P, P, 4], BF16, name="z", bufs=1, align_bytes=64)
-                src, gain, codes, scales, width = (eps, cs, ecc, ece, R) if kind == 0 else (f, as_, fac, fae, Q)
-                s = slice(b * P, (b + 1) * P)
-                nc.gpsimd.tensor_tensor(out=z[:], in0=src[:, k, :, s].rearrange("p t q -> p q t"),
-                                        in1=gain[:, k, :].unsqueeze(1).to_broadcast([P, P, 4]), op=ALU.mult)
-                o = k * width + b * P
-                gaps.append((codes[:, o:o + P], scales[:, o:o + P], z))
+            diags = {}
 
-            def gap_quant():
-                if gaps:
-                    cd, sc, z = gaps.pop(0)
-                    nc.vector.quantize_mx(out=cd.bitcast(FP8X4), scales=sc, in_=z[:].rearrange("p q t -> p (q t)"))
+            def make_diag(kind, k):
+                gainf = third[kind][2]
+                dg = keep.tile([P, 4, P], F32, name="dg%s%d" % (kind, k))
+                for t in range(4):
+                    nc.scalar.activation(out=dg[:, t, :], in_=ident[:], func=ACT.Copy, scale=gainf[:, k, t:t + 1])
+                diags[kind, k] = dg
 
-            ecs = {}
+            scaled = {}
 
-            def mul_c(k, h):
-                if h == 0:
-                    ec = work.tile([P, R, 4], BF16, name="ec", align_bytes=64)
-                    ecs[k] = ec
-                s = slice(h * 256, (h + 1) * 256)
-                nc.vector.tensor_tensor(out=ecs[k][:, s, :].rearrange("p (c i) t -> p c t i", i=4),
-                                        in0=eps[:, k, :, s].rearrange("p t (c i) -> p c t i", i=4),
-                                        in1=cs[:, k, :].unsqueeze(1).unsqueeze(3).to_broadcast([P, 64, 4, 4]), op=ALU.mult)
+            def gain_pe(kind, k, lo, b):
+                src = third[kind][0]
+                pb = bank(b, [P, 4, P])
+                for t in range(4):
+                    nc.tensor.matmul(pb[:, t, :], lhsT=diags[kind, k][:, t, :], rhs=src[k][:, t, lo:lo + P], start=True, stop=True)
+                scaled[kind, k, lo] = pb
 
-            def quant_ec(k):
-                nc.vector.quantize_mx(out=ecc[:, k * R:(k + 1) * R].bitcast(FP8X4), scales=ece[:, k * R:(k + 1) * R],
-                                      in_=ecs[k][:].rearrange("p r t -> p (r t)"))
+            def gain_out(kind, k, lo):
+                base = lo // 256 * 256
+                if lo == base:
+                    ready[kind, k, base] = work.tile([P, 256, 4], BF16, name="zs", bufs=4, align_bytes=64)
+                nc.scalar.copy(out=ready[kind, k, base][:, lo - base:lo - base + P, :], in_=scaled[kind, k, lo][:].rearrange("p t q -> p q t"))
 
-            def mm3(m):
-                dw = psum.tile([P, R], F32, name="dw", tag="ft", bufs=4)
+            planes = {}
+
+            def gain_plane(kind, k, t, lo, hi):
+                src, gainf = third[kind][0], third[kind][2]
+                if t == 0:
+                    planes[kind, k] = keep.tile([P, 4, hi - lo], BF16, name="pl%s%d" % (kind, k))
+                nc.scalar.activation(out=planes[kind, k][:, t, :], in_=src[k][:, t, lo:hi], func=ACT.Copy, scale=gainf[:, k, t:t + 1])
+
+            def gain_inter(eng_copy, kind, k, lo, hi):
+                z = work.tile([P, hi - lo, 4], BF16, name="zs", bufs=4, align_bytes=64)
+                inter(eng_copy, z[:], planes[kind, k][:, :, lo:hi])
+                ready[kind, k, lo] = z
+
+            dws = {}
+
+            def mm3(m, b):
+                dw = bank(b, [P, R])
                 for k in (0, 1):
                     o = k * Q + m * P
                     nc.tensor.matmul_mx(out=dw[:], lhsT=fac[:, o:o + P].bitcast(FP8X4), lhsT_scale=fae[:, o:o + P],
                                         rhs=ecc[:, k * R:(k + 1) * R].bitcast(FP8X4), rhs_scale=ece[:, k * R:(k + 1) * R],
                                         start=(k == 0), stop=(k == 1))
-                d = work.tile([P, R], F32, name="d", bufs=8)
-                nc.scalar.activation(out=d[:].rearrange("p (m u) -> p m u", u=4), in_=dw[:].rearrange("p (u m) -> p m u", u=4), func=ACT.Copy, scale=0.03125)
+                dws[m] = dw
+
+            def dw_out(m):
+                d = work.tile([P, R], F32, name="d", bufs=4)
+                nc.scalar.activation(out=d[:].rearrange("p (m u) -> p m u", u=4), in_=dws[m][:].rearrange("p (u m) -> p m u", u=4), func=ACT.Copy, scale=0.03125)
                 nc.sync.dma_start(out=dwv[m // 4, m % 4], in_=d[:])
 
-            def widen_s(k, t):
-                nc.scalar.activation(out=w1p[:, k, t, :], in_=w1b[:, k, t, :].bitcast(FP8), func=ACT.Copy, scale=w1s[:, k, t:t + 1])
-
             def widen(k, t):
-                nc.vector.tensor_scalar(out=w1p[:, k, t, :], in0=w1b[:, k, t, :].bitcast(FP8), scalar1=w1s[:, k, t:t + 1], scalar2=None, op0=ALU.mult)
+                nc.vector.tensor_scalar(out=w1p[k][:, t, :], in0=w1b[k][:, t, :].bitcast(FP8), scalar1=w1s[:, k, t:t + 1], scalar2=None, op0=ALU.mult)
+
+            w1i = {}
 
             def quant_w1(k):
                 nc.vector.quantize_mx(out=w1c[:, k * R:(k + 1) * R].bitcast(FP8X4), scales=w1e[:, k * R:(k + 1) * R],
-                                      in_=w1i[:, k].rearrange("p r t -> p (r t)"))
+                                      in_=w1i[k][:].rearrange("p r t -> p (r t)"))
 
-            def inter_v1(h):
-                inter(nc.scalar.copy, v1i[:, h * 256:(h + 1) * 256, :], v1s[:, :, h * 256:(h + 1) * 256])
+            v1i = {}
+
+            def inter_v1(h, eng_copy, tag):
+                v1i[h] = work.tile([P, 512, 4], BF16, name="v1i", tag=tag, bufs=1, align_bytes=64)
+                inter(eng_copy, v1i[h][:], v1s[h][:])
 
             def quant_v1(h):
                 nc.vector.quantize_mx(out=v1c[:, h * 512:(h + 1) * 512].bitcast(FP8X4), scales=v1e[:, h * 512:(h + 1) * 512],
-                                      in_=v1i[:, h * 512:(h + 1) * 512, :].rearrange("p q t -> p (q t)"))
+                                      in_=v1i[h][:].rearrange("p q t -> p (q t)"))
 
-            widen_s(0, 0)
-            widen_s(0, 1)
-            for i in range(2):
+            def g_copy(out, in_):
+                nc.gpsimd.tensor_scalar(out=out, in0=in_, scalar1=1.0, scalar2=0.0, op0=ALU.mult, op1=ALU.add)
+
+            nc.scalar.dma_start(out=w1s[:], in_=w1_scale.rearrange("(g p t) o -> p g (t o)", p=P, t=4))
+            nc.sync.dma_start(out=w1b[0][:], in_=w1v[0])
+            load_x1(0)
+            nc.sync.dma_start(out=w1b[1][:], in_=w1v[1])
+            load_x1(1)
+            nc.sync.dma_start(out=gs[:], in_=g.rearrange("(g p t) -> p g t", p=P, t=4))
+            load_x1(2)
+            load_x1(3)
+            nc.sync.dma_start(out=as_[:], in_=a.rearrange("(g p t) -> p g t", p=P, t=4))
+            load_x1(4)
+            nc.sync.dma_start(out=v1s[1][:], in_=v1v[:, :, 512:1024])
+            load_x1(5)
+            nc.sync.dma_start(out=x2s[0][:], in_=x2v[0])
+            load_x1(6)
+            load_x1(7)
+            nc.sync.dma_start(out=v1s[0][:], in_=v1v[:, :, 0:512])
+            nc.sync.dma_start(out=ps[:], in_=pi2.rearrange("(p t) -> p t", t=4))
+            nc.sync.dma_start(out=cs[:], in_=c.rearrange("(g p t) -> p g t", p=P, t=4))
+            nc.sync.dma_start(out=x2s[1][:], in_=x2v[1])
+            make_identity(nc, ident[:])
+            nc.vector.tensor_scalar(out=mhalf[:], in0=ident[:], scalar1=-0.5, scalar2=None, op0=ALU.mult)
+
+            w1i[0] = keep.tile([P, R, 4], BF16, name="w1i0", align_bytes=64)
+            w1i[1] = work.tile([P, R, 4], BF16, name="w1i1", tag="gz", bufs=1, align_bytes=64)
+            for t in range(4):
+                widen(0, t)
+            widen(1, 0)
+            inter(nc.vector.tensor_copy, w1i[0][:, :256], w1p[0][:, :, :256])
+            for t in (1, 2, 3):
+                widen(1, t)
+            inter(g_copy, w1i[1][:], w1p[1][:])
+            inter(g_copy, w1i[0][:, 256:], w1p[0][:, :, 256:])
+            for i in range(4):
                 tanh(i)
-            for k in (0, 1):
-                for t in range(4):
-                    if (k, t) not in ((0, 0), (0, 1)):
-                        widen(k, t)
-            trans_f(0)
-            inter(nc.vector.tensor_copy, w1i[:, 0], w1p[:, 0])
-            inter(nc.scalar.copy, w1i[:, 1, :256], w1p[:, 1, :, :256])
+                trans_f(i, 0, 2 * i)
+                trans_f(i, 1, 2 * i + 1)
+                mul_g(i, 0)
+                mul_g(i, 1)
+            nc.scalar.copy(out=af[:], in_=as_[:])
+            make_diag("fa", 0)
+
+            def scale_pe(e):
+                gain_pe("fa", 0, e * P, e % 2)
+
+            def scale_out(e):
+                gain_out("fa", 0, e * P)
+
+            def front_t(i):
+                trans_f(i, 0, 2)
+                trans_f(i, 1, 3)
+
+            def front_g(i):
+                mul_g(i, 0)
+                mul_g(i, 1)
+
+            def back_u(i):
+                delta(i, 0)
+                delta(i, 1)
+
+            def state_both(i):
+                state_v(i, 0, 512)
+                state_v(i, 512, Q)
+
+            def trans_both(i, b):
+                trans_f(i, 0, b)
+                trans_f(i, 1, b + 1)
+
+            scale_pe(0)
+            tanh(4)
+            trans_both(4, 2)
+            tanh(5)
+            tanh(6)
+            tanh(7)
+            scale_out(0)
+            for i in range(4):
+                quant_fg(i)
             quant_w1(0)
-            inter(nc.vector.tensor_copy, w1i[:, 1, 256:], w1p[:, 1, :, 256:])
-            tanh(2)
-            tanh(3)
-            for q in range(4):
-                inter_v1(q)
-            for i in range(4, 8):
-                tanh(i)
-            side = [(scale_fa, t) for t in range(4)] + [(inter_fa, 0, 2), (inter_fa, 0, 3)] + [(scale_fa, 4 + t) for t in range(4)] + [(inter_fa, 1, h) for h in range(4)]
-            nside = 0
-
-            for s in range(8):
-                j = s - 3
-                if s == 1:
-                    z0 = work.tile([P, P, 4], BF16, name="z", bufs=1, align_bytes=64)
-                    nc.vector.memset(z0[:, 0:1, 0:2], 0.0)
-                if s in (1, 2, 3, 4):
-                    gap_quant()
-                    gap_piece(0, s - 1, 1)
-                mul_g(s)
-                if s < 7:
-                    trans_f(s + 1)
-                if s == 0:
-                    quant_w1(1)
-                if s >= 1:
-                    error(s - 1)
-                if j >= 0:
-                    mul_p(j)
-                if s == 2:
-                    half_x(0)
-                quant_fg(s)
-                mm1(s)
-                if s == 3:
-                    quant_v1(0)
-                    quant_v1(1)
-                if j >= 0:
-                    quant_ep(j)
-                if j >= 2:
-                    state_rest(j - 2)
-                if j + 1 >= 0:
-                    trans_e(j + 1)
-                if j >= 0:
-                    half_x(j + 1)
-                    square(j)
-                while nside < (0, 0, 0, 3, 6, 9, 11, 14)[s]:
-                    side[nside][0](*side[nside][1:])
-                    nside += 1
-                if s >= 4:
-                    gap_quant()
-                    gap_piece(0, s - 4, 0)
-                if j >= 1:
-                    delta(j - 1)
-                    state(j - 1)
-                if j >= 0:
-                    mm2(j)
+            quant_w1(1)
+            for i in range(4):
+                mm1(i, 4 + i)
+            inter_v1(0, g_copy, "gz")
+            for t in range(4):
+                gain_plane("fa", 1, t, 0, Q)
+            front_g(4)
+            trans_both(5, 2)
+            scale_pe(1)
+            for i in range(4):
+                error(i)
+            front_g(5)
+            trans_both(7, 6)
+            trans_both(6, 2)
+            scale_out(1)
+            quant_fg(4)
+            quant_fg(5)
+            mm1(4, 4)
+            mm1(5, 5)
+            scale_pe(2)
+            scale_pe(3)
+            quant_v1(0)
+            gain_tt(nc.gpsimd, "gz", 1, "ec", 0, 0, 256)
+            inter_v1(1, nc.scalar.copy, "v1b")
+            scale_out(2)
+            scale_out(3)
+            front_g(6)
+            error(4)
+            error(5)
+            trans_e(0, 2)
+            trans_e(1, 3)
+            front_g(7)
+            quant3("fa", 0, 0, 256)
+            quant_fg(6)
+            quant_fg(7)
+            mm1(6, 4)
+            mm1(7, 5)
+            scale_pe(4)
+            scale_pe(5)
+            quant3("ec", 0, 0, 256)
+            gain_tt(nc.gpsimd, "gz", 1, "ec", 0, 256, 512)
+            gain_inter(nc.scalar.copy, "fa", 1, 0, 256)
+            square(0)
+            gain_inter(nc.scalar.copy, "fa", 1, 256, 512)
+            scale_out(4)
+            scale_out(5)
+            square(1)
+            mul_p(0)
+            error(6)
+            mul_p(1)
             error(7)
-            mul_p(5)
-            square(5)
-            delta(4)
-            gap_quant()
-            quant_ep(5)
-            state_rest(3)
-            trans_e(6)
-            mm2(5)
-            mul_c(1, 0)
-            mul_c(1, 1)
-            warm_up(4)
-            quant_fa(0, 1)
-            quant_fa(1, 0)
-            quant_fa(1, 1)
-            quant_ec(1)
-            square(6)
-            square(7)
-            mul_p(6)
-            state(4)
-            for m in range(2):
-                mm3(m)
-            trans_e(7)
-            for m in range(2, 4):
-                mm3(m)
-            quant_ep(6)
-            delta(5)
-            mm2(6)
-            mul_p(7)
-            state(5)
-            for m in range(4, 6):
-                mm3(m)
-            quant_ep(7)
-            delta(6)
-            mm2(7)
-            state(6)
-            for m in range(6, 8):
-                mm3(m)
-            delta(7)
-            state(7)
+            trans_e(2, 4)
+            scale_pe(6)
+            quant_ep(0)
+            quant_v1(1)
+            quant_ep(1)
+            mm2(0, 6)
+            mm2(1, 2)
+            scale_pe(7)
+            gain_tt(nc.vector, "zv", 2, "ec", 1, 128, 256)
+            gain_tt(nc.vector, "zv", 2, "ec", 1, 256, 512)
+            quant3("fa", 0, 256, 512)
+            quant3("ec", 1, 128, 256)
+            quant3("fa", 1, 0, 256)
+            quant3("ec", 1, 256, 512)
+            quant3("ec", 0, 256, 512)
+            gain_tt(nc.gpsimd, "gz", 1, "ec", 1, 0, 128)
+            extra_q = {0: [("ec", 1, 0, 128), ("fa", 0, 512, 768)], 1: [("fa", 1, 256, 512), ("fa", 0, 768, 1024)], 2: [("fa", 1, 512, 768)], 3: [("fa", 1, 768, 1024)]}
+            third_mm = {1: (0, 1), 2: (2, 3), 3: (4,), 4: (5,), 5: (6,)}
+            ON_PE = (0, 2, 4)
+            for j in range(6):
+                if j >= 1:
+                    state_g(j - 1)
+                if j in (0, 1):
+                    gain_inter(nc.scalar.copy, "fa", 1, 512 + 256 * j, 768 + 256 * j)
+                if j == 0:
+                    scale_out(6)
+                    scale_out(7)
+                square(j + 2)
+                if j - 1 in ON_PE:
+                    state_out(j - 1)
+                mul_p(j + 2)
+                if j + 3 < 8:
+                    trans_e(j + 3, 4)
+                for m in third_mm.get(j, ()):
+                    mm3(m, (1, 5)[m % 2])
+                back_u(j)
+                if j >= 1:
+                    store_g(j - 1)
+                for m in third_mm.get(j, ()):
+                    dw_out(m)
+                quant_ep(j + 2)
+                mm2(j + 2, 6 if j % 2 == 0 else 2)
+                if j in ON_PE:
+                    state_pe(j, 0)
+                for e in extra_q.get(j, ()):
+                    quant3(*e)
+                if j not in ON_PE:
+                    state_v(j, GC, Q)
+                half_x(j)
+            state_g(5)
+            mm3(7, 5)
+            if 5 in ON_PE:
+                state_out(5)
+            back_u(6)
+            state_pe(6, 4)
+            dw_out(7)
+            back_u(7)
+            store_g(5)
+            state_v(6, 0, GC)
+            state_out(6)
+            state_v(7, 0, 512)
+            state_v(7, 512, 768)
+            state_v(7, 768, Q)

@@ -17,7 +17,8 @@ ALU = mybir.AluOpType
 ACT = mybir.ActivationFunctionType
 
 HALF_ROOT = 0.5 ** 0.5
-GC = 640
+GC = 512
+RC = Q - GC
 
 
 def tile_incrementalpredictivecodingupdate_kernel(tc, x1, x2, w1_bytes, w1_scale, v1, g, pi2, a, c, out_0, out_1):
@@ -26,7 +27,7 @@ def tile_incrementalpredictivecodingupdate_kernel(tc, x1, x2, w1_bytes, w1_scale
     x2v = x2.rearrange("(g p t) r -> g p t r", p=P, t=4)
     w1v = w1_bytes.rearrange("(g p t) r -> g p t r", p=P, t=4)
     v1v = v1.rearrange("(p t) q -> p t q", t=4)
-    dwv = out_1.rearrange("(k p u) r -> k u p r", k=2, u=4)
+    dwv = out_1.rearrange("(k p u) r -> k p u r", k=2, u=4)
     xov = out_0.rearrange("(g p t) q -> g p t q", p=P, t=4)
 
     with ExitStack() as ctx:
@@ -37,7 +38,8 @@ def tile_incrementalpredictivecodingupdate_kernel(tc, x1, x2, w1_bytes, w1_scale
         x1s = [keep.tile([P, Q], BF16, name="x1s%d" % i) for i in range(8)]
         x2s = [keep.tile([P, 4, R], BF16, name="x2s%d" % k) for k in (0, 1)]
         w1b = [keep.tile([P, 4, R], U8, name="w1b%d" % k) for k in (0, 1)]
-        v1s = [keep.tile([P, 4, 512], BF16, name="v1s%d" % h) for h in (0, 1)]
+        v1a = keep.tile([P, 4, Q], BF16, name="v1a")
+        v1s = [v1a[:, :, h * 512:(h + 1) * 512] for h in (0, 1)]
         w1s = keep.tile([P, 2, 4], F32, name="w1s")
         gs = keep.tile([P, 2, 4], BF16, name="gs")
         as_ = keep.tile([P, 2, 4], BF16, name="as_")
@@ -161,7 +163,7 @@ def tile_incrementalpredictivecodingupdate_kernel(tc, x1, x2, w1_bytes, w1_scale
 
             def half_x(i):
                 y = work.tile([P, GC], BF16, name="y", bufs=2)
-                nc.vector.tensor_scalar(out=y[:], in0=x1s[i][:, :GC], scalar1=0.5, scalar2=None, op0=ALU.mult)
+                nc.vector.tensor_scalar(out=y[:], in0=x1s[i][:, RC:], scalar1=0.5, scalar2=None, op0=ALU.mult)
                 xh[i] = y
 
             def delta(i, h):
@@ -172,31 +174,30 @@ def tile_incrementalpredictivecodingupdate_kernel(tc, x1, x2, w1_bytes, w1_scale
 
             outs = {}
 
-            def state_g(i):
-                o = work.tile([P, GC], F32, name="o", bufs=3)
-                nc.gpsimd.tensor_tensor(out=o[:], in0=xh[i][:], in1=us[i][:, :GC], op=ALU.subtract)
-                outs[i] = o
+            def out_tile(i):
+                if i not in outs:
+                    outs[i] = work.tile([P, Q], F32, name="o", bufs=4)
+                return outs[i]
 
-            def store_g(i):
-                nc.sync.dma_start(out=xov[i // 4][:, i % 4, :GC], in_=outs[i][:])
+            def state_g(i):
+                nc.gpsimd.tensor_tensor(out=out_tile(i)[:, RC:], in0=xh[i][:], in1=us[i][:, RC:], op=ALU.subtract)
+
+            def store_x(i, lo, hi):
+                nc.sync.dma_start(out=xov[i // 4][:, i % 4, lo:hi], in_=outs[i][:, lo:hi])
 
             def state_v(i, lo, hi):
-                o = work.tile([P, hi - lo], F32, name="ov", bufs=4)
-                nc.vector.scalar_tensor_tensor(out=o[:], in0=x1s[i][:, lo:hi], scalar=0.5, in1=us[i][:, lo:hi], op0=ALU.mult, op1=ALU.subtract)
-                nc.sync.dma_start(out=xov[i // 4][:, i % 4, lo:hi], in_=o[:])
+                nc.vector.scalar_tensor_tensor(out=out_tile(i)[:, lo:hi], in0=x1s[i][:, lo:hi], scalar=0.5, in1=us[i][:, lo:hi], op0=ALU.mult, op1=ALU.subtract)
 
             sums = {}
 
             def state_pe(i, b):
-                acc = bank(b, [P, Q - GC])
-                nc.tensor.matmul(acc[:], lhsT=mhalf[:], rhs=x1s[i][:, GC:], start=True, stop=False)
-                nc.tensor.matmul(acc[:], lhsT=ident[:], rhs=us[i][:, GC:], start=False, stop=True)
+                acc = bank(b, [P, RC])
+                nc.tensor.matmul(acc[:], lhsT=mhalf[:], rhs=x1s[i][:, :RC], start=True, stop=False)
+                nc.tensor.matmul(acc[:], lhsT=ident[:], rhs=us[i][:, :RC], start=False, stop=True)
                 sums[i] = acc
 
             def state_out(i):
-                o = work.tile([P, Q - GC], F32, name="op", bufs=4)
-                nc.scalar.activation(out=o[:], in_=sums[i][:], func=ACT.Copy, scale=-1.0)
-                nc.sync.dma_start(out=xov[i // 4][:, i % 4, GC:], in_=o[:])
+                nc.scalar.activation(out=out_tile(i)[:, :RC], in_=sums[i][:], func=ACT.Copy, scale=-1.0)
 
             def inter(eng_copy, out, in_):
                 eng_copy(out=out.rearrange("p (c i) t -> p c t i", i=4), in_=in_.rearrange("p t (c i) -> p c t i", i=4))
@@ -239,10 +240,11 @@ def tile_incrementalpredictivecodingupdate_kernel(tc, x1, x2, w1_bytes, w1_scale
             def gain_out(kind, k, lo):
                 base = lo // 256 * 256
                 if lo == base:
-                    ready[kind, k, base] = work.tile([P, 256, 4], BF16, name="zs", bufs=4, align_bytes=64)
+                    ready[kind, k, base] = work.tile([P, 256, 4], BF16, name="zs", bufs=7, align_bytes=64)
                 nc.scalar.copy(out=ready[kind, k, base][:, lo - base:lo - base + P, :], in_=scaled[kind, k, lo][:].rearrange("p t q -> p q t"))
 
             planes = {}
+            first = {"fa": 0, "ec": P}
 
             def gain_plane(kind, k, t, lo, hi):
                 src, gainf = third[kind][0], third[kind][2]
@@ -251,8 +253,8 @@ def tile_incrementalpredictivecodingupdate_kernel(tc, x1, x2, w1_bytes, w1_scale
                 nc.scalar.activation(out=planes[kind, k][:, t, :], in_=src[k][:, t, lo:hi], func=ACT.Copy, scale=gainf[:, k, t:t + 1])
 
             def gain_inter(eng_copy, kind, k, lo, hi):
-                z = work.tile([P, hi - lo, 4], BF16, name="zs", bufs=4, align_bytes=64)
-                inter(eng_copy, z[:], planes[kind, k][:, :, lo:hi])
+                z = work.tile([P, hi - lo, 4], BF16, name="zs", bufs=7, align_bytes=64)
+                inter(eng_copy, z[:], planes[kind, k][:, :, lo - first[kind]:hi - first[kind]])
                 ready[kind, k, lo] = z
 
             dws = {}
@@ -267,12 +269,16 @@ def tile_incrementalpredictivecodingupdate_kernel(tc, x1, x2, w1_bytes, w1_scale
                 dws[m] = dw
 
             def dw_out(m):
-                d = work.tile([P, R], F32, name="d", bufs=4)
-                nc.scalar.activation(out=d[:].rearrange("p (m u) -> p m u", u=4), in_=dws[m][:].rearrange("p (u m) -> p m u", u=4), func=ACT.Copy, scale=0.03125)
-                nc.sync.dma_start(out=dwv[m // 4, m % 4], in_=d[:])
+                d = work.tile([P, 2, R], F32, name="d", bufs=3)
+                for e in (0, 1):
+                    nc.scalar.activation(out=d[:, e, :].rearrange("p (m u) -> p m u", u=4), in_=dws[m + e][:].rearrange("p (u m) -> p m u", u=4), func=ACT.Copy, scale=0.03125)
+                nc.sync.dma_start(out=dwv[m // 4][:, m % 4:m % 4 + 2, :], in_=d[:])
 
             def widen(k, t):
                 nc.vector.tensor_scalar(out=w1p[k][:, t, :], in0=w1b[k][:, t, :].bitcast(FP8), scalar1=w1s[:, k, t:t + 1], scalar2=None, op0=ALU.mult)
+
+            def widen_s(k, t):
+                nc.scalar.activation(out=w1p[k][:, t, :], in_=w1b[k][:, t, :].bitcast(FP8), func=ACT.Copy, scale=w1s[:, k, t:t + 1])
 
             w1i = {}
 
@@ -284,7 +290,7 @@ def tile_incrementalpredictivecodingupdate_kernel(tc, x1, x2, w1_bytes, w1_scale
 
             def inter_v1(h, eng_copy, tag):
                 v1i[h] = work.tile([P, 512, 4], BF16, name="v1i", tag=tag, bufs=1, align_bytes=64)
-                inter(eng_copy, v1i[h][:], v1s[h][:])
+                inter(eng_copy, v1i[h][:], v1s[h])
 
             def quant_v1(h):
                 nc.vector.quantize_mx(out=v1c[:, h * 512:(h + 1) * 512].bitcast(FP8X4), scales=v1e[:, h * 512:(h + 1) * 512],
@@ -300,15 +306,12 @@ def tile_incrementalpredictivecodingupdate_kernel(tc, x1, x2, w1_bytes, w1_scale
             load_x1(1)
             nc.sync.dma_start(out=gs[:], in_=g.rearrange("(g p t) -> p g t", p=P, t=4))
             load_x1(2)
-            load_x1(3)
             nc.sync.dma_start(out=as_[:], in_=a.rearrange("(g p t) -> p g t", p=P, t=4))
-            load_x1(4)
-            nc.sync.dma_start(out=v1s[1][:], in_=v1v[:, :, 512:1024])
-            load_x1(5)
+            load_x1(3)
+            for i in (4, 5, 6, 7):
+                load_x1(i)
+            nc.sync.dma_start(out=v1a[:], in_=v1v)
             nc.sync.dma_start(out=x2s[0][:], in_=x2v[0])
-            load_x1(6)
-            load_x1(7)
-            nc.sync.dma_start(out=v1s[0][:], in_=v1v[:, :, 0:512])
             nc.sync.dma_start(out=ps[:], in_=pi2.rearrange("(p t) -> p t", t=4))
             nc.sync.dma_start(out=cs[:], in_=c.rearrange("(g p t) -> p g t", p=P, t=4))
             nc.sync.dma_start(out=x2s[1][:], in_=x2v[1])
@@ -326,12 +329,13 @@ def tile_incrementalpredictivecodingupdate_kernel(tc, x1, x2, w1_bytes, w1_scale
             inter(g_copy, w1i[1][:], w1p[1][:])
             inter(g_copy, w1i[0][:, 256:], w1p[0][:, :, 256:])
             for i in range(4):
+                if i == 3:
+                    nc.scalar.copy(out=af[:], in_=as_[:])
                 tanh(i)
                 trans_f(i, 0, 2 * i)
                 trans_f(i, 1, 2 * i + 1)
                 mul_g(i, 0)
                 mul_g(i, 1)
-            nc.scalar.copy(out=af[:], in_=as_[:])
             make_diag("fa", 0)
 
             def scale_pe(e):
@@ -374,6 +378,8 @@ def tile_incrementalpredictivecodingupdate_kernel(tc, x1, x2, w1_bytes, w1_scale
             for i in range(4):
                 mm1(i, 4 + i)
             inter_v1(0, g_copy, "gz")
+            v1i[1] = keep.tile([P, 512, 4], BF16, name="v1i1", align_bytes=64)
+            inter(g_copy, v1i[1][:, :256], v1s[1][:, :, :256])
             for t in range(4):
                 gain_plane("fa", 1, t, 0, Q)
             front_g(4)
@@ -384,6 +390,7 @@ def tile_incrementalpredictivecodingupdate_kernel(tc, x1, x2, w1_bytes, w1_scale
             front_g(5)
             trans_both(7, 6)
             trans_both(6, 2)
+            nc.scalar.copy(out=cf[:], in_=cs[:])
             scale_out(1)
             quant_fg(4)
             quant_fg(5)
@@ -393,94 +400,96 @@ def tile_incrementalpredictivecodingupdate_kernel(tc, x1, x2, w1_bytes, w1_scale
             scale_pe(3)
             quant_v1(0)
             gain_tt(nc.gpsimd, "gz", 1, "ec", 0, 0, 256)
-            inter_v1(1, nc.scalar.copy, "v1b")
+            inter(nc.scalar.copy, v1i[1][:, 256:], v1s[1][:, :, 256:])
+            gain_inter(nc.scalar.copy, "fa", 1, 0, 256)
+            gain_inter(nc.scalar.copy, "fa", 1, 256, 512)
             scale_out(2)
             scale_out(3)
             front_g(6)
             error(4)
-            error(5)
             trans_e(0, 2)
             trans_e(1, 3)
             front_g(7)
             quant3("fa", 0, 0, 256)
+            quant3("fa", 1, 0, 256)
             quant_fg(6)
             quant_fg(7)
             mm1(6, 4)
-            mm1(7, 5)
             scale_pe(4)
-            scale_pe(5)
             quant3("ec", 0, 0, 256)
             gain_tt(nc.gpsimd, "gz", 1, "ec", 0, 256, 512)
-            gain_inter(nc.scalar.copy, "fa", 1, 0, 256)
+            error(5)
             square(0)
-            gain_inter(nc.scalar.copy, "fa", 1, 256, 512)
-            scale_out(4)
-            scale_out(5)
-            square(1)
+            gain_plane("ec", 1, 0, P, R)
+            gain_plane("ec", 1, 1, P, R)
+            mm1(7, 5)
+            scale_pe(5)
             mul_p(0)
             error(6)
             mul_p(1)
             error(7)
+            gain_plane("ec", 1, 2, P, R)
+            gain_plane("ec", 1, 3, P, R)
+            scale_out(4)
+            scale_out(5)
+            gain_inter(nc.scalar.copy, "fa", 1, 512, 768)
+            square(1)
             trans_e(2, 4)
-            scale_pe(6)
             quant_ep(0)
             quant_v1(1)
             quant_ep(1)
             mm2(0, 6)
             mm2(1, 2)
+            scale_pe(6)
             scale_pe(7)
-            gain_tt(nc.vector, "zv", 2, "ec", 1, 128, 256)
-            gain_tt(nc.vector, "zv", 2, "ec", 1, 256, 512)
+            gain_inter(nc.vector.tensor_copy, "ec", 1, 128, 384)
+            gain_inter(nc.vector.tensor_copy, "ec", 1, 384, 512)
+            quant3("fa", 1, 256, 512)
             quant3("fa", 0, 256, 512)
-            quant3("ec", 1, 128, 256)
-            quant3("fa", 1, 0, 256)
-            quant3("ec", 1, 256, 512)
             quant3("ec", 0, 256, 512)
             gain_tt(nc.gpsimd, "gz", 1, "ec", 1, 0, 128)
-            extra_q = {0: [("ec", 1, 0, 128), ("fa", 0, 512, 768)], 1: [("fa", 1, 256, 512), ("fa", 0, 768, 1024)], 2: [("fa", 1, 512, 768)], 3: [("fa", 1, 768, 1024)]}
-            third_mm = {1: (0, 1), 2: (2, 3), 3: (4,), 4: (5,), 5: (6,)}
-            ON_PE = (0, 2, 4)
+            extra_q = {0: [("ec", 1, 128, 384), ("ec", 1, 384, 512), ("ec", 1, 0, 128)], 1: [("fa", 1, 512, 768), ("fa", 0, 512, 768)], 2: [("fa", 1, 768, 1024), ("fa", 0, 768, 1024)]}
+            ON_PE = (0, 4)
             for j in range(6):
                 if j >= 1:
                     state_g(j - 1)
-                if j in (0, 1):
-                    gain_inter(nc.scalar.copy, "fa", 1, 512 + 256 * j, 768 + 256 * j)
                 if j == 0:
                     scale_out(6)
                     scale_out(7)
-                square(j + 2)
                 if j - 1 in ON_PE:
                     state_out(j - 1)
+                if j == 1:
+                    gain_inter(nc.scalar.copy, "fa", 1, 768, 1024)
+                square(j + 2)
                 mul_p(j + 2)
                 if j + 3 < 8:
                     trans_e(j + 3, 4)
-                for m in third_mm.get(j, ()):
-                    mm3(m, (1, 5)[m % 2])
+                if 1 <= j <= 4:
+                    mm3(2 * j - 2, 1)
+                    mm3(2 * j - 1, 5)
                 back_u(j)
                 if j >= 1:
-                    store_g(j - 1)
-                for m in third_mm.get(j, ()):
-                    dw_out(m)
+                    store_x(j - 1, 0, Q)
+                if 1 <= j <= 4:
+                    dw_out(2 * j - 2)
+                if j in ON_PE:
+                    state_pe(j, 5 if j == 0 else 0)
                 quant_ep(j + 2)
                 mm2(j + 2, 6 if j % 2 == 0 else 2)
-                if j in ON_PE:
-                    state_pe(j, 0)
+                if j not in ON_PE:
+                    state_v(j, 0, RC)
                 for e in extra_q.get(j, ()):
                     quant3(*e)
-                if j not in ON_PE:
-                    state_v(j, GC, Q)
                 half_x(j)
             state_g(5)
-            mm3(7, 5)
-            if 5 in ON_PE:
-                state_out(5)
             back_u(6)
             state_pe(6, 4)
-            dw_out(7)
             back_u(7)
-            store_g(5)
-            state_v(6, 0, GC)
+            store_x(5, 0, Q)
+            state_v(6, RC, Q)
             state_out(6)
+            store_x(6, 0, Q)
             state_v(7, 0, 512)
-            state_v(7, 512, 768)
-            state_v(7, 768, Q)
+            store_x(7, 0, 512)
+            state_v(7, 512, Q)
+            store_x(7, 512, Q)

@@ -17,8 +17,9 @@ ALU = mybir.AluOpType
 ACT = mybir.ActivationFunctionType
 
 HALF_ROOT = 0.5 ** 0.5
-GC = 512
+GC = 640
 RC = Q - GC
+SJ = 4
 
 
 def tile_incrementalpredictivecodingupdate_kernel(tc, x1, x2, w1_bytes, w1_scale, v1, g, pi2, a, c, out_0, out_1):
@@ -70,17 +71,15 @@ def tile_incrementalpredictivecodingupdate_kernel(tc, x1, x2, w1_bytes, w1_scale
                 nc.sync.dma_start(out=x1s[i][:], in_=x1v[i // 4][:, i % 4, :])
 
             def tanh(i):
-                nc.scalar.activation(out=f[i // 4][:, i % 4, :].rearrange("p (k u m) -> p k u m", k=2, u=4),
-                                     in_=x1s[i][:].rearrange("p (k m u) -> p k u m", k=2, u=4), func=ACT.Tanh)
+                nc.scalar.activation(out=f[i // 4][:, i % 4, :].rearrange("p (u m) -> p u m", u=4),
+                                     in_=x1s[i][:].rearrange("p (m u) -> p u m", u=4), func=ACT.Tanh)
 
             hs = {}
 
             def square(i):
                 h = work.tile([P, Q], F32, name="h", bufs=4)
-                for k in (0, 1):
-                    s = slice(k * 512, (k + 1) * 512)
-                    nc.scalar.activation(out=h[:, s].rearrange("p (b j u) -> p b u j", j=4, u=4),
-                                         in_=f[i // 4][:, i % 4, s].rearrange("p (u b j) -> p b u j", u=4, j=4), func=ACT.Square, scale=HALF_ROOT)
+                nc.scalar.activation(out=h[:].rearrange("p (b j u) -> p b u j", j=SJ, u=4),
+                                     in_=f[i // 4][:, i % 4, :].rearrange("p (u b j) -> p b u j", u=4, j=SJ), func=ACT.Square, scale=HALF_ROOT)
                 hs[i] = h
 
             fts = {}
@@ -88,7 +87,7 @@ def tile_incrementalpredictivecodingupdate_kernel(tc, x1, x2, w1_bytes, w1_scale
             def trans_f(i, k, b):
                 ft = bank(b, [P, 4, P])
                 for t in range(4):
-                    nc.tensor.transpose(ft[:, t, :], f[i // 4][:, i % 4, k * 512 + t * P:k * 512 + (t + 1) * P], ident[:])
+                    nc.tensor.transpose(ft[:, t, :], f[i // 4][:, i % 4, (2 * t + k) * P:(2 * t + k + 1) * P], ident[:])
                 fts[i, k] = ft
 
             fgs = {}
@@ -271,8 +270,8 @@ def tile_incrementalpredictivecodingupdate_kernel(tc, x1, x2, w1_bytes, w1_scale
             def dw_out(m):
                 d = work.tile([P, 2, R], F32, name="d", bufs=3)
                 for e in (0, 1):
-                    nc.scalar.activation(out=d[:, e, :].rearrange("p (m u) -> p m u", u=4), in_=dws[m + e][:].rearrange("p (u m) -> p m u", u=4), func=ACT.Copy, scale=0.03125)
-                nc.sync.dma_start(out=dwv[m // 4][:, m % 4:m % 4 + 2, :], in_=d[:])
+                    nc.scalar.activation(out=d[:, e, :].rearrange("p (m u) -> p m u", u=4), in_=dws[m + 2 * e][:].rearrange("p (u m) -> p m u", u=4), func=ACT.Copy, scale=0.03125)
+                nc.sync.dma_start(out=dwv[m % 2][:, m // 2:m // 2 + 2, :], in_=d[:])
 
             def widen(k, t):
                 nc.vector.tensor_scalar(out=w1p[k][:, t, :], in0=w1b[k][:, t, :].bitcast(FP8), scalar1=w1s[:, k, t:t + 1], scalar2=None, op0=ALU.mult)
@@ -322,10 +321,9 @@ def tile_incrementalpredictivecodingupdate_kernel(tc, x1, x2, w1_bytes, w1_scale
             w1i[1] = work.tile([P, R, 4], BF16, name="w1i1", tag="gz", bufs=1, align_bytes=64)
             for t in range(4):
                 widen(0, t)
-            widen(1, 0)
-            inter(nc.vector.tensor_copy, w1i[0][:, :256], w1p[0][:, :, :256])
-            for t in (1, 2, 3):
+            for t in range(4):
                 widen(1, t)
+            inter(nc.vector.tensor_copy, w1i[0][:, :256], w1p[0][:, :, :256])
             inter(g_copy, w1i[1][:], w1p[1][:])
             inter(g_copy, w1i[0][:, 256:], w1p[0][:, :, 256:])
             for i in range(4):
@@ -371,10 +369,11 @@ def tile_incrementalpredictivecodingupdate_kernel(tc, x1, x2, w1_bytes, w1_scale
             tanh(6)
             tanh(7)
             scale_out(0)
-            for i in range(4):
+            for i in range(3):
                 quant_fg(i)
             quant_w1(0)
             quant_w1(1)
+            quant_fg(3)
             for i in range(4):
                 mm1(i, 4 + i)
             inter_v1(0, g_copy, "gz")
@@ -390,15 +389,14 @@ def tile_incrementalpredictivecodingupdate_kernel(tc, x1, x2, w1_bytes, w1_scale
             front_g(5)
             trans_both(7, 6)
             trans_both(6, 2)
-            nc.scalar.copy(out=cf[:], in_=cs[:])
             scale_out(1)
             quant_fg(4)
+            quant_v1(0)
             quant_fg(5)
             mm1(4, 4)
             mm1(5, 5)
             scale_pe(2)
             scale_pe(3)
-            quant_v1(0)
             gain_tt(nc.gpsimd, "gz", 1, "ec", 0, 0, 256)
             inter(nc.scalar.copy, v1i[1][:, 256:], v1s[1][:, :, 256:])
             gain_inter(nc.scalar.copy, "fa", 1, 0, 256)
@@ -413,26 +411,22 @@ def tile_incrementalpredictivecodingupdate_kernel(tc, x1, x2, w1_bytes, w1_scale
             quant3("fa", 0, 0, 256)
             quant3("fa", 1, 0, 256)
             quant_fg(6)
+            quant3("ec", 0, 0, 256)
             quant_fg(7)
             mm1(6, 4)
-            scale_pe(4)
-            quant3("ec", 0, 0, 256)
             gain_tt(nc.gpsimd, "gz", 1, "ec", 0, 256, 512)
             error(5)
             square(0)
-            gain_plane("ec", 1, 0, P, R)
-            gain_plane("ec", 1, 1, P, R)
             mm1(7, 5)
+            scale_pe(4)
             scale_pe(5)
             mul_p(0)
             error(6)
             mul_p(1)
             error(7)
-            gain_plane("ec", 1, 2, P, R)
-            gain_plane("ec", 1, 3, P, R)
+            gain_inter(nc.scalar.copy, "fa", 1, 512, 768)
             scale_out(4)
             scale_out(5)
-            gain_inter(nc.scalar.copy, "fa", 1, 512, 768)
             square(1)
             trans_e(2, 4)
             quant_ep(0)
@@ -442,52 +436,69 @@ def tile_incrementalpredictivecodingupdate_kernel(tc, x1, x2, w1_bytes, w1_scale
             mm2(1, 2)
             scale_pe(6)
             scale_pe(7)
-            gain_inter(nc.vector.tensor_copy, "ec", 1, 128, 384)
-            gain_inter(nc.vector.tensor_copy, "ec", 1, 384, 512)
+            gain_tt(nc.vector, "zs", 7, "ec", 1, 128, 384)
+            gain_tt(nc.vector, "zs", 7, "ec", 1, 384, 512)
             quant3("fa", 1, 256, 512)
-            quant3("fa", 0, 256, 512)
             quant3("ec", 0, 256, 512)
+            quant3("fa", 0, 256, 512)
             gain_tt(nc.gpsimd, "gz", 1, "ec", 1, 0, 128)
-            extra_q = {0: [("ec", 1, 128, 384), ("ec", 1, 384, 512), ("ec", 1, 0, 128)], 1: [("fa", 1, 512, 768), ("fa", 0, 512, 768)], 2: [("fa", 1, 768, 1024), ("fa", 0, 768, 1024)]}
-            ON_PE = (0, 4)
+            extra_q = {0: [("ec", 1, 384, 512), ("ec", 1, 0, 128), ("ec", 1, 128, 384)], 1: [("fa", 1, 512, 768), ("fa", 0, 512, 768)], 2: [("fa", 1, 768, 1024), ("fa", 0, 768, 1024)]}
+            ON_PE = (0, 2, 5)
             for j in range(6):
                 if j >= 1:
                     state_g(j - 1)
                 if j == 0:
+                    gain_inter(nc.scalar.copy, "fa", 1, 768, 1024)
                     scale_out(6)
                     scale_out(7)
+                if j == 5:
+                    square(7)
                 if j - 1 in ON_PE:
                     state_out(j - 1)
-                if j == 1:
-                    gain_inter(nc.scalar.copy, "fa", 1, 768, 1024)
-                square(j + 2)
+                if j == 0:
+                    square(2)
                 mul_p(j + 2)
+                if 1 <= j <= 4:
+                    m = (j - 1) // 2 * 4 + (j - 1) % 2
+                    mm3(m, 1)
+                    mm3(m + 2, 5)
                 if j + 3 < 8:
                     trans_e(j + 3, 4)
-                if 1 <= j <= 4:
-                    mm3(2 * j - 2, 1)
-                    mm3(2 * j - 1, 5)
                 back_u(j)
                 if j >= 1:
                     store_x(j - 1, 0, Q)
                 if 1 <= j <= 4:
-                    dw_out(2 * j - 2)
+                    dw_out(m)
+                if 1 <= j <= 4:
+                    square(j + 2)
                 if j in ON_PE:
-                    state_pe(j, 5 if j == 0 else 0)
+                    state_pe(j, {0: 5, 5: 1}.get(j, 0))
+                last = extra_q.get(j, [])
+                if j in ON_PE and not last:
+                    half_x(j)
                 quant_ep(j + 2)
                 mm2(j + 2, 6 if j % 2 == 0 else 2)
-                if j not in ON_PE:
+                if j in ON_PE:
+                    if last:
+                        for e in last[:-1]:
+                            quant3(*e)
+                        half_x(j)
+                        quant3(*last[-1])
+                else:
+                    for e in last:
+                        quant3(*e)
+                    half_x(j)
                     state_v(j, 0, RC)
-                for e in extra_q.get(j, ()):
-                    quant3(*e)
-                half_x(j)
             state_g(5)
+            if 5 in ON_PE:
+                state_out(5)
             back_u(6)
-            state_pe(6, 4)
-            back_u(7)
+            state_pe(6, 5)
+            delta(7, 0)
             store_x(5, 0, Q)
             state_v(6, RC, Q)
             state_out(6)
+            delta(7, 1)
             store_x(6, 0, Q)
             state_v(7, 0, 512)
             store_x(7, 0, 512)

@@ -50,6 +50,7 @@ def tile_incrementalpredictivecodingupdate_kernel(tc, x1, x2, w1_bytes, w1_scale
         cf = keep.tile([P, 2, 4], F32, name="cf")
         ident = keep.tile([P, P], F32, name="ident")
         mhalf = keep.tile([P, P], BF16, name="mhalf")
+        identb = keep.tile([P, P], BF16, name="identb")
 
         f = [keep.tile([P, 4, Q], F32, name="f%d" % k) for k in (0, 1)]
         eps = [keep.tile([P, 4, R], F32, name="eps%d" % k) for k in (0, 1)]
@@ -218,6 +219,14 @@ def tile_incrementalpredictivecodingupdate_kernel(tc, x1, x2, w1_bytes, w1_scale
                                   in1=gain[:, k, :].unsqueeze(1).unsqueeze(3).to_broadcast([P, (hi - lo) // 2, 4, 2]), op=ALU.mult)
                 ready[kind, k, lo] = z
 
+            def gain_from_bank(kind, k, lo, hi, cb):
+                src = third[kind][0]
+                z = work.tile([P, hi - lo, 4], BF16, name="zs", bufs=7, align_bytes=64)
+                nc.vector.tensor_tensor(out=z[:].rearrange("p (c i) t -> p c t i", i=2),
+                                        in0=src[k][:, :, lo:hi].rearrange("p t (c i) -> p c t i", i=2),
+                                        in1=cb[:].unsqueeze(1).unsqueeze(3).to_broadcast([P, (hi - lo) // 2, 4, 2]), op=ALU.mult)
+                ready[kind, k, lo] = z
+
             diags = {}
 
             def make_diag(kind, k):
@@ -298,6 +307,8 @@ def tile_incrementalpredictivecodingupdate_kernel(tc, x1, x2, w1_bytes, w1_scale
             def g_copy(out, in_):
                 nc.gpsimd.tensor_scalar(out=out, in0=in_, scalar1=1.0, scalar2=0.0, op0=ALU.mult, op1=ALU.add)
 
+            VG = 192
+            WV = 320
             nc.scalar.dma_start(out=w1s[:], in_=w1_scale.rearrange("(g p t) o -> p g (t o)", p=P, t=4))
             nc.sync.dma_start(out=w1b[0][:], in_=w1v[0])
             load_x1(0)
@@ -315,6 +326,7 @@ def tile_incrementalpredictivecodingupdate_kernel(tc, x1, x2, w1_bytes, w1_scale
             nc.sync.dma_start(out=cs[:], in_=c.rearrange("(g p t) -> p g t", p=P, t=4))
             nc.sync.dma_start(out=x2s[1][:], in_=x2v[1])
             make_identity(nc, ident[:])
+            nc.vector.tensor_copy(out=identb[:], in_=ident[:])
             nc.vector.tensor_scalar(out=mhalf[:], in0=ident[:], scalar1=-0.5, scalar2=None, op0=ALU.mult)
 
             w1i[0] = keep.tile([P, R, 4], BF16, name="w1i0", align_bytes=64)
@@ -323,9 +335,9 @@ def tile_incrementalpredictivecodingupdate_kernel(tc, x1, x2, w1_bytes, w1_scale
                 widen(0, t)
             for t in range(4):
                 widen(1, t)
-            inter(nc.vector.tensor_copy, w1i[0][:, :256], w1p[0][:, :, :256])
+            inter(nc.vector.tensor_copy, w1i[0][:, :WV], w1p[0][:, :, :WV])
             inter(g_copy, w1i[1][:], w1p[1][:])
-            inter(g_copy, w1i[0][:, 256:], w1p[0][:, :, 256:])
+            inter(g_copy, w1i[0][:, WV:], w1p[0][:, :, WV:])
             for i in range(4):
                 if i == 3:
                     nc.scalar.copy(out=af[:], in_=as_[:])
@@ -378,7 +390,7 @@ def tile_incrementalpredictivecodingupdate_kernel(tc, x1, x2, w1_bytes, w1_scale
                 mm1(i, 4 + i)
             inter_v1(0, g_copy, "gz")
             v1i[1] = keep.tile([P, 512, 4], BF16, name="v1i1", align_bytes=64)
-            inter(g_copy, v1i[1][:, :256], v1s[1][:, :, :256])
+            inter(g_copy, v1i[1][:, :VG], v1s[1][:, :, :VG])
             for t in range(4):
                 gain_plane("fa", 1, t, 0, Q)
             front_g(4)
@@ -398,7 +410,7 @@ def tile_incrementalpredictivecodingupdate_kernel(tc, x1, x2, w1_bytes, w1_scale
             scale_pe(2)
             scale_pe(3)
             gain_tt(nc.gpsimd, "gz", 1, "ec", 0, 0, 256)
-            inter(nc.scalar.copy, v1i[1][:, 256:], v1s[1][:, :, 256:])
+            inter(nc.scalar.copy, v1i[1][:, VG:], v1s[1][:, :, VG:])
             gain_inter(nc.scalar.copy, "fa", 1, 0, 256)
             gain_inter(nc.scalar.copy, "fa", 1, 256, 512)
             scale_out(2)
@@ -425,9 +437,11 @@ def tile_incrementalpredictivecodingupdate_kernel(tc, x1, x2, w1_bytes, w1_scale
             mul_p(1)
             error(7)
             gain_inter(nc.scalar.copy, "fa", 1, 512, 768)
+            square(1)
             scale_out(4)
             scale_out(5)
-            square(1)
+            cb = bank(5, [P, 4])
+            nc.tensor.matmul(cb[:], lhsT=identb[:], rhs=cs[:, 1, :], start=True, stop=True)
             trans_e(2, 4)
             quant_ep(0)
             quant_v1(1)
@@ -436,32 +450,30 @@ def tile_incrementalpredictivecodingupdate_kernel(tc, x1, x2, w1_bytes, w1_scale
             mm2(1, 2)
             scale_pe(6)
             scale_pe(7)
-            gain_tt(nc.vector, "zs", 7, "ec", 1, 128, 384)
-            gain_tt(nc.vector, "zs", 7, "ec", 1, 384, 512)
             quant3("fa", 1, 256, 512)
             quant3("ec", 0, 256, 512)
             quant3("fa", 0, 256, 512)
-            gain_tt(nc.gpsimd, "gz", 1, "ec", 1, 0, 128)
-            extra_q = {0: [("ec", 1, 384, 512), ("ec", 1, 0, 128), ("ec", 1, 128, 384)], 1: [("fa", 1, 512, 768), ("fa", 0, 512, 768)], 2: [("fa", 1, 768, 1024), ("fa", 0, 768, 1024)]}
-            ON_PE = (0, 2, 5)
+            gain_tt(nc.gpsimd, "gz", 1, "ec", 1, 0, 256)
+            gain_from_bank("ec", 1, 256, 512, cb)
+            extra_q = {0: [("ec", 1, 0, 256), ("ec", 1, 256, 512)], 1: [("fa", 1, 512, 768), ("fa", 0, 512, 768)], 2: [("fa", 1, 768, 1024), ("fa", 0, 768, 1024)]}
+            ON_PE = (2, 4, 5)
             for j in range(6):
                 if j >= 1:
                     state_g(j - 1)
                 if j == 0:
                     gain_inter(nc.scalar.copy, "fa", 1, 768, 1024)
+                    square(2)
                     scale_out(6)
                     scale_out(7)
-                if j == 5:
-                    square(7)
                 if j - 1 in ON_PE:
                     state_out(j - 1)
-                if j == 0:
-                    square(2)
+                if j == 5:
+                    square(7)
                 mul_p(j + 2)
                 if 1 <= j <= 4:
                     m = (j - 1) // 2 * 4 + (j - 1) % 2
-                    mm3(m, 1)
-                    mm3(m + 2, 5)
+                    mm3(m, 5)
+                    mm3(m + 2, 0 if j == 1 else 1)
                 if j + 3 < 8:
                     trans_e(j + 3, 4)
                 back_u(j)

@@ -16,20 +16,22 @@ FP8X4 = mybir.dt.float8_e4m3fn_x4
 ALU = mybir.AluOpType
 ACT = mybir.ActivationFunctionType
 
-HALF_ROOT = 0.5 ** 0.5
-GC = 640
-RC = Q - GC
-SJ = 4
+HALF = 512
+PIECE = 256
+GP_COLS = 640
+REST_COLS = Q - GP_COLS
+REST_ON_TENSOR = (2, 4, 5)
+W1_VECTOR_COLS = 320
+V1_GPSIMD_COLS = 192
 
 
 def tile_incrementalpredictivecodingupdate_kernel(tc, x1, x2, w1_bytes, w1_scale, v1, g, pi2, a, c, out_0, out_1):
     nc = tc.nc
-    x1v = x1.rearrange("(g p t) q -> g p t q", p=P, t=4)
-    x2v = x2.rearrange("(g p t) r -> g p t r", p=P, t=4)
-    w1v = w1_bytes.rearrange("(g p t) r -> g p t r", p=P, t=4)
-    v1v = v1.rearrange("(p t) q -> p t q", t=4)
-    dwv = out_1.rearrange("(k p u) r -> k p u r", k=2, u=4)
-    xov = out_0.rearrange("(g p t) q -> g p t q", p=P, t=4)
+    x1_rows = x1.rearrange("(g p t) q -> g p t q", p=P, t=4)
+    x2_rows = x2.rearrange("(g p t) r -> g p t r", p=P, t=4)
+    w1_rows = w1_bytes.rearrange("(g p t) r -> g p t r", p=P, t=4)
+    x_new_rows = out_0.rearrange("(g p t) q -> g p t q", p=P, t=4)
+    dw_rows = out_1.rearrange("(g p u) r -> g p u r", g=2, u=4)
 
     with ExitStack() as ctx:
         keep = ctx.enter_context(tc.tile_pool(name="keep", bufs=1))
@@ -39,480 +41,392 @@ def tile_incrementalpredictivecodingupdate_kernel(tc, x1, x2, w1_bytes, w1_scale
         x1s = [keep.tile([P, Q], BF16, name="x1s%d" % i) for i in range(8)]
         x2s = [keep.tile([P, 4, R], BF16, name="x2s%d" % k) for k in (0, 1)]
         w1b = [keep.tile([P, 4, R], U8, name="w1b%d" % k) for k in (0, 1)]
-        v1a = keep.tile([P, 4, Q], BF16, name="v1a")
-        v1s = [v1a[:, :, h * 512:(h + 1) * 512] for h in (0, 1)]
-        w1s = keep.tile([P, 2, 4], F32, name="w1s")
-        gs = keep.tile([P, 2, 4], BF16, name="gs")
-        as_ = keep.tile([P, 2, 4], BF16, name="as_")
-        cs = keep.tile([P, 2, 4], BF16, name="cs")
-        ps = keep.tile([P, 4], BF16, name="ps")
-        af = keep.tile([P, 2, 4], F32, name="af")
-        cf = keep.tile([P, 2, 4], F32, name="cf")
+        v1s = keep.tile([P, 4, Q], BF16, name="v1s")
+        w1_gain = keep.tile([P, 2, 4], F32, name="w1_gain")
+        g_gain = keep.tile([P, 2, 4], BF16, name="g_gain")
+        a_gain = keep.tile([P, 2, 4], BF16, name="a_gain")
+        c_gain = keep.tile([P, 2, 4], BF16, name="c_gain")
+        pi_gain = keep.tile([P, 4], BF16, name="pi_gain")
+        a_f32 = keep.tile([P, 2, 4], F32, name="a_f32")
         ident = keep.tile([P, P], F32, name="ident")
-        mhalf = keep.tile([P, P], BF16, name="mhalf")
-        identb = keep.tile([P, P], BF16, name="identb")
+        minus_half = keep.tile([P, P], BF16, name="minus_half")
+        ident_bf16 = keep.tile([P, P], BF16, name="ident_bf16")
 
         f = [keep.tile([P, 4, Q], F32, name="f%d" % k) for k in (0, 1)]
         eps = [keep.tile([P, 4, R], F32, name="eps%d" % k) for k in (0, 1)]
-        w1p = [keep.tile([P, 4, R], BF16, name="w1p%d" % k) for k in (0, 1)]
-        w1c = keep.tile([P, 2 * R], U32, name="w1c", align_bytes=64)
-        w1e = keep.tile([P, 2 * R], U8, name="w1e", align_bytes=64)
-        v1c = keep.tile([P, Q], U32, name="v1c", align_bytes=64)
-        v1e = keep.tile([P, Q], U8, name="v1e", align_bytes=64)
-        fac = keep.tile([P, 2 * Q], U32, name="fac", align_bytes=64)
-        fae = keep.tile([P, 2 * Q], U8, name="fae", align_bytes=64)
-        ecc = keep.tile([P, 2 * R], U32, name="ecc", align_bytes=64)
-        ece = keep.tile([P, 2 * R], U8, name="ece", align_bytes=64)
+        w1_planes = [keep.tile([P, 4, R], BF16, name="w1_planes%d" % k) for k in (0, 1)]
+        w1_codes = keep.tile([P, 2 * R], U32, name="w1_codes", align_bytes=64)
+        w1_exps = keep.tile([P, 2 * R], U8, name="w1_exps", align_bytes=64)
+        v1_codes = keep.tile([P, Q], U32, name="v1_codes", align_bytes=64)
+        v1_exps = keep.tile([P, Q], U8, name="v1_exps", align_bytes=64)
+        fa_codes = keep.tile([P, 2 * Q], U32, name="fa_codes", align_bytes=64)
+        fa_exps = keep.tile([P, 2 * Q], U8, name="fa_exps", align_bytes=64)
+        ec_codes = keep.tile([P, 2 * R], U32, name="ec_codes", align_bytes=64)
+        ec_exps = keep.tile([P, 2 * R], U8, name="ec_exps", align_bytes=64)
+        a_diag = keep.tile([P, 4, P], F32, name="a_diag")
+        fa_planes = keep.tile([P, 4, Q], BF16, name="fa_planes")
+        w1_inter0 = keep.tile([P, R, 4], BF16, name="w1_inter0", align_bytes=64)
+        v1_inter1 = keep.tile([P, HALF, 4], BF16, name="v1_inter1", align_bytes=64)
 
         def bank(b, shape):
             return psum.tile(shape, F32, name="bank%d" % b)
 
+        def gpsimd_tile(columns):
+            return work.tile([P, columns, 4], BF16, name="gpsimd_out", bufs=1, align_bytes=64)
+
+        def piece_tile():
+            return work.tile([P, PIECE, 4], BF16, name="piece", bufs=7, align_bytes=64)
+
+        def quantize(codes, exps, inter):
+            nc.vector.quantize_mx(out=codes.bitcast(FP8X4), scales=exps, in_=inter)
+
+        def mx_pass(out, lhs_codes, lhs_exps, rhs_codes, rhs_exps, start, stop):
+            nc.tensor.matmul_mx(out=out, lhsT=lhs_codes.bitcast(FP8X4), lhsT_scale=lhs_exps,
+                                rhs=rhs_codes.bitcast(FP8X4), rhs_scale=rhs_exps, start=start, stop=stop)
+
+        def interleave(copy, out, planes):
+            copy(out=out.rearrange("p (c i) t -> p c t i", i=4), in_=planes.rearrange("p t (c i) -> p c t i", i=4))
+
+        def gpsimd_copy(out, in_):
+            nc.gpsimd.tensor_scalar(out=out, in0=in_, scalar1=1.0, scalar2=0.0, op0=ALU.mult, op1=ALU.add)
+
+        def gain_and_interleave(engine, out, planes, gain):
+            columns = out.shape[1]
+            engine.tensor_tensor(out=out.rearrange("p (c i) t -> p c t i", i=2),
+                                 in0=planes.rearrange("p t (c i) -> p c t i", i=2),
+                                 in1=gain.unsqueeze(1).unsqueeze(3).to_broadcast([P, columns // 2, 4, 2]), op=ALU.mult)
+
         with tc.manual_schedule():
             def load_x1(i):
-                nc.sync.dma_start(out=x1s[i][:], in_=x1v[i // 4][:, i % 4, :])
+                nc.sync.dma_start(out=x1s[i][:], in_=x1_rows[i // 4][:, i % 4, :])
+
+            def widen_w1(k, t):
+                nc.vector.tensor_scalar(out=w1_planes[k][:, t, :], in0=w1b[k][:, t, :].bitcast(FP8),
+                                        scalar1=w1_gain[:, k, t:t + 1], scalar2=None, op0=ALU.mult)
+
+            def quant_w1(k, inter):
+                cols = slice(k * R, (k + 1) * R)
+                quantize(w1_codes[:, cols], w1_exps[:, cols], inter[:].rearrange("p r t -> p (r t)"))
 
             def tanh(i):
-                nc.scalar.activation(out=f[i // 4][:, i % 4, :].rearrange("p (u m) -> p u m", u=4),
-                                     in_=x1s[i][:].rearrange("p (m u) -> p u m", u=4), func=ACT.Tanh)
+                nc.scalar.activation(out=f[i // 4][:, i % 4, :].rearrange("p (u b j) -> p b u j", u=4, j=4),
+                                     in_=x1s[i][:].rearrange("p (b j u) -> p b u j", u=4, j=4), func=ACT.Tanh)
 
-            hs = {}
+            f_turned, fg_inter, fg_quant, mu = {}, {}, {}, {}
 
-            def square(i):
-                h = work.tile([P, Q], F32, name="h", bufs=4)
-                nc.scalar.activation(out=h[:].rearrange("p (b j u) -> p b u j", j=SJ, u=4),
-                                     in_=f[i // 4][:, i % 4, :].rearrange("p (u b j) -> p b u j", u=4, j=SJ), func=ACT.Square, scale=HALF_ROOT)
-                hs[i] = h
+            def turn_f(i, b):
+                for k in (0, 1):
+                    turned = bank(b + k, [P, 4, P])
+                    for t in range(4):
+                        nc.tensor.transpose(turned[:, t, :], f[i // 4][:, i % 4, (2 * t + k) * P:(2 * t + k + 1) * P], ident[:])
+                    f_turned[i, k] = turned
 
-            fts = {}
-
-            def trans_f(i, k, b):
-                ft = bank(b, [P, 4, P])
-                for t in range(4):
-                    nc.tensor.transpose(ft[:, t, :], f[i // 4][:, i % 4, (2 * t + k) * P:(2 * t + k + 1) * P], ident[:])
-                fts[i, k] = ft
-
-            fgs = {}
-
-            def mul_g(i, k):
-                if k == 0:
-                    fgs[i] = work.tile([P, 2, P, 4], BF16, name="fg", align_bytes=64, bufs=4)
-                nc.vector.tensor_tensor(out=fgs[i][:, k], in0=fts[i, k][:].rearrange("p t n -> p n t"),
-                                        in1=gs[:, k, :].unsqueeze(1).to_broadcast([P, P, 4]), op=ALU.mult)
-
-            fgq = {}
+            def gain_g(i):
+                fg_inter[i] = work.tile([P, 2, P, 4], BF16, name="fg_inter", align_bytes=64, bufs=4)
+                for k in (0, 1):
+                    nc.vector.tensor_tensor(out=fg_inter[i][:, k], in0=f_turned[i, k][:].rearrange("p t n -> p n t"),
+                                            in1=g_gain[:, k, :].unsqueeze(1).to_broadcast([P, P, 4]), op=ALU.mult)
 
             def quant_fg(i):
-                cd = work.tile([P, 2 * P], U32, name="fgc", align_bytes=64, bufs=4)
-                sc = work.tile([P, 2 * P], U8, name="fge", align_bytes=64, bufs=4)
-                nc.vector.quantize_mx(out=cd[:].bitcast(FP8X4), scales=sc[:], in_=fgs[i][:].rearrange("p k n t -> p (k n t)"))
-                fgq[i] = (cd, sc)
+                codes = work.tile([P, 2 * P], U32, name="fg_codes", align_bytes=64, bufs=4)
+                exps = work.tile([P, 2 * P], U8, name="fg_exps", align_bytes=64, bufs=4)
+                quantize(codes[:], exps[:], fg_inter[i][:].rearrange("p k n t -> p (k n t)"))
+                fg_quant[i] = (codes, exps)
 
-            mus = {}
-
-            def mm1(i, b):
-                mu = bank(b, [P, R])
-                cd, sc = fgq[i]
+            def matmul_mu(i, b):
+                mu[i] = bank(b, [P, R])
+                codes, exps = fg_quant[i]
                 for k in (0, 1):
-                    nc.tensor.matmul_mx(out=mu[:], lhsT=cd[:, k * P:(k + 1) * P].bitcast(FP8X4), lhsT_scale=sc[:, k * P:(k + 1) * P],
-                                        rhs=w1c[:, k * R:(k + 1) * R].bitcast(FP8X4), rhs_scale=w1e[:, k * R:(k + 1) * R],
-                                        start=(k == 0), stop=(k == 1))
-                mus[i] = mu
+                    mx_pass(mu[i][:], codes[:, k * P:(k + 1) * P], exps[:, k * P:(k + 1) * P],
+                            w1_codes[:, k * R:(k + 1) * R], w1_exps[:, k * R:(k + 1) * R], k == 0, k == 1)
 
             def error(i):
-                nc.vector.tensor_tensor(out=eps[i // 4][:, i % 4, :].rearrange("p (u m) -> p u m", u=4),
-                                        in0=x2s[i // 4][:, i % 4, :].rearrange("p (m u) -> p u m", u=4),
-                                        in1=mus[i][:].rearrange("p (m u) -> p u m", u=4), op=ALU.subtract)
+                nc.vector.tensor_tensor(out=eps[i // 4][:, i % 4, :].rearrange("p (u b j) -> p b u j", u=4, j=4),
+                                        in0=x2s[i // 4][:, i % 4, :].rearrange("p (b j u) -> p b u j", u=4, j=4),
+                                        in1=mu[i][:].rearrange("p (b j u) -> p b u j", u=4, j=4), op=ALU.subtract)
 
-            ets = {}
+            eps_turned, ep_inter, ep_quant, back, half_sq, u, half_x, x_new, sums = {}, {}, {}, {}, {}, {}, {}, {}, {}
 
-            def trans_e(i, b):
-                et = bank(b, [P, 4, P])
+            def quant_v1(h, inter):
+                cols = slice(h * HALF, (h + 1) * HALF)
+                quantize(v1_codes[:, cols], v1_exps[:, cols], inter[:].rearrange("p q t -> p (q t)"))
+
+            def turn_eps(i, b):
+                eps_turned[i] = bank(b, [P, 4, P])
                 for t in range(4):
-                    nc.tensor.transpose(et[:, t, :], eps[i // 4][:, i % 4, t * P:(t + 1) * P], ident[:])
-                ets[i] = et
+                    nc.tensor.transpose(eps_turned[i][:, t, :], eps[i // 4][:, i % 4, t * P:(t + 1) * P], ident[:])
 
-            epb = {}
-
-            def mul_p(i):
-                ep = work.tile([P, P, 4], BF16, name="ep", align_bytes=64, bufs=4)
-                nc.vector.tensor_tensor(out=ep[:], in0=ets[i][:].rearrange("p t n -> p n t"),
-                                        in1=ps[:].unsqueeze(1).to_broadcast([P, P, 4]), op=ALU.mult)
-                epb[i] = ep
-
-            epq = {}
+            def gain_pi(i):
+                ep_inter[i] = work.tile([P, P, 4], BF16, name="ep_inter", align_bytes=64, bufs=4)
+                nc.vector.tensor_tensor(out=ep_inter[i][:], in0=eps_turned[i][:].rearrange("p t n -> p n t"),
+                                        in1=pi_gain[:].unsqueeze(1).to_broadcast([P, P, 4]), op=ALU.mult)
 
             def quant_ep(i):
-                cd = work.tile([P, P], U32, name="epc", align_bytes=64, bufs=4)
-                sc = work.tile([P, P], U8, name="epe", align_bytes=64, bufs=4)
-                nc.vector.quantize_mx(out=cd[:].bitcast(FP8X4), scales=sc[:], in_=epb[i][:].rearrange("p n t -> p (n t)"))
-                epq[i] = (cd, sc)
+                codes = work.tile([P, P], U32, name="ep_codes", align_bytes=64, bufs=4)
+                exps = work.tile([P, P], U8, name="ep_exps", align_bytes=64, bufs=4)
+                quantize(codes[:], exps[:], ep_inter[i][:].rearrange("p n t -> p (n t)"))
+                ep_quant[i] = (codes, exps)
 
-            bks = {}
-
-            def mm2(i, b):
-                cd, sc = epq[i]
+            def matmul_back(i):
+                codes, exps = ep_quant[i]
                 for h in (0, 1):
-                    bk = bank(b + h, [P, 512])
-                    nc.tensor.matmul_mx(out=bk[:], lhsT=cd[:].bitcast(FP8X4), lhsT_scale=sc[:],
-                                        rhs=v1c[:, h * 512:(h + 1) * 512].bitcast(FP8X4), rhs_scale=v1e[:, h * 512:(h + 1) * 512],
-                                        start=True, stop=True)
-                    bks[i, h] = bk
+                    cols = slice(h * HALF, (h + 1) * HALF)
+                    back[i, h] = bank((6, 2)[i % 2] + h, [P, HALF])
+                    mx_pass(back[i, h][:], codes[:], exps[:], v1_codes[:, cols], v1_exps[:, cols], True, True)
 
-            us = {}
-            xh = {}
+            def square(i):
+                half_sq[i] = work.tile([P, Q], F32, name="half_sq", bufs=4)
+                nc.scalar.activation(out=half_sq[i][:].rearrange("p (b j u) -> p b u j", j=4, u=4),
+                                     in_=f[i // 4][:, i % 4, :].rearrange("p (u b j) -> p b u j", u=4, j=4),
+                                     func=ACT.Square, scale=0.5 ** 0.5)
 
-            def half_x(i):
-                y = work.tile([P, GC], BF16, name="y", bufs=2)
-                nc.vector.tensor_scalar(out=y[:], in0=x1s[i][:, RC:], scalar1=0.5, scalar2=None, op0=ALU.mult)
-                xh[i] = y
-
-            def delta(i, h):
+            def slope_back(i, h):
                 if h == 0:
-                    us[i] = work.tile([P, Q], F32, name="u", bufs=4)
-                s = slice(h * 512, (h + 1) * 512)
-                nc.vector.scalar_tensor_tensor(out=us[i][:, s], in0=hs[i][:, s], scalar=0.5, in1=bks[i, h][:], op0=ALU.subtract, op1=ALU.mult)
+                    u[i] = work.tile([P, Q], F32, name="u", bufs=4)
+                cols = slice(h * HALF, (h + 1) * HALF)
+                nc.vector.scalar_tensor_tensor(out=u[i][:, cols], in0=half_sq[i][:, cols], scalar=0.5, in1=back[i, h][:],
+                                               op0=ALU.subtract, op1=ALU.mult)
 
-            outs = {}
+            def x_new_tile(i):
+                if i not in x_new:
+                    x_new[i] = work.tile([P, Q], F32, name="x_new", bufs=4)
+                return x_new[i]
 
-            def out_tile(i):
-                if i not in outs:
-                    outs[i] = work.tile([P, Q], F32, name="o", bufs=4)
-                return outs[i]
+            def halve_x(i):
+                half_x[i] = work.tile([P, GP_COLS], BF16, name="half_x", bufs=2)
+                nc.vector.tensor_scalar(out=half_x[i][:], in0=x1s[i][:, REST_COLS:], scalar1=0.5, scalar2=None, op0=ALU.mult)
 
-            def state_g(i):
-                nc.gpsimd.tensor_tensor(out=out_tile(i)[:, RC:], in0=xh[i][:], in1=us[i][:, RC:], op=ALU.subtract)
+            def state_gpsimd(i):
+                nc.gpsimd.tensor_tensor(out=x_new_tile(i)[:, REST_COLS:], in0=half_x[i][:], in1=u[i][:, REST_COLS:], op=ALU.subtract)
+
+            def state_vector(i, lo, hi):
+                nc.vector.scalar_tensor_tensor(out=x_new_tile(i)[:, lo:hi], in0=x1s[i][:, lo:hi], scalar=0.5, in1=u[i][:, lo:hi],
+                                               op0=ALU.mult, op1=ALU.subtract)
+
+            def state_sum(i, b):
+                sums[i] = bank(b, [P, REST_COLS])
+                nc.tensor.matmul(sums[i][:], lhsT=minus_half[:], rhs=x1s[i][:, :REST_COLS], start=True, stop=False)
+                nc.tensor.matmul(sums[i][:], lhsT=ident[:], rhs=u[i][:, :REST_COLS], start=False, stop=True)
+
+            def state_sum_out(i):
+                nc.scalar.activation(out=x_new_tile(i)[:, :REST_COLS], in_=sums[i][:], func=ACT.Copy, scale=-1.0)
 
             def store_x(i, lo, hi):
-                nc.sync.dma_start(out=xov[i // 4][:, i % 4, lo:hi], in_=outs[i][:, lo:hi])
+                nc.sync.dma_start(out=x_new_rows[i // 4][:, i % 4, lo:hi], in_=x_new[i][:, lo:hi])
 
-            def state_v(i, lo, hi):
-                nc.vector.scalar_tensor_tensor(out=out_tile(i)[:, lo:hi], in0=x1s[i][:, lo:hi], scalar=0.5, in1=us[i][:, lo:hi], op0=ALU.mult, op1=ALU.subtract)
+            fa_piece, ec_piece, fa_scaled, dw = {}, {}, {}, {}
 
-            sums = {}
+            def quant_fa(k, n):
+                cols = slice(k * Q + n * PIECE, k * Q + (n + 1) * PIECE)
+                quantize(fa_codes[:, cols], fa_exps[:, cols], fa_piece[k, n][:].rearrange("p q t -> p (q t)"))
 
-            def state_pe(i, b):
-                acc = bank(b, [P, RC])
-                nc.tensor.matmul(acc[:], lhsT=mhalf[:], rhs=x1s[i][:, :RC], start=True, stop=False)
-                nc.tensor.matmul(acc[:], lhsT=ident[:], rhs=us[i][:, :RC], start=False, stop=True)
-                sums[i] = acc
+            def quant_ec(k, n):
+                cols = slice(k * R + n * PIECE, k * R + (n + 1) * PIECE)
+                quantize(ec_codes[:, cols], ec_exps[:, cols], ec_piece[k, n][:].rearrange("p r t -> p (r t)"))
 
-            def state_out(i):
-                nc.scalar.activation(out=out_tile(i)[:, :RC], in_=sums[i][:], func=ACT.Copy, scale=-1.0)
-
-            def inter(eng_copy, out, in_):
-                eng_copy(out=out.rearrange("p (c i) t -> p c t i", i=4), in_=in_.rearrange("p t (c i) -> p c t i", i=4))
-
-            third = {"fa": (f, as_, af, fac, fae, Q), "ec": (eps, cs, cf, ecc, ece, R)}
-            ready = {}
-
-            def quant3(kind, k, lo, hi):
-                src, gain, gainf, codes, scales, width = third[kind]
-                o = k * width
-                nc.vector.quantize_mx(out=codes[:, o + lo:o + hi].bitcast(FP8X4), scales=scales[:, o + lo:o + hi],
-                                      in_=ready[kind, k, lo][:].rearrange("p q t -> p (q t)"))
-
-            def gain_tt(eng, tag, bufs, kind, k, lo, hi):
-                src, gain, gainf, codes, scales, width = third[kind]
-                z = work.tile([P, hi - lo, 4], BF16, name="z" + tag, tag=tag, bufs=bufs, align_bytes=64)
-                eng.tensor_tensor(out=z[:].rearrange("p (c i) t -> p c t i", i=2),
-                                  in0=src[k][:, :, lo:hi].rearrange("p t (c i) -> p c t i", i=2),
-                                  in1=gain[:, k, :].unsqueeze(1).unsqueeze(3).to_broadcast([P, (hi - lo) // 2, 4, 2]), op=ALU.mult)
-                ready[kind, k, lo] = z
-
-            def gain_from_bank(kind, k, lo, hi, cb):
-                src = third[kind][0]
-                z = work.tile([P, hi - lo, 4], BF16, name="zs", bufs=7, align_bytes=64)
-                nc.vector.tensor_tensor(out=z[:].rearrange("p (c i) t -> p c t i", i=2),
-                                        in0=src[k][:, :, lo:hi].rearrange("p t (c i) -> p c t i", i=2),
-                                        in1=cb[:].unsqueeze(1).unsqueeze(3).to_broadcast([P, (hi - lo) // 2, 4, 2]), op=ALU.mult)
-                ready[kind, k, lo] = z
-
-            diags = {}
-
-            def make_diag(kind, k):
-                gainf = third[kind][2]
-                dg = keep.tile([P, 4, P], F32, name="dg%s%d" % (kind, k))
+            def scale_fa0(e):
+                fa_scaled[e] = bank(e % 2, [P, 4, P])
                 for t in range(4):
-                    nc.scalar.activation(out=dg[:, t, :], in_=ident[:], func=ACT.Copy, scale=gainf[:, k, t:t + 1])
-                diags[kind, k] = dg
+                    nc.tensor.matmul(fa_scaled[e][:, t, :], lhsT=a_diag[:, t, :], rhs=f[0][:, t, e * P:(e + 1) * P], start=True, stop=True)
 
-            scaled = {}
+            def scale_fa0_out(e):
+                if e % 2 == 0:
+                    fa_piece[0, e // 2] = piece_tile()
+                nc.scalar.copy(out=fa_piece[0, e // 2][:, e % 2 * P:(e % 2 + 1) * P, :], in_=fa_scaled[e][:].rearrange("p t q -> p q t"))
 
-            def gain_pe(kind, k, lo, b):
-                src = third[kind][0]
-                pb = bank(b, [P, 4, P])
-                for t in range(4):
-                    nc.tensor.matmul(pb[:, t, :], lhsT=diags[kind, k][:, t, :], rhs=src[k][:, t, lo:lo + P], start=True, stop=True)
-                scaled[kind, k, lo] = pb
+            def interleave_fa1(n):
+                fa_piece[1, n] = piece_tile()
+                interleave(nc.scalar.copy, fa_piece[1, n][:], fa_planes[:, :, n * PIECE:(n + 1) * PIECE])
 
-            def gain_out(kind, k, lo):
-                base = lo // 256 * 256
-                if lo == base:
-                    ready[kind, k, base] = work.tile([P, 256, 4], BF16, name="zs", bufs=7, align_bytes=64)
-                nc.scalar.copy(out=ready[kind, k, base][:, lo - base:lo - base + P, :], in_=scaled[kind, k, lo][:].rearrange("p t q -> p q t"))
+            def gain_c_gpsimd(k, n):
+                ec_piece[k, n] = gpsimd_tile(PIECE)
+                gain_and_interleave(nc.gpsimd, ec_piece[k, n][:], eps[k][:, :, n * PIECE:(n + 1) * PIECE], c_gain[:, k, :])
 
-            planes = {}
-            first = {"fa": 0, "ec": P}
-
-            def gain_plane(kind, k, t, lo, hi):
-                src, gainf = third[kind][0], third[kind][2]
-                if t == 0:
-                    planes[kind, k] = keep.tile([P, 4, hi - lo], BF16, name="pl%s%d" % (kind, k))
-                nc.scalar.activation(out=planes[kind, k][:, t, :], in_=src[k][:, t, lo:hi], func=ACT.Copy, scale=gainf[:, k, t:t + 1])
-
-            def gain_inter(eng_copy, kind, k, lo, hi):
-                z = work.tile([P, hi - lo, 4], BF16, name="zs", bufs=7, align_bytes=64)
-                inter(eng_copy, z[:], planes[kind, k][:, :, lo - first[kind]:hi - first[kind]])
-                ready[kind, k, lo] = z
-
-            dws = {}
-
-            def mm3(m, b):
-                dw = bank(b, [P, R])
+            def matmul_dw(m, b):
+                dw[m] = bank(b, [P, R])
                 for k in (0, 1):
-                    o = k * Q + m * P
-                    nc.tensor.matmul_mx(out=dw[:], lhsT=fac[:, o:o + P].bitcast(FP8X4), lhsT_scale=fae[:, o:o + P],
-                                        rhs=ecc[:, k * R:(k + 1) * R].bitcast(FP8X4), rhs_scale=ece[:, k * R:(k + 1) * R],
-                                        start=(k == 0), stop=(k == 1))
-                dws[m] = dw
+                    cols = slice(k * Q + m * P, k * Q + (m + 1) * P)
+                    mx_pass(dw[m][:], fa_codes[:, cols], fa_exps[:, cols],
+                            ec_codes[:, k * R:(k + 1) * R], ec_exps[:, k * R:(k + 1) * R], k == 0, k == 1)
 
-            def dw_out(m):
-                d = work.tile([P, 2, R], F32, name="d", bufs=3)
+            def store_dw(m):
+                pair = work.tile([P, 2, R], F32, name="dw_pair", bufs=3)
                 for e in (0, 1):
-                    nc.scalar.activation(out=d[:, e, :].rearrange("p (m u) -> p m u", u=4), in_=dws[m + 2 * e][:].rearrange("p (u m) -> p m u", u=4), func=ACT.Copy, scale=0.03125)
-                nc.sync.dma_start(out=dwv[m % 2][:, m // 2:m // 2 + 2, :], in_=d[:])
+                    nc.scalar.activation(out=pair[:, e, :].rearrange("p (m u) -> p m u", u=4),
+                                         in_=dw[m + 2 * e][:].rearrange("p (u m) -> p m u", u=4), func=ACT.Copy, scale=1.0 / 32.0)
+                nc.sync.dma_start(out=dw_rows[m % 2][:, m // 2:m // 2 + 2, :], in_=pair[:])
 
-            def widen(k, t):
-                nc.vector.tensor_scalar(out=w1p[k][:, t, :], in0=w1b[k][:, t, :].bitcast(FP8), scalar1=w1s[:, k, t:t + 1], scalar2=None, op0=ALU.mult)
+            def load_gain(gain, values):
+                nc.sync.dma_start(out=gain[:], in_=values.rearrange("(g p t) -> p g t", p=P, t=4))
 
-            def widen_s(k, t):
-                nc.scalar.activation(out=w1p[k][:, t, :], in_=w1b[k][:, t, :].bitcast(FP8), func=ACT.Copy, scale=w1s[:, k, t:t + 1])
-
-            w1i = {}
-
-            def quant_w1(k):
-                nc.vector.quantize_mx(out=w1c[:, k * R:(k + 1) * R].bitcast(FP8X4), scales=w1e[:, k * R:(k + 1) * R],
-                                      in_=w1i[k][:].rearrange("p r t -> p (r t)"))
-
-            v1i = {}
-
-            def inter_v1(h, eng_copy, tag):
-                v1i[h] = work.tile([P, 512, 4], BF16, name="v1i", tag=tag, bufs=1, align_bytes=64)
-                inter(eng_copy, v1i[h][:], v1s[h])
-
-            def quant_v1(h):
-                nc.vector.quantize_mx(out=v1c[:, h * 512:(h + 1) * 512].bitcast(FP8X4), scales=v1e[:, h * 512:(h + 1) * 512],
-                                      in_=v1i[h][:].rearrange("p q t -> p (q t)"))
-
-            def g_copy(out, in_):
-                nc.gpsimd.tensor_scalar(out=out, in0=in_, scalar1=1.0, scalar2=0.0, op0=ALU.mult, op1=ALU.add)
-
-            VG = 192
-            WV = 320
-            nc.scalar.dma_start(out=w1s[:], in_=w1_scale.rearrange("(g p t) o -> p g (t o)", p=P, t=4))
-            nc.sync.dma_start(out=w1b[0][:], in_=w1v[0])
-            load_x1(0)
-            nc.sync.dma_start(out=w1b[1][:], in_=w1v[1])
-            load_x1(1)
-            nc.sync.dma_start(out=gs[:], in_=g.rearrange("(g p t) -> p g t", p=P, t=4))
+            nc.scalar.dma_start(out=w1_gain[:], in_=w1_scale.rearrange("(g p t) o -> p g (t o)", p=P, t=4))
+            for k in (0, 1):
+                nc.sync.dma_start(out=w1b[k][:], in_=w1_rows[k])
+                load_x1(k)
+            load_gain(g_gain, g)
             load_x1(2)
-            nc.sync.dma_start(out=as_[:], in_=a.rearrange("(g p t) -> p g t", p=P, t=4))
-            load_x1(3)
-            for i in (4, 5, 6, 7):
+            load_gain(a_gain, a)
+            for i in range(3, 8):
                 load_x1(i)
-            nc.sync.dma_start(out=v1a[:], in_=v1v)
-            nc.sync.dma_start(out=x2s[0][:], in_=x2v[0])
-            nc.sync.dma_start(out=ps[:], in_=pi2.rearrange("(p t) -> p t", t=4))
-            nc.sync.dma_start(out=cs[:], in_=c.rearrange("(g p t) -> p g t", p=P, t=4))
-            nc.sync.dma_start(out=x2s[1][:], in_=x2v[1])
+            nc.sync.dma_start(out=v1s[:], in_=v1.rearrange("(p t) q -> p t q", t=4))
+            nc.sync.dma_start(out=x2s[0][:], in_=x2_rows[0])
+            nc.sync.dma_start(out=pi_gain[:], in_=pi2.rearrange("(p t) -> p t", t=4))
+            load_gain(c_gain, c)
+            nc.sync.dma_start(out=x2s[1][:], in_=x2_rows[1])
             make_identity(nc, ident[:])
-            nc.vector.tensor_copy(out=identb[:], in_=ident[:])
-            nc.vector.tensor_scalar(out=mhalf[:], in0=ident[:], scalar1=-0.5, scalar2=None, op0=ALU.mult)
+            nc.vector.tensor_copy(out=ident_bf16[:], in_=ident[:])
+            nc.vector.tensor_scalar(out=minus_half[:], in0=ident[:], scalar1=-0.5, scalar2=None, op0=ALU.mult)
 
-            w1i[0] = keep.tile([P, R, 4], BF16, name="w1i0", align_bytes=64)
-            w1i[1] = work.tile([P, R, 4], BF16, name="w1i1", tag="gz", bufs=1, align_bytes=64)
-            for t in range(4):
-                widen(0, t)
-            for t in range(4):
-                widen(1, t)
-            inter(nc.vector.tensor_copy, w1i[0][:, :WV], w1p[0][:, :, :WV])
-            inter(g_copy, w1i[1][:], w1p[1][:])
-            inter(g_copy, w1i[0][:, WV:], w1p[0][:, :, WV:])
-            for i in range(4):
-                if i == 3:
-                    nc.scalar.copy(out=af[:], in_=as_[:])
+            w1_inter1 = gpsimd_tile(R)
+            for k in (0, 1):
+                for t in range(4):
+                    widen_w1(k, t)
+            interleave(nc.vector.tensor_copy, w1_inter0[:, :W1_VECTOR_COLS], w1_planes[0][:, :, :W1_VECTOR_COLS])
+            interleave(gpsimd_copy, w1_inter1[:], w1_planes[1][:])
+            interleave(gpsimd_copy, w1_inter0[:, W1_VECTOR_COLS:], w1_planes[0][:, :, W1_VECTOR_COLS:])
+            for i in range(3):
                 tanh(i)
-                trans_f(i, 0, 2 * i)
-                trans_f(i, 1, 2 * i + 1)
-                mul_g(i, 0)
-                mul_g(i, 1)
-            make_diag("fa", 0)
-
-            def scale_pe(e):
-                gain_pe("fa", 0, e * P, e % 2)
-
-            def scale_out(e):
-                gain_out("fa", 0, e * P)
-
-            def front_t(i):
-                trans_f(i, 0, 2)
-                trans_f(i, 1, 3)
-
-            def front_g(i):
-                mul_g(i, 0)
-                mul_g(i, 1)
-
-            def back_u(i):
-                delta(i, 0)
-                delta(i, 1)
-
-            def state_both(i):
-                state_v(i, 0, 512)
-                state_v(i, 512, Q)
-
-            def trans_both(i, b):
-                trans_f(i, 0, b)
-                trans_f(i, 1, b + 1)
-
-            scale_pe(0)
-            tanh(4)
-            trans_both(4, 2)
-            tanh(5)
-            tanh(6)
-            tanh(7)
-            scale_out(0)
+            nc.scalar.copy(out=a_f32[:], in_=a_gain[:])
+            tanh(3)
+            for i in range(4):
+                turn_f(i, 2 * i)
+                gain_g(i)
+            for t in range(4):
+                nc.scalar.activation(out=a_diag[:, t, :], in_=ident[:], func=ACT.Copy, scale=a_f32[:, 0, t:t + 1])
+            scale_fa0(0)
+            for i in range(4, 8):
+                tanh(i)
+            turn_f(4, 2)
+            scale_fa0_out(0)
             for i in range(3):
                 quant_fg(i)
-            quant_w1(0)
-            quant_w1(1)
+            quant_w1(0, w1_inter0)
+            quant_w1(1, w1_inter1)
             quant_fg(3)
             for i in range(4):
-                mm1(i, 4 + i)
-            inter_v1(0, g_copy, "gz")
-            v1i[1] = keep.tile([P, 512, 4], BF16, name="v1i1", align_bytes=64)
-            inter(g_copy, v1i[1][:, :VG], v1s[1][:, :, :VG])
+                matmul_mu(i, 4 + i)
+
+            v1_inter0 = gpsimd_tile(HALF)
+            interleave(gpsimd_copy, v1_inter0[:], v1s[:, :, :HALF])
+            interleave(gpsimd_copy, v1_inter1[:, :V1_GPSIMD_COLS], v1s[:, :, HALF:HALF + V1_GPSIMD_COLS])
             for t in range(4):
-                gain_plane("fa", 1, t, 0, Q)
-            front_g(4)
-            trans_both(5, 2)
-            scale_pe(1)
+                nc.scalar.activation(out=fa_planes[:, t, :], in_=f[1][:, t, :], func=ACT.Copy, scale=a_f32[:, 1, t:t + 1])
+            gain_g(4)
+            turn_f(5, 2)
+            scale_fa0(1)
             for i in range(4):
                 error(i)
-            front_g(5)
-            trans_both(7, 6)
-            trans_both(6, 2)
-            scale_out(1)
+            gain_g(5)
+            turn_f(7, 6)
+            turn_f(6, 2)
+            scale_fa0_out(1)
             quant_fg(4)
-            quant_v1(0)
+            quant_v1(0, v1_inter0)
             quant_fg(5)
-            mm1(4, 4)
-            mm1(5, 5)
-            scale_pe(2)
-            scale_pe(3)
-            gain_tt(nc.gpsimd, "gz", 1, "ec", 0, 0, 256)
-            inter(nc.scalar.copy, v1i[1][:, VG:], v1s[1][:, :, VG:])
-            gain_inter(nc.scalar.copy, "fa", 1, 0, 256)
-            gain_inter(nc.scalar.copy, "fa", 1, 256, 512)
-            scale_out(2)
-            scale_out(3)
-            front_g(6)
+            matmul_mu(4, 4)
+            matmul_mu(5, 5)
+            scale_fa0(2)
+            scale_fa0(3)
+
+            gain_c_gpsimd(0, 0)
+            interleave(nc.scalar.copy, v1_inter1[:, V1_GPSIMD_COLS:], v1s[:, :, HALF + V1_GPSIMD_COLS:])
+            interleave_fa1(0)
+            interleave_fa1(1)
+            scale_fa0_out(2)
+            scale_fa0_out(3)
+            gain_g(6)
             error(4)
-            trans_e(0, 2)
-            trans_e(1, 3)
-            front_g(7)
-            quant3("fa", 0, 0, 256)
-            quant3("fa", 1, 0, 256)
+            turn_eps(0, 2)
+            turn_eps(1, 3)
+            gain_g(7)
+            quant_fa(0, 0)
+            quant_fa(1, 0)
             quant_fg(6)
-            quant3("ec", 0, 0, 256)
+            quant_ec(0, 0)
             quant_fg(7)
-            mm1(6, 4)
-            gain_tt(nc.gpsimd, "gz", 1, "ec", 0, 256, 512)
+            matmul_mu(6, 4)
+
+            gain_c_gpsimd(0, 1)
             error(5)
             square(0)
-            mm1(7, 5)
-            scale_pe(4)
-            scale_pe(5)
-            mul_p(0)
+            matmul_mu(7, 5)
+            scale_fa0(4)
+            scale_fa0(5)
+            gain_pi(0)
             error(6)
-            mul_p(1)
+            gain_pi(1)
             error(7)
-            gain_inter(nc.scalar.copy, "fa", 1, 512, 768)
+            interleave_fa1(2)
             square(1)
-            scale_out(4)
-            scale_out(5)
-            cb = bank(5, [P, 4])
-            nc.tensor.matmul(cb[:], lhsT=identb[:], rhs=cs[:, 1, :], start=True, stop=True)
-            trans_e(2, 4)
+            scale_fa0_out(4)
+            scale_fa0_out(5)
+            c_bank = bank(5, [P, 4])
+            nc.tensor.matmul(c_bank[:], lhsT=ident_bf16[:], rhs=c_gain[:, 1, :], start=True, stop=True)
+            turn_eps(2, 4)
             quant_ep(0)
-            quant_v1(1)
+            quant_v1(1, v1_inter1)
             quant_ep(1)
-            mm2(0, 6)
-            mm2(1, 2)
-            scale_pe(6)
-            scale_pe(7)
-            quant3("fa", 1, 256, 512)
-            quant3("ec", 0, 256, 512)
-            quant3("fa", 0, 256, 512)
-            gain_tt(nc.gpsimd, "gz", 1, "ec", 1, 0, 256)
-            gain_from_bank("ec", 1, 256, 512, cb)
-            extra_q = {0: [("ec", 1, 0, 256), ("ec", 1, 256, 512)], 1: [("fa", 1, 512, 768), ("fa", 0, 512, 768)], 2: [("fa", 1, 768, 1024), ("fa", 0, 768, 1024)]}
-            ON_PE = (2, 4, 5)
+            matmul_back(0)
+            matmul_back(1)
+            scale_fa0(6)
+            scale_fa0(7)
+            quant_fa(1, 1)
+            quant_ec(0, 1)
+            quant_fa(0, 1)
+            gain_c_gpsimd(1, 0)
+            ec_piece[1, 1] = piece_tile()
+            gain_and_interleave(nc.vector, ec_piece[1, 1][:], eps[1][:, :, PIECE:], c_bank[:])
+            interleave_fa1(3)
+            square(2)
+            scale_fa0_out(6)
+            scale_fa0_out(7)
+
             for j in range(6):
                 if j >= 1:
-                    state_g(j - 1)
-                if j == 0:
-                    gain_inter(nc.scalar.copy, "fa", 1, 768, 1024)
-                    square(2)
-                    scale_out(6)
-                    scale_out(7)
-                if j - 1 in ON_PE:
-                    state_out(j - 1)
+                    state_gpsimd(j - 1)
+                if j - 1 in REST_ON_TENSOR:
+                    state_sum_out(j - 1)
                 if j == 5:
                     square(7)
-                mul_p(j + 2)
+                gain_pi(j + 2)
                 if 1 <= j <= 4:
                     m = (j - 1) // 2 * 4 + (j - 1) % 2
-                    mm3(m, 5)
-                    mm3(m + 2, 0 if j == 1 else 1)
+                    matmul_dw(m, 5)
+                    matmul_dw(m + 2, 0 if j == 1 else 1)
                 if j + 3 < 8:
-                    trans_e(j + 3, 4)
-                back_u(j)
+                    turn_eps(j + 3, 4)
+                slope_back(j, 0)
+                slope_back(j, 1)
                 if j >= 1:
                     store_x(j - 1, 0, Q)
                 if 1 <= j <= 4:
-                    dw_out(m)
-                if 1 <= j <= 4:
+                    store_dw(m)
                     square(j + 2)
-                if j in ON_PE:
-                    state_pe(j, {0: 5, 5: 1}.get(j, 0))
-                last = extra_q.get(j, [])
-                if j in ON_PE and not last:
-                    half_x(j)
-                quant_ep(j + 2)
-                mm2(j + 2, 6 if j % 2 == 0 else 2)
-                if j in ON_PE:
-                    if last:
-                        for e in last[:-1]:
-                            quant3(*e)
-                        half_x(j)
-                        quant3(*last[-1])
-                else:
-                    for e in last:
-                        quant3(*e)
-                    half_x(j)
-                    state_v(j, 0, RC)
-            state_g(5)
-            if 5 in ON_PE:
-                state_out(5)
-            back_u(6)
-            state_pe(6, 5)
-            delta(7, 0)
+                if j in REST_ON_TENSOR:
+                    state_sum(j, 1 if j == 5 else 0)
+                run = [(quant_ep, j + 2)]
+                if j == 0:
+                    run = run + [(quant_ec, 1, 0), (quant_ec, 1, 1)]
+                if j in (1, 2):
+                    run = run + [(quant_fa, 1, j + 1), (quant_fa, 0, j + 1)]
+                if j not in REST_ON_TENSOR:
+                    run = run + [(state_vector, j, 0, REST_COLS)]
+                run = run[:-1] + [(halve_x, j)] + run[-1:]
+                for call in run:
+                    call[0](*call[1:])
+                matmul_back(j + 2)
+
+            state_gpsimd(5)
+            state_sum_out(5)
+            slope_back(6, 0)
+            slope_back(6, 1)
+            state_sum(6, 5)
+            slope_back(7, 0)
             store_x(5, 0, Q)
-            state_v(6, RC, Q)
-            state_out(6)
-            delta(7, 1)
+            state_vector(6, REST_COLS, Q)
+            state_sum_out(6)
+            slope_back(7, 1)
             store_x(6, 0, Q)
-            state_v(7, 0, 512)
-            store_x(7, 0, 512)
-            state_v(7, 512, Q)
-            store_x(7, 512, Q)
+            for h in (0, 1):
+                state_vector(7, h * HALF, (h + 1) * HALF)
+                store_x(7, h * HALF, (h + 1) * HALF)

@@ -18,7 +18,7 @@ ACT = mybir.ActivationFunctionType
 
 HALF = 512
 PIECE = 256
-GP_COLS = 640
+GP_COLS = 608
 REST_COLS = Q - GP_COLS
 REST_ON_TENSOR = (2, 4, 5)
 W1_VECTOR_COLS = 320
@@ -92,9 +92,9 @@ def tile_incrementalpredictivecodingupdate_kernel(tc, x1, x2, w1_bytes, w1_scale
 
         def gain_and_interleave(engine, out, planes, gain):
             columns = out.shape[1]
-            engine.tensor_tensor(out=out.rearrange("p (c i) t -> p c t i", i=2),
-                                 in0=planes.rearrange("p t (c i) -> p c t i", i=2),
-                                 in1=gain.unsqueeze(1).unsqueeze(3).to_broadcast([P, columns // 2, 4, 2]), op=ALU.mult)
+            engine.tensor_tensor(out=out.rearrange("p (c i) t -> p c t i", i=4),
+                                 in0=planes.rearrange("p t (c i) -> p c t i", i=4),
+                                 in1=gain.unsqueeze(1).unsqueeze(3).to_broadcast([P, columns // 4, 4, 4]), op=ALU.mult)
 
         with tc.manual_schedule():
             def load_x1(i):

@@ -340,7 +340,6 @@ def tile_incrementalpredictivecodingupdate_kernel(tc, x1, x2, w1_bytes, w1_scale
             turn_eps(1, 3)
             gain_g(7)
             quant_fa(0, 0)
-            quant_fa(1, 0)
             quant_fg(6)
             quant_ec(0, 0)
             quant_fg(7)
@@ -356,10 +355,10 @@ def tile_incrementalpredictivecodingupdate_kernel(tc, x1, x2, w1_bytes, w1_scale
             error(6)
             gain_pi(1)
             error(7)
-            interleave_fa1(2)
-            square(1)
             scale_fa0_out(4)
+            interleave_fa1(2)
             scale_fa0_out(5)
+            square(1)
             c_bank = bank(5, [P, 4])
             nc.tensor.matmul(c_bank[:], lhsT=ident_bf16[:], rhs=c_gain[:, 1, :], start=True, stop=True)
             turn_eps(2, 4)
@@ -370,16 +369,17 @@ def tile_incrementalpredictivecodingupdate_kernel(tc, x1, x2, w1_bytes, w1_scale
             matmul_back(1)
             scale_fa0(6)
             scale_fa0(7)
+            quant_fa(1, 0)
             quant_fa(1, 1)
             quant_ec(0, 1)
             quant_fa(0, 1)
             gain_c_gpsimd(1, 0)
             ec_piece[1, 1] = piece_tile()
             gain_and_interleave(nc.vector, ec_piece[1, 1][:], eps[1][:, :, PIECE:], c_bank[:])
-            interleave_fa1(3)
-            square(2)
             scale_fa0_out(6)
+            interleave_fa1(3)
             scale_fa0_out(7)
+            square(2)
 
             for j in range(6):
                 if j >= 1:

@@ -20,7 +20,7 @@ HALF = 512
 PIECE = 256
 GP_COLS = 608
 REST_COLS = Q - GP_COLS
-REST_ON_TENSOR = (2, 4, 5)
+REST_ON_TENSOR = (0, 2, 4, 5)
 W1_VECTOR_COLS = 320
 V1_GPSIMD_COLS = 192
 
@@ -74,9 +74,6 @@ def tile_incrementalpredictivecodingupdate_kernel(tc, x1, x2, w1_bytes, w1_scale
         def gpsimd_tile(columns):
             return work.tile([P, columns, 4], BF16, name="gpsimd_out", bufs=1, align_bytes=64)
 
-        def piece_tile():
-            return work.tile([P, PIECE, 4], BF16, name="piece", bufs=7, align_bytes=64)
-
         def quantize(codes, exps, inter):
             nc.vector.quantize_mx(out=codes.bitcast(FP8X4), scales=exps, in_=inter)
 
@@ -122,16 +119,19 @@ def tile_incrementalpredictivecodingupdate_kernel(tc, x1, x2, w1_bytes, w1_scale
                     f_turned[i, k] = turned
 
             def gain_g(i):
-                fg_inter[i] = work.tile([P, 2, P, 4], BF16, name="fg_inter", align_bytes=64, bufs=4)
+                if i % 2 == 0:
+                    fg_inter[i // 2] = work.tile([P, 2, 2, P, 4], BF16, name="fg_inter", align_bytes=64)
                 for k in (0, 1):
-                    nc.vector.tensor_tensor(out=fg_inter[i][:, k], in0=f_turned[i, k][:].rearrange("p t n -> p n t"),
+                    nc.vector.tensor_tensor(out=fg_inter[i // 2][:, i % 2, k], in0=f_turned[i, k][:].rearrange("p t n -> p n t"),
                                             in1=g_gain[:, k, :].unsqueeze(1).to_broadcast([P, P, 4]), op=ALU.mult)
 
-            def quant_fg(i):
-                codes = work.tile([P, 2 * P], U32, name="fg_codes", align_bytes=64, bufs=4)
-                exps = work.tile([P, 2 * P], U8, name="fg_exps", align_bytes=64, bufs=4)
-                quantize(codes[:], exps[:], fg_inter[i][:].rearrange("p k n t -> p (k n t)"))
-                fg_quant[i] = (codes, exps)
+            def quant_fg(i, tiles=1):
+                codes = work.tile([P, tiles, 2 * P], U32, name="fg_codes", align_bytes=64)
+                exps = work.tile([P, tiles, 2 * P], U8, name="fg_exps", align_bytes=64)
+                quantize(codes[:].rearrange("p i c -> p (i c)"), exps[:].rearrange("p i c -> p (i c)"),
+                         fg_inter[i // 2][:, i % 2:i % 2 + tiles].rearrange("p i k n t -> p (i k n t)"))
+                for e in range(tiles):
+                    fg_quant[i + e] = (codes[:, e], exps[:, e])
 
             def matmul_mu(i, b):
                 mu[i] = bank(b, [P, R])
@@ -216,9 +216,14 @@ def tile_incrementalpredictivecodingupdate_kernel(tc, x1, x2, w1_bytes, w1_scale
 
             fa_piece, ec_piece, fa_scaled, dw = {}, {}, {}, {}
 
-            def quant_fa(k, n):
-                cols = slice(k * Q + n * PIECE, k * Q + (n + 1) * PIECE)
-                quantize(fa_codes[:, cols], fa_exps[:, cols], fa_piece[k, n][:].rearrange("p q t -> p (q t)"))
+            def fa_tile(n):
+                if n not in fa_piece:
+                    fa_piece[n] = work.tile([P, 2, PIECE, 4], BF16, name="fa_piece", bufs=3, align_bytes=64)
+                return fa_piece[n]
+
+            def quant_fa(n):
+                cols = slice(2 * n * PIECE, 2 * (n + 1) * PIECE)
+                quantize(fa_codes[:, cols], fa_exps[:, cols], fa_piece[n][:].rearrange("p k q t -> p (k q t)"))
 
             def quant_ec(k, n):
                 cols = slice(k * R + n * PIECE, k * R + (n + 1) * PIECE)
@@ -230,13 +235,10 @@ def tile_incrementalpredictivecodingupdate_kernel(tc, x1, x2, w1_bytes, w1_scale
                     nc.tensor.matmul(fa_scaled[e][:, t, :], lhsT=a_diag[:, t, :], rhs=f[0][:, t, e * P:(e + 1) * P], start=True, stop=True)
 
             def scale_fa0_out(e):
-                if e % 2 == 0:
-                    fa_piece[0, e // 2] = piece_tile()
-                nc.scalar.copy(out=fa_piece[0, e // 2][:, e % 2 * P:(e % 2 + 1) * P, :], in_=fa_scaled[e][:].rearrange("p t q -> p q t"))
+                nc.scalar.copy(out=fa_tile(e // 2)[:, 0, e % 2 * P:(e % 2 + 1) * P, :], in_=fa_scaled[e][:].rearrange("p t q -> p q t"))
 
             def interleave_fa1(n):
-                fa_piece[1, n] = piece_tile()
-                interleave(nc.scalar.copy, fa_piece[1, n][:], fa_planes[:, :, n * PIECE:(n + 1) * PIECE])
+                interleave(nc.scalar.copy, fa_tile(n)[:, 1], fa_planes[:, :, n * PIECE:(n + 1) * PIECE])
 
             def gain_c_gpsimd(k, n):
                 ec_piece[k, n] = gpsimd_tile(PIECE)
@@ -245,7 +247,8 @@ def tile_incrementalpredictivecodingupdate_kernel(tc, x1, x2, w1_bytes, w1_scale
             def matmul_dw(m, b):
                 dw[m] = bank(b, [P, R])
                 for k in (0, 1):
-                    cols = slice(k * Q + m * P, k * Q + (m + 1) * P)
+                    first = (m // 2 * 2 + k) * PIECE + m % 2 * P
+                    cols = slice(first, first + P)
                     mx_pass(dw[m][:], fa_codes[:, cols], fa_exps[:, cols],
                             ec_codes[:, k * R:(k + 1) * R], ec_exps[:, k * R:(k + 1) * R], k == 0, k == 1)
 
@@ -298,11 +301,10 @@ def tile_incrementalpredictivecodingupdate_kernel(tc, x1, x2, w1_bytes, w1_scale
                 tanh(i)
             turn_f(4, 2)
             scale_fa0_out(0)
-            for i in range(3):
-                quant_fg(i)
+            quant_fg(0, tiles=2)
             quant_w1(0, w1_inter0)
             quant_w1(1, w1_inter1)
-            quant_fg(3)
+            quant_fg(2, tiles=2)
             for i in range(4):
                 matmul_mu(i, 4 + i)
 
@@ -339,7 +341,6 @@ def tile_incrementalpredictivecodingupdate_kernel(tc, x1, x2, w1_bytes, w1_scale
             turn_eps(0, 2)
             turn_eps(1, 3)
             gain_g(7)
-            quant_fa(0, 0)
             quant_fg(6)
             quant_ec(0, 0)
             quant_fg(7)
@@ -369,13 +370,12 @@ def tile_incrementalpredictivecodingupdate_kernel(tc, x1, x2, w1_bytes, w1_scale
             matmul_back(1)
             scale_fa0(6)
             scale_fa0(7)
-            quant_fa(1, 0)
-            quant_fa(1, 1)
+            quant_fa(0)
             quant_ec(0, 1)
-            quant_fa(0, 1)
-            gain_c_gpsimd(1, 0)
-            ec_piece[1, 1] = piece_tile()
-            gain_and_interleave(nc.vector, ec_piece[1, 1][:], eps[1][:, :, PIECE:], c_bank[:])
+            quant_fa(1)
+            ec_inter1 = gpsimd_tile(R)
+            gain_and_interleave(nc.gpsimd, ec_inter1[:, :PIECE], eps[1][:, :, :PIECE], c_gain[:, 1, :])
+            gain_and_interleave(nc.vector, ec_inter1[:, PIECE:], eps[1][:, :, PIECE:], c_bank[:])
             scale_fa0_out(6)
             interleave_fa1(3)
             scale_fa0_out(7)
@@ -392,7 +392,7 @@ def tile_incrementalpredictivecodingupdate_kernel(tc, x1, x2, w1_bytes, w1_scale
                 if 1 <= j <= 4:
                     m = (j - 1) // 2 * 4 + (j - 1) % 2
                     matmul_dw(m, 5)
-                    matmul_dw(m + 2, 0 if j == 1 else 1)
+                    matmul_dw(m + 2, 1)
                 if j + 3 < 8:
                     turn_eps(j + 3, 4)
                 slope_back(j, 0)
@@ -406,9 +406,9 @@ def tile_incrementalpredictivecodingupdate_kernel(tc, x1, x2, w1_bytes, w1_scale
                     state_sum(j, 1 if j == 5 else 0)
                 run = [(quant_ep, j + 2)]
                 if j == 0:
-                    run = run + [(quant_ec, 1, 0), (quant_ec, 1, 1)]
+                    run = run + [(quantize, ec_codes[:, R:], ec_exps[:, R:], ec_inter1[:].rearrange("p r t -> p (r t)"))]
                 if j in (1, 2):
-                    run = run + [(quant_fa, 1, j + 1), (quant_fa, 0, j + 1)]
+                    run = run + [(quant_fa, j + 1)]
                 if j not in REST_ON_TENSOR:
                     run = run + [(state_vector, j, 0, REST_COLS)]
                 run = run[:-1] + [(halve_x, j)] + run[-1:]

@@ -55,14 +55,14 @@ def tile_incrementalpredictivecodingupdate_kernel(tc, x1, x2, w1_bytes, w1_scale
         f = [keep.tile([P, 4, Q], F32, name="f%d" % k) for k in (0, 1)]
         eps = [keep.tile([P, 4, R], F32, name="eps%d" % k) for k in (0, 1)]
         w1_planes = [keep.tile([P, 4, R], BF16, name="w1_planes%d" % k) for k in (0, 1)]
-        w1_codes = keep.tile([P, 2 * R], U32, name="w1_codes", align_bytes=64)
-        w1_exps = keep.tile([P, 2 * R], U8, name="w1_exps", align_bytes=64)
-        v1_codes = keep.tile([P, Q], U32, name="v1_codes", align_bytes=64)
-        v1_exps = keep.tile([P, Q], U8, name="v1_exps", align_bytes=64)
-        fa_codes = keep.tile([P, 2 * Q], U32, name="fa_codes", align_bytes=64)
-        fa_exps = keep.tile([P, 2 * Q], U8, name="fa_exps", align_bytes=64)
-        ec_codes = keep.tile([P, 2 * R], U32, name="ec_codes", align_bytes=64)
-        ec_exps = keep.tile([P, 2 * R], U8, name="ec_exps", align_bytes=64)
+        w1_codes = keep.tile([P, 2 * R], U32, name="w1_codes", align_bytes=256)
+        w1_exps = keep.tile([P, 2 * R], U8, name="w1_exps", align_bytes=256)
+        v1_codes = keep.tile([P, Q], U32, name="v1_codes", align_bytes=256)
+        v1_exps = keep.tile([P, Q], U8, name="v1_exps", align_bytes=256)
+        fa_codes = keep.tile([P, 2 * Q], U32, name="fa_codes", align_bytes=256)
+        fa_exps = keep.tile([P, 2 * Q], U8, name="fa_exps", align_bytes=256)
+        ec_codes = keep.tile([P, 2 * R], U32, name="ec_codes", align_bytes=256)
+        ec_exps = keep.tile([P, 2 * R], U8, name="ec_exps", align_bytes=256)
         a_diag = keep.tile([P, 4, P], F32, name="a_diag")
         fa_planes = keep.tile([P, 4, Q], BF16, name="fa_planes")
         w1_inter0 = keep.tile([P, R, 4], BF16, name="w1_inter0", align_bytes=64)
@@ -126,8 +126,8 @@ def tile_incrementalpredictivecodingupdate_kernel(tc, x1, x2, w1_bytes, w1_scale
                                             in1=g_gain[:, k, :].unsqueeze(1).to_broadcast([P, P, 4]), op=ALU.mult)
 
             def quant_fg(i, tiles=1):
-                codes = work.tile([P, tiles, 2 * P], U32, name="fg_codes", align_bytes=64)
-                exps = work.tile([P, tiles, 2 * P], U8, name="fg_exps", align_bytes=64)
+                codes = work.tile([P, tiles, 2 * P], U32, name="fg_codes", align_bytes=256)
+                exps = work.tile([P, tiles, 2 * P], U8, name="fg_exps", align_bytes=256)
                 quantize(codes[:].rearrange("p i c -> p (i c)"), exps[:].rearrange("p i c -> p (i c)"),
                          fg_inter[i // 2][:, i % 2:i % 2 + tiles].rearrange("p i k n t -> p (i k n t)"))
                 for e in range(tiles):
@@ -162,8 +162,8 @@ def tile_incrementalpredictivecodingupdate_kernel(tc, x1, x2, w1_bytes, w1_scale
                                         in1=pi_gain[:].unsqueeze(1).to_broadcast([P, P, 4]), op=ALU.mult)
 
             def quant_ep(i):
-                codes = work.tile([P, P], U32, name="ep_codes", align_bytes=64, bufs=4)
-                exps = work.tile([P, P], U8, name="ep_exps", align_bytes=64, bufs=4)
+                codes = work.tile([P, P], U32, name="ep_codes", align_bytes=256, bufs=4)
+                exps = work.tile([P, P], U8, name="ep_exps", align_bytes=256, bufs=4)
                 quantize(codes[:], exps[:], ep_inter[i][:].rearrange("p n t -> p (n t)"))
                 ep_quant[i] = (codes, exps)
 

@@ -18,11 +18,14 @@ ACT = mybir.ActivationFunctionType
 
 HALF = 512
 PIECE = 256
-GP_COLS = 608
-REST_COLS = Q - GP_COLS
-REST_ON_TENSOR = (0, 2, 4, 5)
-W1_VECTOR_COLS = 320
-V1_GPSIMD_COLS = 192
+REST_ON_TENSOR = (0, 5)
+REST_ON_VECTOR = (1, 2, 3, 4)
+GP_COLS = {0: 608, 1: 736, 2: 736, 3: 736, 4: 736, 5: 512}
+GATE = 64
+EC_FIRST_COLS = 256
+W1_VECTOR_COLS = 96
+EC_GPSIMD_COLS = 224
+EC_SCALAR_COLS = 160
 
 
 def tile_incrementalpredictivecodingupdate_kernel(tc, x1, x2, w1_bytes, w1_scale, v1, g, pi2, a, c, out_0, out_1):
@@ -35,7 +38,7 @@ def tile_incrementalpredictivecodingupdate_kernel(tc, x1, x2, w1_bytes, w1_scale
 
     with ExitStack() as ctx:
         keep = ctx.enter_context(tc.tile_pool(name="keep", bufs=1))
-        work = ctx.enter_context(tc.tile_pool(name="work", bufs=2))
+        work = ctx.enter_context(tc.tile_pool(name="work", bufs=1))
         psum = ctx.enter_context(tc.psum_pool(name="psum", bufs=1))
 
         x1s = [keep.tile([P, Q], BF16, name="x1s%d" % i) for i in range(8)]
@@ -48,38 +51,41 @@ def tile_incrementalpredictivecodingupdate_kernel(tc, x1, x2, w1_bytes, w1_scale
         c_gain = keep.tile([P, 2, 4], BF16, name="c_gain")
         pi_gain = keep.tile([P, 4], BF16, name="pi_gain")
         a_f32 = keep.tile([P, 2, 4], F32, name="a_f32")
+        c_f32 = keep.tile([P, 4], F32, name="c_f32")
         ident = keep.tile([P, P], F32, name="ident")
         minus_half = keep.tile([P, P], BF16, name="minus_half")
         ident_bf16 = keep.tile([P, P], BF16, name="ident_bf16")
 
         f = [keep.tile([P, 4, Q], F32, name="f%d" % k) for k in (0, 1)]
         eps = [keep.tile([P, 4, R], F32, name="eps%d" % k) for k in (0, 1)]
-        w1_planes = [keep.tile([P, 4, R], BF16, name="w1_planes%d" % k) for k in (0, 1)]
         w1_codes = keep.tile([P, 2 * R], U32, name="w1_codes", align_bytes=256)
         w1_exps = keep.tile([P, 2 * R], U8, name="w1_exps", align_bytes=256)
         v1_codes = keep.tile([P, Q], U32, name="v1_codes", align_bytes=256)
         v1_exps = keep.tile([P, Q], U8, name="v1_exps", align_bytes=256)
+        fg_codes = keep.tile([P, 8 * 2 * P], U32, name="fg_codes", align_bytes=256)
+        fg_exps = keep.tile([P, 8 * 2 * P], U8, name="fg_exps", align_bytes=256)
+        ep_codes = keep.tile([P, 8 * P], U32, name="ep_codes", align_bytes=256)
+        ep_exps = keep.tile([P, 8 * P], U8, name="ep_exps", align_bytes=256)
         fa_codes = keep.tile([P, 2 * Q], U32, name="fa_codes", align_bytes=256)
         fa_exps = keep.tile([P, 2 * Q], U8, name="fa_exps", align_bytes=256)
         ec_codes = keep.tile([P, 2 * R], U32, name="ec_codes", align_bytes=256)
         ec_exps = keep.tile([P, 2 * R], U8, name="ec_exps", align_bytes=256)
         a_diag = keep.tile([P, 4, P], F32, name="a_diag")
-        fa_planes = keep.tile([P, 4, Q], BF16, name="fa_planes")
-        w1_inter0 = keep.tile([P, R, 4], BF16, name="w1_inter0", align_bytes=64)
-        v1_inter1 = keep.tile([P, HALF, 4], BF16, name="v1_inter1", align_bytes=64)
 
         def bank(b, shape):
             return psum.tile(shape, F32, name="bank%d" % b)
 
         def gpsimd_tile(columns):
-            return work.tile([P, columns, 4], BF16, name="gpsimd_out", bufs=1, align_bytes=64)
+            return work.tile([P, columns, 4], BF16, name="gpsimd_out", align_bytes=64)
 
-        def quantize(codes, exps, inter):
-            nc.vector.quantize_mx(out=codes.bitcast(FP8X4), scales=exps, in_=inter)
+        def quantize(codes, exps, first, inter):
+            cols = slice(first, first + inter.shape[1] // 4)
+            nc.vector.quantize_mx(out=codes[:, cols].bitcast(FP8X4), scales=exps[:, cols], in_=inter)
 
-        def mx_pass(out, lhs_codes, lhs_exps, rhs_codes, rhs_exps, start, stop):
-            nc.tensor.matmul_mx(out=out, lhsT=lhs_codes.bitcast(FP8X4), lhsT_scale=lhs_exps,
-                                rhs=rhs_codes.bitcast(FP8X4), rhs_scale=rhs_exps, start=start, stop=stop)
+        def mx_pass(out, lhs, lhs_first, rhs, rhs_first, start, stop):
+            lhs_cols, rhs_cols = slice(lhs_first, lhs_first + P), slice(rhs_first, rhs_first + HALF)
+            nc.tensor.matmul_mx(out=out, lhsT=lhs[0][:, lhs_cols].bitcast(FP8X4), lhsT_scale=lhs[1][:, lhs_cols],
+                                rhs=rhs[0][:, rhs_cols].bitcast(FP8X4), rhs_scale=rhs[1][:, rhs_cols], start=start, stop=stop)
 
         def interleave(copy, out, planes):
             copy(out=out.rearrange("p (c i) t -> p c t i", i=4), in_=planes.rearrange("p t (c i) -> p c t i", i=4))
@@ -87,29 +93,19 @@ def tile_incrementalpredictivecodingupdate_kernel(tc, x1, x2, w1_bytes, w1_scale
         def gpsimd_copy(out, in_):
             nc.gpsimd.tensor_scalar(out=out, in0=in_, scalar1=1.0, scalar2=0.0, op0=ALU.mult, op1=ALU.add)
 
-        def gain_and_interleave(engine, out, planes, gain):
-            columns = out.shape[1]
-            engine.tensor_tensor(out=out.rearrange("p (c i) t -> p c t i", i=4),
-                                 in0=planes.rearrange("p t (c i) -> p c t i", i=4),
-                                 in1=gain.unsqueeze(1).unsqueeze(3).to_broadcast([P, columns // 4, 4, 4]), op=ALU.mult)
-
         with tc.manual_schedule():
             def load_x1(i):
                 nc.sync.dma_start(out=x1s[i][:], in_=x1_rows[i // 4][:, i % 4, :])
 
             def widen_w1(k, t):
-                nc.vector.tensor_scalar(out=w1_planes[k][:, t, :], in0=w1b[k][:, t, :].bitcast(FP8),
+                nc.vector.tensor_scalar(out=w1_planes[:, t, k, :], in0=w1b[k][:, t, :].bitcast(FP8),
                                         scalar1=w1_gain[:, k, t:t + 1], scalar2=None, op0=ALU.mult)
-
-            def quant_w1(k, inter):
-                cols = slice(k * R, (k + 1) * R)
-                quantize(w1_codes[:, cols], w1_exps[:, cols], inter[:].rearrange("p r t -> p (r t)"))
 
             def tanh(i):
                 nc.scalar.activation(out=f[i // 4][:, i % 4, :].rearrange("p (u b j) -> p b u j", u=4, j=4),
                                      in_=x1s[i][:].rearrange("p (b j u) -> p b u j", u=4, j=4), func=ACT.Tanh)
 
-            f_turned, fg_inter, fg_quant, mu = {}, {}, {}, {}
+            f_turned, fg_inter, mu = {}, {}, {}
 
             def turn_f(i, b):
                 for k in (0, 1):
@@ -118,38 +114,27 @@ def tile_incrementalpredictivecodingupdate_kernel(tc, x1, x2, w1_bytes, w1_scale
                         nc.tensor.transpose(turned[:, t, :], f[i // 4][:, i % 4, (2 * t + k) * P:(2 * t + k + 1) * P], ident[:])
                     f_turned[i, k] = turned
 
-            def gain_g(i):
-                if i % 2 == 0:
-                    fg_inter[i // 2] = work.tile([P, 2, 2, P, 4], BF16, name="fg_inter", align_bytes=64)
-                for k in (0, 1):
-                    nc.vector.tensor_tensor(out=fg_inter[i // 2][:, i % 2, k], in0=f_turned[i, k][:].rearrange("p t n -> p n t"),
+            def gain_g(i, passes=(0, 1)):
+                if i // 4 not in fg_inter:
+                    fg_inter[i // 4] = work.tile([P, 4, 2, P, 4], BF16, name="fg_inter", bufs=2, align_bytes=64)
+                for k in passes:
+                    nc.vector.tensor_tensor(out=fg_inter[i // 4][:, i % 4, k], in0=f_turned[i, k][:].rearrange("p t n -> p n t"),
                                             in1=g_gain[:, k, :].unsqueeze(1).to_broadcast([P, P, 4]), op=ALU.mult)
 
-            def quant_fg(i, tiles=1):
-                codes = work.tile([P, tiles, 2 * P], U32, name="fg_codes", align_bytes=256)
-                exps = work.tile([P, tiles, 2 * P], U8, name="fg_exps", align_bytes=256)
-                quantize(codes[:].rearrange("p i c -> p (i c)"), exps[:].rearrange("p i c -> p (i c)"),
-                         fg_inter[i // 2][:, i % 2:i % 2 + tiles].rearrange("p i k n t -> p (i k n t)"))
-                for e in range(tiles):
-                    fg_quant[i + e] = (codes[:, e], exps[:, e])
+            def quant_fg(i, tiles):
+                quantize(fg_codes, fg_exps, 2 * P * i, fg_inter[i // 4][:, i % 4:i % 4 + tiles].rearrange("p i k n t -> p (i k n t)"))
 
             def matmul_mu(i, b):
                 mu[i] = bank(b, [P, R])
-                codes, exps = fg_quant[i]
                 for k in (0, 1):
-                    mx_pass(mu[i][:], codes[:, k * P:(k + 1) * P], exps[:, k * P:(k + 1) * P],
-                            w1_codes[:, k * R:(k + 1) * R], w1_exps[:, k * R:(k + 1) * R], k == 0, k == 1)
+                    mx_pass(mu[i][:], (fg_codes, fg_exps), (2 * i + k) * P, (w1_codes, w1_exps), k * R, k == 0, k == 1)
 
             def error(i):
                 nc.vector.tensor_tensor(out=eps[i // 4][:, i % 4, :].rearrange("p (u b j) -> p b u j", u=4, j=4),
                                         in0=x2s[i // 4][:, i % 4, :].rearrange("p (b j u) -> p b u j", u=4, j=4),
                                         in1=mu[i][:].rearrange("p (b j u) -> p b u j", u=4, j=4), op=ALU.subtract)
 
-            eps_turned, ep_inter, ep_quant, back, half_sq, u, half_x, x_new, sums = {}, {}, {}, {}, {}, {}, {}, {}, {}
-
-            def quant_v1(h, inter):
-                cols = slice(h * HALF, (h + 1) * HALF)
-                quantize(v1_codes[:, cols], v1_exps[:, cols], inter[:].rearrange("p q t -> p (q t)"))
+            eps_turned, ep_inter, back, half_sq, u, half_x, x_new, sums = {}, {}, {}, {}, {}, {}, {}, {}
 
             def turn_eps(i, b):
                 eps_turned[i] = bank(b, [P, 4, P])
@@ -157,31 +142,29 @@ def tile_incrementalpredictivecodingupdate_kernel(tc, x1, x2, w1_bytes, w1_scale
                     nc.tensor.transpose(eps_turned[i][:, t, :], eps[i // 4][:, i % 4, t * P:(t + 1) * P], ident[:])
 
             def gain_pi(i):
-                ep_inter[i] = work.tile([P, P, 4], BF16, name="ep_inter", align_bytes=64, bufs=4)
-                nc.vector.tensor_tensor(out=ep_inter[i][:], in0=eps_turned[i][:].rearrange("p t n -> p n t"),
+                if i // 4 not in ep_inter:
+                    ep_inter[i // 4] = work.tile([P, 4, P, 4], BF16, name="ep_inter", bufs=2, align_bytes=64)
+                nc.vector.tensor_tensor(out=ep_inter[i // 4][:, i % 4], in0=eps_turned[i][:].rearrange("p t n -> p n t"),
                                         in1=pi_gain[:].unsqueeze(1).to_broadcast([P, P, 4]), op=ALU.mult)
 
-            def quant_ep(i):
-                codes = work.tile([P, P], U32, name="ep_codes", align_bytes=256, bufs=4)
-                exps = work.tile([P, P], U8, name="ep_exps", align_bytes=256, bufs=4)
-                quantize(codes[:], exps[:], ep_inter[i][:].rearrange("p n t -> p (n t)"))
-                ep_quant[i] = (codes, exps)
+            def quant_ep(i, tiles):
+                quantize(ep_codes, ep_exps, P * i, ep_inter[i // 4][:, i % 4:i % 4 + tiles].rearrange("p i n t -> p (i n t)"))
 
-            def matmul_back(i):
-                codes, exps = ep_quant[i]
+            def matmul_back(i, banks):
                 for h in (0, 1):
-                    cols = slice(h * HALF, (h + 1) * HALF)
-                    back[i, h] = bank((6, 2)[i % 2] + h, [P, HALF])
-                    mx_pass(back[i, h][:], codes[:], exps[:], v1_codes[:, cols], v1_exps[:, cols], True, True)
+                    back[i, h] = bank(banks[h], [P, HALF])
+                    mx_pass(back[i, h][:], (ep_codes, ep_exps), i * P, (v1_codes, v1_exps), h * HALF, True, True)
 
-            def square(i):
-                half_sq[i] = work.tile([P, Q], F32, name="half_sq", bufs=4)
-                nc.scalar.activation(out=half_sq[i][:].rearrange("p (b j u) -> p b u j", j=4, u=4),
-                                     in_=f[i // 4][:, i % 4, :].rearrange("p (u b j) -> p b u j", u=4, j=4),
+            def square(i, halves=(0, 1)):
+                if i not in half_sq:
+                    half_sq[i] = work.tile([P, Q], F32, name="half_sq", bufs=4)
+                lines = slice(halves[0] * HALF // 16, (halves[-1] + 1) * HALF // 16)
+                nc.scalar.activation(out=half_sq[i][:].rearrange("p (b j u) -> p b u j", j=4, u=4)[:, lines],
+                                     in_=f[i // 4][:, i % 4, :].rearrange("p (u b j) -> p b u j", u=4, j=4)[:, lines],
                                      func=ACT.Square, scale=0.5 ** 0.5)
 
             def slope_back(i, h):
-                if h == 0:
+                if i not in u:
                     u[i] = work.tile([P, Q], F32, name="u", bufs=4)
                 cols = slice(h * HALF, (h + 1) * HALF)
                 nc.vector.scalar_tensor_tensor(out=u[i][:, cols], in0=half_sq[i][:, cols], scalar=0.5, in1=back[i, h][:],
@@ -192,29 +175,44 @@ def tile_incrementalpredictivecodingupdate_kernel(tc, x1, x2, w1_bytes, w1_scale
                     x_new[i] = work.tile([P, Q], F32, name="x_new", bufs=4)
                 return x_new[i]
 
-            def halve_x(i):
-                half_x[i] = work.tile([P, GP_COLS], BF16, name="half_x", bufs=2)
-                nc.vector.tensor_scalar(out=half_x[i][:], in0=x1s[i][:, REST_COLS:], scalar1=0.5, scalar2=None, op0=ALU.mult)
+            def rest_cols(i):
+                return Q - GP_COLS[i]
+
+            def halve_x(i, lo=0, hi=None):
+                first = rest_cols(i)
+                hi = hi or Q - first
+                if lo == 0:
+                    half_x[i] = work.tile([P, Q - first], BF16, name="half_x", bufs=4)
+                nc.vector.tensor_scalar(out=half_x[i][:, lo:hi], in0=x1s[i][:, first + lo:first + hi],
+                                        scalar1=0.5, scalar2=None, op0=ALU.mult)
 
             def state_gpsimd(i):
-                nc.gpsimd.tensor_tensor(out=x_new_tile(i)[:, REST_COLS:], in0=half_x[i][:], in1=u[i][:, REST_COLS:], op=ALU.subtract)
+                first = rest_cols(i)
+                nc.gpsimd.tensor_tensor(out=x_new_tile(i)[:, first:], in0=half_x[i][:], in1=u[i][:, first:], op=ALU.subtract)
 
             def state_vector(i, lo, hi):
                 nc.vector.scalar_tensor_tensor(out=x_new_tile(i)[:, lo:hi], in0=x1s[i][:, lo:hi], scalar=0.5, in1=u[i][:, lo:hi],
                                                op0=ALU.mult, op1=ALU.subtract)
 
-            def state_sum(i, b):
-                sums[i] = bank(b, [P, REST_COLS])
-                nc.tensor.matmul(sums[i][:], lhsT=minus_half[:], rhs=x1s[i][:, :REST_COLS], start=True, stop=False)
-                nc.tensor.matmul(sums[i][:], lhsT=ident[:], rhs=u[i][:, :REST_COLS], start=False, stop=True)
+            def lay_x(i, lo, hi, b, stop=True):
+                sums[i, lo] = bank(b, [P, hi - lo])
+                nc.tensor.matmul(sums[i, lo][:], lhsT=minus_half[:], rhs=x1s[i][:, lo:hi], start=True, stop=stop)
 
-            def state_sum_out(i):
-                nc.scalar.activation(out=x_new_tile(i)[:, :REST_COLS], in_=sums[i][:], func=ACT.Copy, scale=-1.0)
+            def state_from_bank(i, lo, hi):
+                nc.vector.scalar_tensor_tensor(out=x_new_tile(i)[:, lo:hi], in0=sums[i, lo][:], scalar=-1.0, in1=u[i][:, lo:hi],
+                                               op0=ALU.mult, op1=ALU.subtract)
 
-            def store_x(i, lo, hi):
+            def state_sum(i, lo, hi, b):
+                lay_x(i, lo, hi, b, stop=False)
+                nc.tensor.matmul(sums[i, lo][:], lhsT=ident[:], rhs=u[i][:, lo:hi], start=False, stop=True)
+
+            def state_sum_out(i, lo, hi):
+                nc.scalar.activation(out=x_new_tile(i)[:, lo:hi], in_=sums[i, lo][:], func=ACT.Copy, scale=-1.0)
+
+            def store_x(i, lo=0, hi=Q):
                 nc.sync.dma_start(out=x_new_rows[i // 4][:, i % 4, lo:hi], in_=x_new[i][:, lo:hi])
 
-            fa_piece, ec_piece, fa_scaled, dw = {}, {}, {}, {}
+            fa_piece, ec_inter, fa_scaled, dw, dw_out = {}, {}, {}, {}, {}
 
             def fa_tile(n):
                 if n not in fa_piece:
@@ -222,42 +220,50 @@ def tile_incrementalpredictivecodingupdate_kernel(tc, x1, x2, w1_bytes, w1_scale
                 return fa_piece[n]
 
             def quant_fa(n):
-                cols = slice(2 * n * PIECE, 2 * (n + 1) * PIECE)
-                quantize(fa_codes[:, cols], fa_exps[:, cols], fa_piece[n][:].rearrange("p k q t -> p (k q t)"))
+                quantize(fa_codes, fa_exps, 2 * n * PIECE, fa_piece[n][:].rearrange("p k q t -> p (k q t)"))
 
-            def quant_ec(k, n):
-                cols = slice(k * R + n * PIECE, k * R + (n + 1) * PIECE)
-                quantize(ec_codes[:, cols], ec_exps[:, cols], ec_piece[k, n][:].rearrange("p r t -> p (r t)"))
-
-            def scale_fa0(e):
-                fa_scaled[e] = bank(e % 2, [P, 4, P])
-                for t in range(4):
+            def scale_fa0(e, planes=range(4)):
+                if e not in fa_scaled:
+                    fa_scaled[e] = bank(6 + e % 2, [P, 4, P])
+                for t in planes:
                     nc.tensor.matmul(fa_scaled[e][:, t, :], lhsT=a_diag[:, t, :], rhs=f[0][:, t, e * P:(e + 1) * P], start=True, stop=True)
 
             def scale_fa0_out(e):
                 nc.scalar.copy(out=fa_tile(e // 2)[:, 0, e % 2 * P:(e % 2 + 1) * P, :], in_=fa_scaled[e][:].rearrange("p t q -> p q t"))
 
+            def plane_fa1(t):
+                nc.scalar.activation(out=fa_planes[:, t, :], in_=f[1][:, t, :], func=ACT.Copy, scale=a_f32[:, 1, t:t + 1])
+
             def interleave_fa1(n):
                 interleave(nc.scalar.copy, fa_tile(n)[:, 1], fa_planes[:, :, n * PIECE:(n + 1) * PIECE])
 
-            def gain_c_gpsimd(k, n):
-                ec_piece[k, n] = gpsimd_tile(PIECE)
-                gain_and_interleave(nc.gpsimd, ec_piece[k, n][:], eps[k][:, :, n * PIECE:(n + 1) * PIECE], c_gain[:, k, :])
+            def gain_c(engine, k, lo, hi, gain):
+                if engine is nc.gpsimd:
+                    ec_inter[k, lo] = gpsimd_tile(R)
+                engine.tensor_tensor(out=ec_inter[k, lo if k == 0 else 0][:, lo:hi].rearrange("p (c i) t -> p c t i", i=4),
+                                     in0=eps[k][:, :, lo:hi].rearrange("p t (c i) -> p c t i", i=4),
+                                     in1=gain.unsqueeze(1).unsqueeze(3).to_broadcast([P, (hi - lo) // 4, 4, 4]), op=ALU.mult)
+
+            def quant_ec_first():
+                quantize(ec_codes, ec_exps, 0, ec_inter[0, 0][:, :EC_FIRST_COLS].rearrange("p r t -> p (r t)"))
+
+            def quant_ec(k):
+                lo = EC_FIRST_COLS if k == 0 else 0
+                quantize(ec_codes, ec_exps, k * R + lo, ec_inter[k, lo][:, lo:].rearrange("p r t -> p (r t)"))
 
             def matmul_dw(m, b):
                 dw[m] = bank(b, [P, R])
                 for k in (0, 1):
-                    first = (m // 2 * 2 + k) * PIECE + m % 2 * P
-                    cols = slice(first, first + P)
-                    mx_pass(dw[m][:], fa_codes[:, cols], fa_exps[:, cols],
-                            ec_codes[:, k * R:(k + 1) * R], ec_exps[:, k * R:(k + 1) * R], k == 0, k == 1)
+                    mx_pass(dw[m][:], (fa_codes, fa_exps), (m // 2 * 2 + k) * PIECE + m % 2 * P, (ec_codes, ec_exps), k * R, k == 0, k == 1)
 
             def store_dw(m):
-                pair = work.tile([P, 2, R], F32, name="dw_pair", bufs=3)
+                if m % 2 == 0:
+                    dw_out[m // 4] = work.tile([P, 2, 2, R], F32, name="fg_inter", bufs=2, align_bytes=64)
+                pair = dw_out[m // 4][:, m % 2]
                 for e in (0, 1):
                     nc.scalar.activation(out=pair[:, e, :].rearrange("p (m u) -> p m u", u=4),
                                          in_=dw[m + 2 * e][:].rearrange("p (u m) -> p m u", u=4), func=ACT.Copy, scale=1.0 / 32.0)
-                nc.sync.dma_start(out=dw_rows[m % 2][:, m // 2:m // 2 + 2, :], in_=pair[:])
+                nc.sync.dma_start(out=dw_rows[m % 2][:, m // 2:m // 2 + 2, :], in_=pair)
 
             def load_gain(gain, values):
                 nc.sync.dma_start(out=gain[:], in_=values.rearrange("(g p t) -> p g t", p=P, t=4))
@@ -280,153 +286,168 @@ def tile_incrementalpredictivecodingupdate_kernel(tc, x1, x2, w1_bytes, w1_scale
             nc.vector.tensor_copy(out=ident_bf16[:], in_=ident[:])
             nc.vector.tensor_scalar(out=minus_half[:], in0=ident[:], scalar1=-0.5, scalar2=None, op0=ALU.mult)
 
-            w1_inter1 = gpsimd_tile(R)
+            w1_planes = work.tile([P, 4, 2, R], BF16, name="planes")
             for k in (0, 1):
                 for t in range(4):
+                    if (k, t) == (1, 3):
+                        halve_x(0, 0, GP_COLS[0] - GATE)
                     widen_w1(k, t)
-            interleave(nc.vector.tensor_copy, w1_inter0[:, :W1_VECTOR_COLS], w1_planes[0][:, :, :W1_VECTOR_COLS])
-            interleave(gpsimd_copy, w1_inter1[:], w1_planes[1][:])
-            interleave(gpsimd_copy, w1_inter0[:, W1_VECTOR_COLS:], w1_planes[0][:, :, W1_VECTOR_COLS:])
+            w1_inter = gpsimd_tile(2 * R)
+            planes = w1_planes[:].rearrange("p t k r -> p t (k r)")
+            interleave(nc.vector.tensor_copy, w1_inter[:, :W1_VECTOR_COLS], planes[:, :, :W1_VECTOR_COLS])
+            interleave(gpsimd_copy, w1_inter[:, W1_VECTOR_COLS:], planes[:, :, W1_VECTOR_COLS:])
             for i in range(3):
                 tanh(i)
             nc.scalar.copy(out=a_f32[:], in_=a_gain[:])
             tanh(3)
             for i in range(4):
-                turn_f(i, 2 * i)
+                turn_f(i, (6, 0, 2, 4)[i])
                 gain_g(i)
             for t in range(4):
                 nc.scalar.activation(out=a_diag[:, t, :], in_=ident[:], func=ACT.Copy, scale=a_f32[:, 0, t:t + 1])
             scale_fa0(0)
             for i in range(4, 8):
                 tanh(i)
-            turn_f(4, 2)
+            turn_f(4, 0)
             scale_fa0_out(0)
-            quant_fg(0, tiles=2)
-            quant_w1(0, w1_inter0)
-            quant_w1(1, w1_inter1)
-            quant_fg(2, tiles=2)
+            quant_fg(0, 2)
+            quantize(w1_codes, w1_exps, 0, w1_inter[:].rearrange("p r t -> p (r t)"))
+            quant_fg(2, 2)
             for i in range(4):
-                matmul_mu(i, 4 + i)
+                matmul_mu(i, 2 + i)
 
-            v1_inter0 = gpsimd_tile(HALF)
-            interleave(gpsimd_copy, v1_inter0[:], v1s[:, :, :HALF])
-            interleave(gpsimd_copy, v1_inter1[:, :V1_GPSIMD_COLS], v1s[:, :, HALF:HALF + V1_GPSIMD_COLS])
+            v1_inter = gpsimd_tile(Q)
+            interleave(gpsimd_copy, v1_inter[:], v1s[:])
+            fa_planes = work.tile([P, 4, Q], BF16, name="planes")
             for t in range(4):
-                nc.scalar.activation(out=fa_planes[:, t, :], in_=f[1][:, t, :], func=ACT.Copy, scale=a_f32[:, 1, t:t + 1])
+                plane_fa1(t)
             gain_g(4)
-            turn_f(5, 2)
-            scale_fa0(1)
+            turn_f(5, 0)
             for i in range(4):
                 error(i)
-            gain_g(5)
-            turn_f(7, 6)
             turn_f(6, 2)
-            scale_fa0_out(1)
-            quant_fg(4)
-            quant_v1(0, v1_inter0)
-            quant_fg(5)
-            matmul_mu(4, 4)
-            matmul_mu(5, 5)
+            scale_fa0(1)
+            turn_f(7, 4)
             scale_fa0(2)
+            gain_g(5)
+            gain_g(6, (0,))
+            scale_fa0_out(1)
+            quant_fg(4, 1)
+            matmul_mu(4, 0)
+            turn_eps(0, 2)
+            quantize(v1_codes, v1_exps, 0, v1_inter[:].rearrange("p q t -> p (q t)"))
+            quant_fg(5, 1)
+            matmul_mu(5, 1)
             scale_fa0(3)
 
-            gain_c_gpsimd(0, 0)
-            interleave(nc.scalar.copy, v1_inter1[:, V1_GPSIMD_COLS:], v1s[:, :, HALF + V1_GPSIMD_COLS:])
+            gain_c(nc.gpsimd, 0, 0, EC_FIRST_COLS, c_gain[:, 0, :])
             interleave_fa1(0)
-            interleave_fa1(1)
             scale_fa0_out(2)
-            scale_fa0_out(3)
-            gain_g(6)
-            error(4)
-            turn_eps(0, 2)
-            turn_eps(1, 3)
-            gain_g(7)
-            quant_fg(6)
-            quant_ec(0, 0)
-            quant_fg(7)
-            matmul_mu(6, 4)
-
-            gain_c_gpsimd(0, 1)
-            error(5)
+            interleave_fa1(1)
+            nc.scalar.copy(out=c_f32[:], in_=c_gain[:, 1, :])
             square(0)
-            matmul_mu(7, 5)
-            scale_fa0(4)
-            scale_fa0(5)
+            scale_fa0_out(3)
+            gain_g(6, (1,))
+            error(4)
             gain_pi(0)
-            error(6)
-            gain_pi(1)
-            error(7)
-            scale_fa0_out(4)
-            interleave_fa1(2)
-            scale_fa0_out(5)
+            turn_eps(1, 3)
+            turn_eps(2, 0)
+            gain_g(7)
+            quant_fg(6, 1)
+            matmul_mu(6, 2)
+            quant_ec_first()
+            quant_fg(7, 1)
+            matmul_mu(7, 4)
+            scale_fa0(4)
+            gain_c(nc.gpsimd, 0, EC_FIRST_COLS, R, c_gain[:, 0, :])
             square(1)
-            c_bank = bank(5, [P, 4])
+            error(5)
+            scale_fa0(5)
+            gain_pi(1)
+            error(6)
+            gain_pi(2)
+            error(7)
+            interleave_fa1(2)
+            scale_fa0_out(4)
+            ec_planes = work.tile([P, 4, EC_SCALAR_COLS], BF16, name="ec_planes")
+            for t in range(4):
+                nc.scalar.activation(out=ec_planes[:, t, :], in_=eps[1][:, t, R - EC_SCALAR_COLS:], func=ACT.Copy, scale=c_f32[:, t:t + 1])
+            scale_fa0_out(5)
+            c_bank = bank(3, [P, 4])
             nc.tensor.matmul(c_bank[:], lhsT=ident_bf16[:], rhs=c_gain[:, 1, :], start=True, stop=True)
-            turn_eps(2, 4)
-            quant_ep(0)
-            quant_v1(1, v1_inter1)
-            quant_ep(1)
-            matmul_back(0)
-            matmul_back(1)
+            turn_eps(3, 4)
+            quant_ep(0, 3)
+            matmul_back(0, (5, 0))
+            matmul_back(1, (1, 2))
             scale_fa0(6)
             scale_fa0(7)
             quant_fa(0)
-            quant_ec(0, 1)
+            quant_ec(0)
             quant_fa(1)
-            ec_inter1 = gpsimd_tile(R)
-            gain_and_interleave(nc.gpsimd, ec_inter1[:, :PIECE], eps[1][:, :, :PIECE], c_gain[:, 1, :])
-            gain_and_interleave(nc.vector, ec_inter1[:, PIECE:], eps[1][:, :, PIECE:], c_bank[:])
-            scale_fa0_out(6)
-            interleave_fa1(3)
-            scale_fa0_out(7)
-            square(2)
 
+            gain_c(nc.gpsimd, 1, 0, EC_GPSIMD_COLS, c_gain[:, 1, :])
+            gain_c(nc.vector, 1, EC_GPSIMD_COLS, R - EC_SCALAR_COLS, c_bank[:])
+            interleave(nc.scalar.copy, ec_inter[1, 0][:, R - EC_SCALAR_COLS:], ec_planes[:])
+            square(2)
+            scale_fa0_out(6)
+            scale_fa0_out(7)
+            interleave_fa1(3)
             for j in range(6):
                 if j >= 1:
                     state_gpsimd(j - 1)
-                if j - 1 in REST_ON_TENSOR:
-                    state_sum_out(j - 1)
-                if j == 5:
-                    square(7)
-                gain_pi(j + 2)
+                if j == 1:
+                    state_sum_out(0, 0, rest_cols(0))
+                    square(3, (0,))
+                if j < 5:
+                    gain_pi(j + 3)
+                if j < 2:
+                    turn_eps(j + 4, 4)
                 if 1 <= j <= 4:
                     m = (j - 1) // 2 * 4 + (j - 1) % 2
-                    matmul_dw(m, 5)
-                    matmul_dw(m + 2, 1)
-                if j + 3 < 8:
-                    turn_eps(j + 3, 4)
+                    matmul_dw(m, 6)
+                    matmul_dw(m + 2, 7)
+                    if j in (2, 3):
+                        turn_eps(j + 4, 4)
+                    matmul_back(j + 1, ((5, 0), (1, 2))[(j + 1) % 2])
+                if j == 5:
+                    matmul_back(6, (5, 0))
+                    matmul_back(7, (6, 7))
+                    lay_x(6, 0, HALF, 3)
                 slope_back(j, 0)
+                if j - 1 in REST_ON_VECTOR:
+                    state_from_bank(j - 1, 0, rest_cols(j - 1))
                 slope_back(j, 1)
                 if j >= 1:
-                    store_x(j - 1, 0, Q)
+                    store_x(j - 1)
+                if j in REST_ON_TENSOR:
+                    state_sum(j, 0, rest_cols(j), {0: 3, 5: 1}[j])
+                else:
+                    lay_x(j, 0, rest_cols(j), 4 if j == 4 else 3)
                 if 1 <= j <= 4:
                     store_dw(m)
-                    square(j + 2)
-                if j in REST_ON_TENSOR:
-                    state_sum(j, 1 if j == 5 else 0)
-                run = [(quant_ep, j + 2)]
+                    square(j + 2, (1,))
+                    square(j + 3, (0,) if j < 4 else (0, 1))
                 if j == 0:
-                    run = run + [(quantize, ec_codes[:, R:], ec_exps[:, R:], ec_inter1[:].rearrange("p r t -> p (r t)"))]
+                    quant_ec(1)
+                    halve_x(0, GP_COLS[0] - GATE, GP_COLS[0])
                 if j in (1, 2):
-                    run = run + [(quant_fa, j + 1)]
-                if j not in REST_ON_TENSOR:
-                    run = run + [(state_vector, j, 0, REST_COLS)]
-                run = run[:-1] + [(halve_x, j)] + run[-1:]
-                for call in run:
-                    call[0](*call[1:])
-                matmul_back(j + 2)
+                    quant_fa(j + 1)
+                if j == 3:
+                    halve_x(5)
+                if 1 <= j <= 4:
+                    halve_x(j)
+                if j < 5:
+                    quant_ep(j + 3, 1)
 
             state_gpsimd(5)
-            state_sum_out(5)
+            state_sum_out(5, 0, rest_cols(5))
             slope_back(6, 0)
             slope_back(6, 1)
-            state_sum(6, 5)
             slope_back(7, 0)
-            store_x(5, 0, Q)
-            state_vector(6, REST_COLS, Q)
-            state_sum_out(6)
+            store_x(5)
+            state_from_bank(6, 0, HALF)
+            store_x(6, 0, HALF)
             slope_back(7, 1)
-            store_x(6, 0, Q)
-            for h in (0, 1):
-                state_vector(7, h * HALF, (h + 1) * HALF)
-                store_x(7, h * HALF, (h + 1) * HALF)
+            for i, h in ((6, 1), (7, 0), (7, 1)):
+                state_vector(i, h * HALF, (h + 1) * HALF)
+                store_x(i, h * HALF, (h + 1) * HALF)

@@ -20,10 +20,11 @@ HALF = 512
 PIECE = 256
 REST_ON_TENSOR = (0, 5)
 REST_ON_VECTOR = (1, 2, 3, 4)
-GP_COLS = {0: 608, 1: 736, 2: 736, 3: 736, 4: 736, 5: 512}
+GP_COLS = {0: 608, 1: 736, 2: 736, 3: 736, 4: 736, 5: 640}
 GATE = 64
 EC_FIRST_COLS = 256
 W1_VECTOR_COLS = 96
+V1_SCALAR_QUADS = 24
 EC_GPSIMD_COLS = 224
 EC_SCALAR_COLS = 160
 
@@ -54,6 +55,7 @@ def tile_incrementalpredictivecodingupdate_kernel(tc, x1, x2, w1_bytes, w1_scale
         c_f32 = keep.tile([P, 4], F32, name="c_f32")
         ident = keep.tile([P, P], F32, name="ident")
         minus_half = keep.tile([P, P], BF16, name="minus_half")
+        plus_half = keep.tile([P, P], BF16, name="plus_half")
         ident_bf16 = keep.tile([P, P], BF16, name="ident_bf16")
 
         f = [keep.tile([P, 4, Q], F32, name="f%d" % k) for k in (0, 1)]
@@ -158,10 +160,16 @@ def tile_incrementalpredictivecodingupdate_kernel(tc, x1, x2, w1_bytes, w1_scale
             def square(i, halves=(0, 1)):
                 if i not in half_sq:
                     half_sq[i] = work.tile([P, Q], F32, name="half_sq", bufs=4)
-                lines = slice(halves[0] * HALF // 16, (halves[-1] + 1) * HALF // 16)
-                nc.scalar.activation(out=half_sq[i][:].rearrange("p (b j u) -> p b u j", j=4, u=4)[:, lines],
-                                     in_=f[i // 4][:, i % 4, :].rearrange("p (u b j) -> p b u j", u=4, j=4)[:, lines],
+                w = slice(halves[0], halves[-1] + 1)
+                nc.scalar.activation(out=half_sq[i][:].rearrange("p (w m e) -> p w m e", w=2, e=2)[:, w],
+                                     in_=f[i // 4][:, i % 4, :].rearrange("p (w e m) -> p w m e", w=2, e=2)[:, w],
                                      func=ACT.Square, scale=0.5 ** 0.5)
+
+            def units(tile, lo, hi):
+                return tile[:].rearrange("p (w m e) -> p m w e", w=2, e=2)[:, lo // 4:hi // 4]
+
+            def quads(plain):
+                return plain.rearrange("p (m w e) -> p m w e", w=2, e=2)
 
             def slope_back(i, h):
                 if i not in u:
@@ -188,23 +196,20 @@ def tile_incrementalpredictivecodingupdate_kernel(tc, x1, x2, w1_bytes, w1_scale
 
             def state_gpsimd(i):
                 first = rest_cols(i)
-                nc.gpsimd.tensor_tensor(out=x_new_tile(i)[:, first:], in0=half_x[i][:], in1=u[i][:, first:], op=ALU.subtract)
+                nc.gpsimd.tensor_tensor(out=quads(x_new_tile(i)[:, first:]), in0=quads(half_x[i][:]), in1=units(u[i], first, Q), op=ALU.subtract)
 
-            def state_vector(i, lo, hi):
-                nc.vector.scalar_tensor_tensor(out=x_new_tile(i)[:, lo:hi], in0=x1s[i][:, lo:hi], scalar=0.5, in1=u[i][:, lo:hi],
-                                               op0=ALU.mult, op1=ALU.subtract)
-
-            def lay_x(i, lo, hi, b, stop=True):
+            def lay_x(i, lo, hi, b):
                 sums[i, lo] = bank(b, [P, hi - lo])
-                nc.tensor.matmul(sums[i, lo][:], lhsT=minus_half[:], rhs=x1s[i][:, lo:hi], start=True, stop=stop)
+                nc.tensor.matmul(sums[i, lo][:], lhsT=plus_half[:], rhs=x1s[i][:, lo:hi], start=True, stop=True)
 
             def state_from_bank(i, lo, hi):
-                nc.vector.scalar_tensor_tensor(out=x_new_tile(i)[:, lo:hi], in0=sums[i, lo][:], scalar=-1.0, in1=u[i][:, lo:hi],
-                                               op0=ALU.mult, op1=ALU.subtract)
+                nc.vector.tensor_tensor(out=quads(x_new_tile(i)[:, lo:hi]), in0=quads(sums[i, lo][:]), in1=units(u[i], lo, hi), op=ALU.subtract)
 
             def state_sum(i, lo, hi, b):
-                lay_x(i, lo, hi, b, stop=False)
-                nc.tensor.matmul(sums[i, lo][:], lhsT=ident[:], rhs=u[i][:, lo:hi], start=False, stop=True)
+                sums[i, lo] = bank(b, [P, hi - lo])
+                nc.tensor.matmul(sums[i, lo][:], lhsT=minus_half[:], rhs=x1s[i][:, lo:hi], start=True, stop=False)
+                nc.tensor.matmul(quads(sums[i, lo][:]).rearrange("p m w e -> p w m e"), lhsT=ident[:],
+                                 rhs=units(u[i], lo, hi).rearrange("p m w e -> p w m e"), start=False, stop=True)
 
             def state_sum_out(i, lo, hi):
                 nc.scalar.activation(out=x_new_tile(i)[:, lo:hi], in_=sums[i, lo][:], func=ACT.Copy, scale=-1.0)
@@ -284,6 +289,7 @@ def tile_incrementalpredictivecodingupdate_kernel(tc, x1, x2, w1_bytes, w1_scale
             nc.sync.dma_start(out=x2s[1][:], in_=x2_rows[1])
             make_identity(nc, ident[:])
             nc.vector.tensor_copy(out=ident_bf16[:], in_=ident[:])
+            nc.vector.tensor_scalar(out=plus_half[:], in0=ident[:], scalar1=0.5, scalar2=None, op0=ALU.mult)
             nc.vector.tensor_scalar(out=minus_half[:], in0=ident[:], scalar1=-0.5, scalar2=None, op0=ALU.mult)
 
             w1_planes = work.tile([P, 4, 2, R], BF16, name="planes")
@@ -317,8 +323,12 @@ def tile_incrementalpredictivecodingupdate_kernel(tc, x1, x2, w1_bytes, w1_scale
                 matmul_mu(i, 2 + i)
 
             v1_inter = gpsimd_tile(Q)
-            interleave(gpsimd_copy, v1_inter[:], v1s[:])
+            v1_out = v1_inter[:].rearrange("p (w m e) t -> p w m t e", w=2, e=2)
+            v1_in = v1s[:].rearrange("p t (m w e) -> p w m t e", w=2, e=2)
+            for w in (0, 1):
+                gpsimd_copy(v1_out[:, w, V1_SCALAR_QUADS:], v1_in[:, w, V1_SCALAR_QUADS:])
             fa_planes = work.tile([P, 4, Q], BF16, name="planes")
+            nc.scalar.copy(out=v1_out[:, :, :V1_SCALAR_QUADS], in_=v1_in[:, :, :V1_SCALAR_QUADS])
             for t in range(4):
                 plane_fa1(t)
             gain_g(4)
@@ -441,13 +451,16 @@ def tile_incrementalpredictivecodingupdate_kernel(tc, x1, x2, w1_bytes, w1_scale
 
             state_gpsimd(5)
             state_sum_out(5, 0, rest_cols(5))
+            lay_x(6, HALF, Q, 4)
+            lay_x(7, 0, HALF, 2)
             slope_back(6, 0)
             slope_back(6, 1)
+            lay_x(7, HALF, Q, 5)
             slope_back(7, 0)
             store_x(5)
             state_from_bank(6, 0, HALF)
             store_x(6, 0, HALF)
             slope_back(7, 1)
             for i, h in ((6, 1), (7, 0), (7, 1)):
-                state_vector(i, h * HALF, (h + 1) * HALF)
+                state_from_bank(i, h * HALF, (h + 1) * HALF)
                 store_x(i, h * HALF, (h + 1) * HALF)

@@ -18,15 +18,14 @@ ACT = mybir.ActivationFunctionType
 
 HALF = 512
 PIECE = 256
-REST_ON_TENSOR = (0, 5)
-REST_ON_VECTOR = (1, 2, 3, 4)
-GP_COLS = {0: 608, 1: 736, 2: 736, 3: 736, 4: 736, 5: 640}
+GP_COLS = {0: 704, 1: 704, 2: 704, 3: 704, 4: 512, 5: 512, 6: 384}
+SUM_COLS = {4: 256, 5: 192, 6: 128}
 GATE = 64
 EC_FIRST_COLS = 256
 W1_VECTOR_COLS = 96
 V1_SCALAR_QUADS = 24
 EC_GPSIMD_COLS = 224
-EC_SCALAR_COLS = 160
+EC_SCALAR_COLS = R - EC_GPSIMD_COLS
 
 
 def tile_incrementalpredictivecodingupdate_kernel(tc, x1, x2, w1_bytes, w1_scale, v1, g, pi2, a, c, out_0, out_1):
@@ -56,7 +55,6 @@ def tile_incrementalpredictivecodingupdate_kernel(tc, x1, x2, w1_bytes, w1_scale
         ident = keep.tile([P, P], F32, name="ident")
         minus_half = keep.tile([P, P], BF16, name="minus_half")
         plus_half = keep.tile([P, P], BF16, name="plus_half")
-        ident_bf16 = keep.tile([P, P], BF16, name="ident_bf16")
 
         f = [keep.tile([P, 4, Q], F32, name="f%d" % k) for k in (0, 1)]
         eps = [keep.tile([P, 4, R], F32, name="eps%d" % k) for k in (0, 1)]
@@ -171,11 +169,11 @@ def tile_incrementalpredictivecodingupdate_kernel(tc, x1, x2, w1_bytes, w1_scale
             def quads(plain):
                 return plain.rearrange("p (m w e) -> p m w e", w=2, e=2)
 
-            def slope_back(i, h):
+            def slope_back(i, h, part=slice(0, HALF)):
                 if i not in u:
                     u[i] = work.tile([P, Q], F32, name="u", bufs=4)
-                cols = slice(h * HALF, (h + 1) * HALF)
-                nc.vector.scalar_tensor_tensor(out=u[i][:, cols], in0=half_sq[i][:, cols], scalar=0.5, in1=back[i, h][:],
+                cols = slice(h * HALF + part.start, h * HALF + part.stop)
+                nc.vector.scalar_tensor_tensor(out=u[i][:, cols], in0=half_sq[i][:, cols], scalar=0.5, in1=back[i, h][:, part],
                                                op0=ALU.subtract, op1=ALU.mult)
 
             def x_new_tile(i):
@@ -186,11 +184,14 @@ def tile_incrementalpredictivecodingupdate_kernel(tc, x1, x2, w1_bytes, w1_scale
             def rest_cols(i):
                 return Q - GP_COLS[i]
 
+            def vector_cols(i):
+                return rest_cols(i) - SUM_COLS.get(i, 0)
+
             def halve_x(i, lo=0, hi=None):
                 first = rest_cols(i)
                 hi = hi or Q - first
                 if lo == 0:
-                    half_x[i] = work.tile([P, Q - first], BF16, name="half_x", bufs=4)
+                    half_x[i] = work.tile([P, Q - first], BF16, name="half_x", bufs=5)
                 nc.vector.tensor_scalar(out=half_x[i][:, lo:hi], in0=x1s[i][:, first + lo:first + hi],
                                         scalar1=0.5, scalar2=None, op0=ALU.mult)
 
@@ -227,11 +228,15 @@ def tile_incrementalpredictivecodingupdate_kernel(tc, x1, x2, w1_bytes, w1_scale
             def quant_fa(n):
                 quantize(fa_codes, fa_exps, 2 * n * PIECE, fa_piece[n][:].rearrange("p k q t -> p (k q t)"))
 
+            def chunk(e):
+                n, h = divmod(e, 2)
+                return n // 2 * 4 + n % 2 + 2 * h
+
             def scale_fa0(e, planes=range(4)):
                 if e not in fa_scaled:
                     fa_scaled[e] = bank(6 + e % 2, [P, 4, P])
                 for t in planes:
-                    nc.tensor.matmul(fa_scaled[e][:, t, :], lhsT=a_diag[:, t, :], rhs=f[0][:, t, e * P:(e + 1) * P], start=True, stop=True)
+                    nc.tensor.matmul(fa_scaled[e][:, t, :], lhsT=a_diag[:, t, :], rhs=f[0][:, t, chunk(e) * P:(chunk(e) + 1) * P], start=True, stop=True)
 
             def scale_fa0_out(e):
                 nc.scalar.copy(out=fa_tile(e // 2)[:, 0, e % 2 * P:(e % 2 + 1) * P, :], in_=fa_scaled[e][:].rearrange("p t q -> p q t"))
@@ -240,7 +245,8 @@ def tile_incrementalpredictivecodingupdate_kernel(tc, x1, x2, w1_bytes, w1_scale
                 nc.scalar.activation(out=fa_planes[:, t, :], in_=f[1][:, t, :], func=ACT.Copy, scale=a_f32[:, 1, t:t + 1])
 
             def interleave_fa1(n):
-                interleave(nc.scalar.copy, fa_tile(n)[:, 1], fa_planes[:, :, n * PIECE:(n + 1) * PIECE])
+                planes = fa_planes[:].rearrange("p t (w h k c i) -> p w k h c t i", w=2, h=2, k=2, i=4)[:, n // 2, n % 2]
+                nc.scalar.copy(out=fa_tile(n)[:, 1].rearrange("p (h c i) t -> p h c t i", h=2, i=4), in_=planes)
 
             def gain_c(engine, k, lo, hi, gain):
                 if engine is nc.gpsimd:
@@ -256,19 +262,21 @@ def tile_incrementalpredictivecodingupdate_kernel(tc, x1, x2, w1_bytes, w1_scale
                 lo = EC_FIRST_COLS if k == 0 else 0
                 quantize(ec_codes, ec_exps, k * R + lo, ec_inter[k, lo][:, lo:].rearrange("p r t -> p (r t)"))
 
-            def matmul_dw(m, b):
-                dw[m] = bank(b, [P, R])
+            def matmul_dw(e, b):
+                dw[e] = bank(b, [P, R])
                 for k in (0, 1):
-                    mx_pass(dw[m][:], (fa_codes, fa_exps), (m // 2 * 2 + k) * PIECE + m % 2 * P, (ec_codes, ec_exps), k * R, k == 0, k == 1)
+                    mx_pass(dw[e][:], (fa_codes, fa_exps), (e // 2 * 2 + k) * PIECE + e % 2 * P, (ec_codes, ec_exps), k * R, k == 0, k == 1)
 
-            def store_dw(m):
-                if m % 2 == 0:
-                    dw_out[m // 4] = work.tile([P, 2, 2, R], F32, name="fg_inter", bufs=2, align_bytes=64)
-                pair = dw_out[m // 4][:, m % 2]
-                for e in (0, 1):
-                    nc.scalar.activation(out=pair[:, e, :].rearrange("p (m u) -> p m u", u=4),
-                                         in_=dw[m + 2 * e][:].rearrange("p (u m) -> p m u", u=4), func=ACT.Copy, scale=1.0 / 32.0)
-                nc.sync.dma_start(out=dw_rows[m % 2][:, m // 2:m // 2 + 2, :], in_=pair)
+            def empty_dw(n):
+                if n % 2 == 0:
+                    dw_out[n // 2] = work.tile([P, 2, 2, R], F32, name="fg_inter", bufs=2, align_bytes=64)
+                pair = dw_out[n // 2][:, n % 2]
+                for h in (0, 1):
+                    nc.scalar.activation(out=pair[:, h, :].rearrange("p (m u) -> p m u", u=4),
+                                         in_=dw[2 * n + h][:].rearrange("p (u m) -> p m u", u=4), func=ACT.Copy, scale=1.0 / 32.0)
+
+            def store_dw(n):
+                nc.sync.dma_start(out=dw_rows[n % 2][:, n // 2 * 2:n // 2 * 2 + 2, :], in_=dw_out[n // 2][:, n % 2])
 
             def load_gain(gain, values):
                 nc.sync.dma_start(out=gain[:], in_=values.rearrange("(g p t) -> p g t", p=P, t=4))
@@ -288,7 +296,6 @@ def tile_incrementalpredictivecodingupdate_kernel(tc, x1, x2, w1_bytes, w1_scale
             load_gain(c_gain, c)
             nc.sync.dma_start(out=x2s[1][:], in_=x2_rows[1])
             make_identity(nc, ident[:])
-            nc.vector.tensor_copy(out=ident_bf16[:], in_=ident[:])
             nc.vector.tensor_scalar(out=plus_half[:], in0=ident[:], scalar1=0.5, scalar2=None, op0=ALU.mult)
             nc.vector.tensor_scalar(out=minus_half[:], in0=ident[:], scalar1=-0.5, scalar2=None, op0=ALU.mult)
 
@@ -383,84 +390,99 @@ def tile_incrementalpredictivecodingupdate_kernel(tc, x1, x2, w1_bytes, w1_scale
             for t in range(4):
                 nc.scalar.activation(out=ec_planes[:, t, :], in_=eps[1][:, t, R - EC_SCALAR_COLS:], func=ACT.Copy, scale=c_f32[:, t:t + 1])
             scale_fa0_out(5)
-            c_bank = bank(3, [P, 4])
-            nc.tensor.matmul(c_bank[:], lhsT=ident_bf16[:], rhs=c_gain[:, 1, :], start=True, stop=True)
             turn_eps(3, 4)
+            turn_eps(4, 3)
             quant_ep(0, 3)
             matmul_back(0, (5, 0))
             matmul_back(1, (1, 2))
             scale_fa0(6)
-            scale_fa0(7)
             quant_fa(0)
             quant_ec(0)
             quant_fa(1)
 
             gain_c(nc.gpsimd, 1, 0, EC_GPSIMD_COLS, c_gain[:, 1, :])
-            gain_c(nc.vector, 1, EC_GPSIMD_COLS, R - EC_SCALAR_COLS, c_bank[:])
             interleave(nc.scalar.copy, ec_inter[1, 0][:, R - EC_SCALAR_COLS:], ec_planes[:])
-            square(2)
+            gain_pi(3)
+            turn_eps(5, 4)
+            scale_fa0(7)
             scale_fa0_out(6)
+            square(2)
             scale_fa0_out(7)
-            interleave_fa1(3)
-            for j in range(6):
+            def back_banks(i):
+                return (0, 3) if i == 2 else ((5, 0), (1, 2))[i % 2]
+
+            def dw_pair(n):
+                matmul_dw(2 * n, 6)
+                matmul_dw(2 * n + 1, 7 if n else 5)
+
+            for j in range(4):
                 if j >= 1:
                     state_gpsimd(j - 1)
+                gain_pi(j + 4)
                 if j == 1:
-                    state_sum_out(0, 0, rest_cols(0))
-                    square(3, (0,))
-                if j < 5:
-                    gain_pi(j + 3)
-                if j < 2:
-                    turn_eps(j + 4, 4)
-                if 1 <= j <= 4:
-                    m = (j - 1) // 2 * 4 + (j - 1) % 2
-                    matmul_dw(m, 6)
-                    matmul_dw(m + 2, 7)
-                    if j in (2, 3):
-                        turn_eps(j + 4, 4)
-                    matmul_back(j + 1, ((5, 0), (1, 2))[(j + 1) % 2])
-                if j == 5:
-                    matmul_back(6, (5, 0))
-                    matmul_back(7, (6, 7))
-                    lay_x(6, 0, HALF, 3)
+                    dw_pair(0)
+                    empty_dw(0)
+                if j in (1, 2):
+                    turn_eps(j + 5, 4)
                 slope_back(j, 0)
-                if j - 1 in REST_ON_VECTOR:
-                    state_from_bank(j - 1, 0, rest_cols(j - 1))
+                if j >= 1:
+                    state_from_bank(j - 1, 0, vector_cols(j - 1))
                 slope_back(j, 1)
                 if j >= 1:
+                    matmul_back(j + 1, back_banks(j + 1))
+                    dw_pair(j)
                     store_x(j - 1)
-                if j in REST_ON_TENSOR:
-                    state_sum(j, 0, rest_cols(j), {0: 3, 5: 1}[j])
-                else:
-                    lay_x(j, 0, rest_cols(j), 4 if j == 4 else 3)
-                if 1 <= j <= 4:
-                    store_dw(m)
-                    square(j + 2, (1,))
-                    square(j + 3, (0,) if j < 4 else (0, 1))
+                    if j == 1:
+                        store_dw(0)
+                        interleave_fa1(3)
+                    empty_dw(j)
+                    store_dw(j)
+                    square(j + 2, (0, 1) if j == 1 else (1,))
+                    if j < 3:
+                        square(j + 3, (0,))
+                lay_x(j, 0, vector_cols(j), 5 if j == 1 else 3)
                 if j == 0:
                     quant_ec(1)
+                    quant_ep(3, 1)
                     halve_x(0, GP_COLS[0] - GATE, GP_COLS[0])
                 if j in (1, 2):
                     quant_fa(j + 1)
                 if j == 3:
-                    halve_x(5)
-                if 1 <= j <= 4:
+                    for i in (6, 5, 4):
+                        halve_x(i)
+                if j >= 1:
                     halve_x(j)
-                if j < 5:
-                    quant_ep(j + 3, 1)
+                quant_ep(j + 4, 1)
 
-            state_gpsimd(5)
-            state_sum_out(5, 0, rest_cols(5))
-            lay_x(6, HALF, Q, 4)
-            lay_x(7, 0, HALF, 2)
-            slope_back(6, 0)
-            slope_back(6, 1)
-            lay_x(7, HALF, Q, 5)
-            slope_back(7, 0)
-            store_x(5)
-            state_from_bank(6, 0, HALF)
-            store_x(6, 0, HALF)
-            slope_back(7, 1)
-            for i, h in ((6, 1), (7, 0), (7, 1)):
-                state_from_bank(i, h * HALF, (h + 1) * HALF)
-                store_x(i, h * HALF, (h + 1) * HALF)
+            square(6)
+            matmul_back(5, back_banks(5))
+            lay_x(4, 0, vector_cols(4), 4)
+            for j in (4, 5, 6):
+                state_gpsimd(j - 1)
+                slope_back(j, 0)
+                state_from_bank(j - 1, 0, vector_cols(j - 1))
+                slope_back(j, 1)
+                if j > 4:
+                    state_sum_out(j - 1, vector_cols(j - 1), rest_cols(j - 1))
+                    if j == 5:
+                        square(7)
+                store_x(j - 1)
+                if j < 6:
+                    lay_x(j + 1, 0, vector_cols(j + 1), 3 + j % 2)
+                state_sum(j, vector_cols(j), rest_cols(j), 6 + j % 2)
+                if j < 6:
+                    matmul_back(j + 2, back_banks(j))
+            state_gpsimd(6)
+            lay_x(7, 0, HALF, 3)
+            lay_x(7, HALF, Q, 7)
+            state_sum_out(6, vector_cols(6), rest_cols(6))
+            parts = [(h, part) for part in (slice(0, HALF // 2), slice(HALF // 2, HALF)) for h in (0, 1)]
+            slope_back(7, *parts[0])
+            slope_back(7, *parts[1])
+            state_from_bank(6, 0, vector_cols(6))
+            store_x(6)
+            slope_back(7, *parts[2])
+            slope_back(7, *parts[3])
+            for h in (0, 1):
+                state_from_bank(7, h * HALF, (h + 1) * HALF)
+                store_x(7, h * HALF, (h + 1) * HALF)

@@ -429,17 +429,18 @@ def tile_incrementalpredictivecodingupdate_kernel(tc, x1, x2, w1_bytes, w1_scale
                     state_from_bank(j - 1, 0, vector_cols(j - 1))
                 slope_back(j, 1)
                 if j >= 1:
-                    matmul_back(j + 1, back_banks(j + 1))
+                    if j != 2:
+                        matmul_back(j + 1, back_banks(j + 1))
                     dw_pair(j)
+                    if j == 2:
+                        matmul_back(3, back_banks(3))
                     store_x(j - 1)
                     if j == 1:
                         store_dw(0)
                         interleave_fa1(3)
                     empty_dw(j)
                     store_dw(j)
-                    square(j + 2, (0, 1) if j == 1 else (1,))
-                    if j < 3:
-                        square(j + 3, (0,))
+                    square(j + 2)
                 lay_x(j, 0, vector_cols(j), 5 if j == 1 else 3)
                 if j == 0:
                     quant_ec(1)

@@ -18,13 +18,13 @@ ACT = mybir.ActivationFunctionType
 
 HALF = 512
 PIECE = 256
-GP_COLS = {0: 704, 1: 704, 2: 704, 3: 704, 4: 512, 5: 512, 6: 384}
-SUM_COLS = {4: 256, 5: 192, 6: 128}
+GP_COLS = {0: 704, 1: 704, 2: 704, 3: 576, 4: 448, 5: 448, 6: 320}
+SUM_COLS = {4: 320, 5: 256, 6: 192}
 GATE = 64
 EC_FIRST_COLS = 256
 W1_VECTOR_COLS = 96
 V1_SCALAR_QUADS = 24
-EC_GPSIMD_COLS = 224
+EC_GPSIMD_COLS = 216
 EC_SCALAR_COLS = R - EC_GPSIMD_COLS
 
 
@@ -206,9 +206,11 @@ def tile_incrementalpredictivecodingupdate_kernel(tc, x1, x2, w1_bytes, w1_scale
             def state_from_bank(i, lo, hi):
                 nc.vector.tensor_tensor(out=quads(x_new_tile(i)[:, lo:hi]), in0=quads(sums[i, lo][:]), in1=units(u[i], lo, hi), op=ALU.subtract)
 
-            def state_sum(i, lo, hi, b):
+            def open_sum(i, lo, hi, b):
                 sums[i, lo] = bank(b, [P, hi - lo])
                 nc.tensor.matmul(sums[i, lo][:], lhsT=minus_half[:], rhs=x1s[i][:, lo:hi], start=True, stop=False)
+
+            def close_sum(i, lo, hi):
                 nc.tensor.matmul(quads(sums[i, lo][:]).rearrange("p m w e -> p w m e"), lhsT=ident[:],
                                  rhs=units(u[i], lo, hi).rearrange("p m w e -> p w m e"), start=False, stop=True)
 
@@ -458,32 +460,36 @@ def tile_incrementalpredictivecodingupdate_kernel(tc, x1, x2, w1_bytes, w1_scale
             square(6)
             matmul_back(5, back_banks(5))
             lay_x(4, 0, vector_cols(4), 4)
+            matmul_back(6, (6, 7))
+            square(7, (0,))
             for j in (4, 5, 6):
                 state_gpsimd(j - 1)
                 slope_back(j, 0)
+                open_sum(j, vector_cols(j), rest_cols(j), {4: 5, 5: 1, 6: 6}[j])
                 state_from_bank(j - 1, 0, vector_cols(j - 1))
                 slope_back(j, 1)
                 if j > 4:
                     state_sum_out(j - 1, vector_cols(j - 1), rest_cols(j - 1))
                     if j == 5:
-                        square(7)
+                        square(7, (1,))
                 store_x(j - 1)
-                if j < 6:
-                    lay_x(j + 1, 0, vector_cols(j + 1), 3 + j % 2)
-                state_sum(j, vector_cols(j), rest_cols(j), 6 + j % 2)
-                if j < 6:
-                    matmul_back(j + 2, back_banks(j))
+                if j == 4:
+                    lay_x(5, 0, vector_cols(5), 3)
+                if j == 5:
+                    matmul_back(7, (0, 4))
+                close_sum(j, vector_cols(j), rest_cols(j))
+                if j == 5:
+                    lay_x(6, 0, vector_cols(6), 2)
             state_gpsimd(6)
             lay_x(7, 0, HALF, 3)
             lay_x(7, HALF, Q, 7)
             state_sum_out(6, vector_cols(6), rest_cols(6))
             parts = [(h, part) for part in (slice(0, HALF // 2), slice(HALF // 2, HALF)) for h in (0, 1)]
             slope_back(7, *parts[0])
-            slope_back(7, *parts[1])
             state_from_bank(6, 0, vector_cols(6))
             store_x(6)
-            slope_back(7, *parts[2])
-            slope_back(7, *parts[3])
+            for h, part in parts[1:]:
+                slope_back(7, h, part)
             for h in (0, 1):
                 state_from_bank(7, h * HALF, (h + 1) * HALF)
                 store_x(7, h * HALF, (h + 1) * HALF)

@@ -18,13 +18,13 @@ ACT = mybir.ActivationFunctionType
 
 HALF = 512
 PIECE = 256
-GP_COLS = {0: 704, 1: 704, 2: 704, 3: 576, 4: 448, 5: 448, 6: 320}
-SUM_COLS = {4: 320, 5: 256, 6: 192}
+GP_COLS = {0: 736, 1: 640, 2: 736, 3: 640, 4: 448, 5: 448, 6: 320}
+SUM_COLS = {1: 384, 4: 320, 5: 256, 6: 192}
 GATE = 64
 EC_FIRST_COLS = 256
-W1_VECTOR_COLS = 96
-V1_SCALAR_QUADS = 24
-EC_GPSIMD_COLS = 216
+W1_VECTOR_COLS = 64
+V1_SCALAR_QUADS = 48
+EC_GPSIMD_COLS = 224
 EC_SCALAR_COLS = R - EC_GPSIMD_COLS
 
 
@@ -134,7 +134,8 @@ def tile_incrementalpredictivecodingupdate_kernel(tc, x1, x2, w1_bytes, w1_scale
                                         in0=x2s[i // 4][:, i % 4, :].rearrange("p (b j u) -> p b u j", u=4, j=4),
                                         in1=mu[i][:].rearrange("p (b j u) -> p b u j", u=4, j=4), op=ALU.subtract)
 
-            eps_turned, ep_inter, back, half_sq, u, half_x, x_new, sums = {}, {}, {}, {}, {}, {}, {}, {}
+            eps_turned, back, half_sq, u, half_x, x_new, sums = {}, {}, {}, {}, {}, {}, {}
+            ep_inter = work.tile([P, 8, P, 4], BF16, name="ep_inter", align_bytes=64)
 
             def turn_eps(i, b):
                 eps_turned[i] = bank(b, [P, 4, P])
@@ -142,13 +143,11 @@ def tile_incrementalpredictivecodingupdate_kernel(tc, x1, x2, w1_bytes, w1_scale
                     nc.tensor.transpose(eps_turned[i][:, t, :], eps[i // 4][:, i % 4, t * P:(t + 1) * P], ident[:])
 
             def gain_pi(i):
-                if i // 4 not in ep_inter:
-                    ep_inter[i // 4] = work.tile([P, 4, P, 4], BF16, name="ep_inter", bufs=2, align_bytes=64)
-                nc.vector.tensor_tensor(out=ep_inter[i // 4][:, i % 4], in0=eps_turned[i][:].rearrange("p t n -> p n t"),
+                nc.vector.tensor_tensor(out=ep_inter[:, i], in0=eps_turned[i][:].rearrange("p t n -> p n t"),
                                         in1=pi_gain[:].unsqueeze(1).to_broadcast([P, P, 4]), op=ALU.mult)
 
             def quant_ep(i, tiles):
-                quantize(ep_codes, ep_exps, P * i, ep_inter[i // 4][:, i % 4:i % 4 + tiles].rearrange("p i n t -> p (i n t)"))
+                quantize(ep_codes, ep_exps, P * i, ep_inter[:, i:i + tiles].rearrange("p i n t -> p (i n t)"))
 
             def matmul_back(i, banks):
                 for h in (0, 1):
@@ -187,13 +186,14 @@ def tile_incrementalpredictivecodingupdate_kernel(tc, x1, x2, w1_bytes, w1_scale
             def vector_cols(i):
                 return rest_cols(i) - SUM_COLS.get(i, 0)
 
-            def halve_x(i, lo=0, hi=None):
+            def halve_x(i, lo=0, hi=None, engine=nc.vector):
                 first = rest_cols(i)
                 hi = hi or Q - first
                 if lo == 0:
-                    half_x[i] = work.tile([P, Q - first], BF16, name="half_x", bufs=5)
-                nc.vector.tensor_scalar(out=half_x[i][:, lo:hi], in0=x1s[i][:, first + lo:first + hi],
-                                        scalar1=0.5, scalar2=None, op0=ALU.mult)
+                    half_x[i] = work.tile([P, Q - first], BF16, name="half_x%d" % (i % 2 if i < 4 else i))
+                add_zero = {} if engine is nc.vector else dict(op1=ALU.add)
+                engine.tensor_scalar(out=half_x[i][:, lo:hi], in0=x1s[i][:, first + lo:first + hi],
+                                     scalar1=0.5, scalar2=0.0 if add_zero else None, op0=ALU.mult, **add_zero)
 
             def state_gpsimd(i):
                 first = rest_cols(i)
@@ -336,6 +336,7 @@ def tile_incrementalpredictivecodingupdate_kernel(tc, x1, x2, w1_bytes, w1_scale
             v1_in = v1s[:].rearrange("p t (m w e) -> p w m t e", w=2, e=2)
             for w in (0, 1):
                 gpsimd_copy(v1_out[:, w, V1_SCALAR_QUADS:], v1_in[:, w, V1_SCALAR_QUADS:])
+            halve_x(5, engine=nc.gpsimd)
             fa_planes = work.tile([P, 4, Q], BF16, name="planes")
             nc.scalar.copy(out=v1_out[:, :, :V1_SCALAR_QUADS], in_=v1_in[:, :, :V1_SCALAR_QUADS])
             for t in range(4):
@@ -427,12 +428,16 @@ def tile_incrementalpredictivecodingupdate_kernel(tc, x1, x2, w1_bytes, w1_scale
                 if j in (1, 2):
                     turn_eps(j + 5, 4)
                 slope_back(j, 0)
-                if j >= 1:
+                if j >= 1 and vector_cols(j - 1):
                     state_from_bank(j - 1, 0, vector_cols(j - 1))
                 slope_back(j, 1)
+                if j - 1 in SUM_COLS:
+                    state_sum_out(j - 1, 0, rest_cols(j - 1))
                 if j >= 1:
                     if j != 2:
                         matmul_back(j + 1, back_banks(j + 1))
+                    if j == 3:
+                        lay_x(3, 0, vector_cols(3), 4)
                     dw_pair(j)
                     if j == 2:
                         matmul_back(3, back_banks(3))
@@ -440,48 +445,55 @@ def tile_incrementalpredictivecodingupdate_kernel(tc, x1, x2, w1_bytes, w1_scale
                     if j == 1:
                         store_dw(0)
                         interleave_fa1(3)
+                    if j == 3:
+                        square(5, (0,))
                     empty_dw(j)
                     store_dw(j)
-                    square(j + 2)
-                lay_x(j, 0, vector_cols(j), 5 if j == 1 else 3)
+                    square(j + 2, (1,) if j == 3 else (0, 1))
+                if j in SUM_COLS:
+                    open_sum(j, 0, rest_cols(j), 5 if j == 1 else 3)
+                    close_sum(j, 0, rest_cols(j))
+                elif j < 3:
+                    lay_x(j, 0, vector_cols(j), 5 if j == 1 else 3)
                 if j == 0:
                     quant_ec(1)
-                    quant_ep(3, 1)
                     halve_x(0, GP_COLS[0] - GATE, GP_COLS[0])
                 if j in (1, 2):
                     quant_fa(j + 1)
                 if j == 3:
-                    for i in (6, 5, 4):
+                    for i in (6, 4):
                         halve_x(i)
                 if j >= 1:
                     halve_x(j)
-                quant_ep(j + 4, 1)
+                quant_ep(*((j + 4, 1) if j else (3, 2)))
 
             square(6)
             matmul_back(5, back_banks(5))
-            lay_x(4, 0, vector_cols(4), 4)
+            if vector_cols(4):
+                lay_x(4, 0, vector_cols(4), 3)
             matmul_back(6, (6, 7))
             square(7, (0,))
             for j in (4, 5, 6):
                 state_gpsimd(j - 1)
                 slope_back(j, 0)
                 open_sum(j, vector_cols(j), rest_cols(j), {4: 5, 5: 1, 6: 6}[j])
-                state_from_bank(j - 1, 0, vector_cols(j - 1))
+                if vector_cols(j - 1):
+                    state_from_bank(j - 1, 0, vector_cols(j - 1))
                 slope_back(j, 1)
-                if j > 4:
+                if j - 1 in SUM_COLS:
                     state_sum_out(j - 1, vector_cols(j - 1), rest_cols(j - 1))
-                    if j == 5:
-                        square(7, (1,))
-                store_x(j - 1)
-                if j == 4:
-                    lay_x(5, 0, vector_cols(5), 3)
                 if j == 5:
-                    matmul_back(7, (0, 4))
+                    square(7, (1,))
+                store_x(j - 1)
+                if j == 4 and vector_cols(5):
+                    lay_x(5, 0, vector_cols(5), 4)
+                if j == 5:
+                    matmul_back(7, (0, 3))
                 close_sum(j, vector_cols(j), rest_cols(j))
                 if j == 5:
                     lay_x(6, 0, vector_cols(6), 2)
             state_gpsimd(6)
-            lay_x(7, 0, HALF, 3)
+            lay_x(7, 0, HALF, 4)
             lay_x(7, HALF, Q, 7)
             state_sum_out(6, vector_cols(6), rest_cols(6))
             parts = [(h, part) for part in (slice(0, HALF // 2), slice(HALF // 2, HALF)) for h in (0, 1)]

@@ -42,7 +42,7 @@ def tile_incrementalpredictivecodingupdate_kernel(tc, x1, x2, w1_bytes, w1_scale
         psum = ctx.enter_context(tc.psum_pool(name="psum", bufs=1))
 
         x1s = [keep.tile([P, Q], BF16, name="x1s%d" % i) for i in range(8)]
-        x2s = [keep.tile([P, 4, R], BF16, name="x2s%d" % k) for k in (0, 1)]
+        x2s = [work.tile([P, 4, R], BF16, name="x2s", bufs=2) for k in (0, 1)]
         w1b = [keep.tile([P, 4, R], U8, name="w1b%d" % k) for k in (0, 1)]
         v1s = keep.tile([P, 4, Q], BF16, name="v1s")
         w1_gain = keep.tile([P, 2, 4], F32, name="w1_gain")
@@ -56,7 +56,7 @@ def tile_incrementalpredictivecodingupdate_kernel(tc, x1, x2, w1_bytes, w1_scale
         minus_half = keep.tile([P, P], BF16, name="minus_half")
         plus_half = keep.tile([P, P], BF16, name="plus_half")
 
-        f = [keep.tile([P, 4, Q], F32, name="f%d" % k) for k in (0, 1)]
+        f = [work.tile([P, Q], F32, name="f", bufs=8) for i in range(8)]
         eps = [keep.tile([P, 4, R], F32, name="eps%d" % k) for k in (0, 1)]
         w1_codes = keep.tile([P, 2 * R], U32, name="w1_codes", align_bytes=256)
         w1_exps = keep.tile([P, 2 * R], U8, name="w1_exps", align_bytes=256)
@@ -102,7 +102,7 @@ def tile_incrementalpredictivecodingupdate_kernel(tc, x1, x2, w1_bytes, w1_scale
                                         scalar1=w1_gain[:, k, t:t + 1], scalar2=None, op0=ALU.mult)
 
             def tanh(i):
-                nc.scalar.activation(out=f[i // 4][:, i % 4, :].rearrange("p (u b j) -> p b u j", u=4, j=4),
+                nc.scalar.activation(out=f[i][:].rearrange("p (u b j) -> p b u j", u=4, j=4),
                                      in_=x1s[i][:].rearrange("p (b j u) -> p b u j", u=4, j=4), func=ACT.Tanh)
 
             f_turned, fg_inter, mu = {}, {}, {}
@@ -111,7 +111,7 @@ def tile_incrementalpredictivecodingupdate_kernel(tc, x1, x2, w1_bytes, w1_scale
                 for k in (0, 1):
                     turned = bank(b + k, [P, 4, P])
                     for t in range(4):
-                        nc.tensor.transpose(turned[:, t, :], f[i // 4][:, i % 4, (2 * t + k) * P:(2 * t + k + 1) * P], ident[:])
+                        nc.tensor.transpose(turned[:, t, :], f[i][:, (2 * t + k) * P:(2 * t + k + 1) * P], ident[:])
                     f_turned[i, k] = turned
 
             def gain_g(i, passes=(0, 1)):
@@ -159,7 +159,7 @@ def tile_incrementalpredictivecodingupdate_kernel(tc, x1, x2, w1_bytes, w1_scale
                     half_sq[i] = work.tile([P, Q], F32, name="half_sq", bufs=4)
                 w = slice(halves[0], halves[-1] + 1)
                 nc.scalar.activation(out=half_sq[i][:].rearrange("p (w m e) -> p w m e", w=2, e=2)[:, w],
-                                     in_=f[i // 4][:, i % 4, :].rearrange("p (w e m) -> p w m e", w=2, e=2)[:, w],
+                                     in_=f[i][:].rearrange("p (w e m) -> p w m e", w=2, e=2)[:, w],
                                      func=ACT.Square, scale=0.5 ** 0.5)
 
             def units(tile, lo, hi):
@@ -170,14 +170,14 @@ def tile_incrementalpredictivecodingupdate_kernel(tc, x1, x2, w1_bytes, w1_scale
 
             def slope_back(i, h, part=slice(0, HALF)):
                 if i not in u:
-                    u[i] = work.tile([P, Q], F32, name="u", bufs=4)
+                    u[i] = work.tile([P, Q], F32, name="u", bufs=4) if i < 6 else work.tile([P, Q], F32, name="x2s", bufs=2)
                 cols = slice(h * HALF + part.start, h * HALF + part.stop)
                 nc.vector.scalar_tensor_tensor(out=u[i][:, cols], in0=half_sq[i][:, cols], scalar=0.5, in1=back[i, h][:, part],
                                                op0=ALU.subtract, op1=ALU.mult)
 
             def x_new_tile(i):
                 if i not in x_new:
-                    x_new[i] = work.tile([P, Q], F32, name="x_new", bufs=4)
+                    x_new[i] = work.tile([P, Q], F32, name="x_new", bufs=4) if i < 4 else work.tile([P, Q], F32, name="f", bufs=8)
                 return x_new[i]
 
             def rest_cols(i):
@@ -238,13 +238,13 @@ def tile_incrementalpredictivecodingupdate_kernel(tc, x1, x2, w1_bytes, w1_scale
                 if e not in fa_scaled:
                     fa_scaled[e] = bank(6 + e % 2, [P, 4, P])
                 for t in planes:
-                    nc.tensor.matmul(fa_scaled[e][:, t, :], lhsT=a_diag[:, t, :], rhs=f[0][:, t, chunk(e) * P:(chunk(e) + 1) * P], start=True, stop=True)
+                    nc.tensor.matmul(fa_scaled[e][:, t, :], lhsT=a_diag[:, t, :], rhs=f[t][:, chunk(e) * P:(chunk(e) + 1) * P], start=True, stop=True)
 
             def scale_fa0_out(e):
                 nc.scalar.copy(out=fa_tile(e // 2)[:, 0, e % 2 * P:(e % 2 + 1) * P, :], in_=fa_scaled[e][:].rearrange("p t q -> p q t"))
 
             def plane_fa1(t):
-                nc.scalar.activation(out=fa_planes[:, t, :], in_=f[1][:, t, :], func=ACT.Copy, scale=a_f32[:, 1, t:t + 1])
+                nc.scalar.activation(out=fa_planes[:, t, :], in_=f[4 + t][:], func=ACT.Copy, scale=a_f32[:, 1, t:t + 1])
 
             def interleave_fa1(n):
                 planes = fa_planes[:].rearrange("p t (w h k c i) -> p w k h c t i", w=2, h=2, k=2, i=4)[:, n // 2, n % 2]
@@ -406,6 +406,8 @@ def tile_incrementalpredictivecodingupdate_kernel(tc, x1, x2, w1_bytes, w1_scale
             gain_c(nc.gpsimd, 1, 0, EC_GPSIMD_COLS, c_gain[:, 1, :])
             interleave(nc.scalar.copy, ec_inter[1, 0][:, R - EC_SCALAR_COLS:], ec_planes[:])
             gain_pi(3)
+            gain_pi(4)
+            lay_x(0, 0, vector_cols(0), 3)
             turn_eps(5, 4)
             scale_fa0(7)
             scale_fa0_out(6)
@@ -421,7 +423,8 @@ def tile_incrementalpredictivecodingupdate_kernel(tc, x1, x2, w1_bytes, w1_scale
             for j in range(4):
                 if j >= 1:
                     state_gpsimd(j - 1)
-                gain_pi(j + 4)
+                if j >= 1:
+                    gain_pi(j + 4)
                 if j == 1:
                     dw_pair(0)
                     empty_dw(0)
@@ -434,10 +437,10 @@ def tile_incrementalpredictivecodingupdate_kernel(tc, x1, x2, w1_bytes, w1_scale
                 if j - 1 in SUM_COLS:
                     state_sum_out(j - 1, 0, rest_cols(j - 1))
                 if j >= 1:
-                    if j != 2:
-                        matmul_back(j + 1, back_banks(j + 1))
                     if j == 3:
                         lay_x(3, 0, vector_cols(3), 4)
+                    if j != 2:
+                        matmul_back(j + 1, back_banks(j + 1))
                     dw_pair(j)
                     if j == 2:
                         matmul_back(3, back_banks(3))
@@ -453,8 +456,8 @@ def tile_incrementalpredictivecodingupdate_kernel(tc, x1, x2, w1_bytes, w1_scale
                 if j in SUM_COLS:
                     open_sum(j, 0, rest_cols(j), 5 if j == 1 else 3)
                     close_sum(j, 0, rest_cols(j))
-                elif j < 3:
-                    lay_x(j, 0, vector_cols(j), 5 if j == 1 else 3)
+                elif j == 2:
+                    lay_x(2, 0, vector_cols(2), 3)
                 if j == 0:
                     quant_ec(1)
                     halve_x(0, GP_COLS[0] - GATE, GP_COLS[0])
@@ -468,10 +471,8 @@ def tile_incrementalpredictivecodingupdate_kernel(tc, x1, x2, w1_bytes, w1_scale
                 quant_ep(*((j + 4, 1) if j else (3, 2)))
 
             square(6)
+            lay_x(4, 0, vector_cols(4), 3)
             matmul_back(5, back_banks(5))
-            if vector_cols(4):
-                lay_x(4, 0, vector_cols(4), 3)
-            matmul_back(6, (6, 7))
             square(7, (0,))
             for j in (4, 5, 6):
                 state_gpsimd(j - 1)
@@ -485,16 +486,17 @@ def tile_incrementalpredictivecodingupdate_kernel(tc, x1, x2, w1_bytes, w1_scale
                 if j == 5:
                     square(7, (1,))
                 store_x(j - 1)
-                if j == 4 and vector_cols(5):
+                if j == 4:
                     lay_x(5, 0, vector_cols(5), 4)
+                    matmul_back(6, (6, 7))
                 if j == 5:
                     matmul_back(7, (0, 3))
                 close_sum(j, vector_cols(j), rest_cols(j))
                 if j == 5:
                     lay_x(6, 0, vector_cols(6), 2)
             state_gpsimd(6)
-            lay_x(7, 0, HALF, 4)
             lay_x(7, HALF, Q, 7)
+            lay_x(7, 0, HALF, 4)
             state_sum_out(6, vector_cols(6), rest_cols(6))
             parts = [(h, part) for part in (slice(0, HALF // 2), slice(HALF // 2, HALF)) for h in (0, 1)]
             slope_back(7, *parts[0])

@@ -23,7 +23,7 @@ SUM_COLS = {1: 384, 4: 320, 5: 256, 6: 192}
 GATE = 64
 EC_FIRST_COLS = 256
 W1_VECTOR_COLS = 64
-V1_SCALAR_QUADS = 48
+V1_SCALAR_QUADS = 24
 EC_GPSIMD_COLS = 224
 EC_SCALAR_COLS = R - EC_GPSIMD_COLS
 
@@ -336,7 +336,6 @@ def tile_incrementalpredictivecodingupdate_kernel(tc, x1, x2, w1_bytes, w1_scale
             v1_in = v1s[:].rearrange("p t (m w e) -> p w m t e", w=2, e=2)
             for w in (0, 1):
                 gpsimd_copy(v1_out[:, w, V1_SCALAR_QUADS:], v1_in[:, w, V1_SCALAR_QUADS:])
-            halve_x(5, engine=nc.gpsimd)
             fa_planes = work.tile([P, 4, Q], BF16, name="planes")
             nc.scalar.copy(out=v1_out[:, :, :V1_SCALAR_QUADS], in_=v1_in[:, :, :V1_SCALAR_QUADS])
             for t in range(4):
@@ -437,34 +436,35 @@ def tile_incrementalpredictivecodingupdate_kernel(tc, x1, x2, w1_bytes, w1_scale
                 if j - 1 in SUM_COLS:
                     state_sum_out(j - 1, 0, rest_cols(j - 1))
                 if j >= 1:
-                    if j == 3:
-                        lay_x(3, 0, vector_cols(3), 4)
+                    if j >= 2:
+                        lay_x(j, 0, vector_cols(j), j + 1)
                     if j != 2:
                         matmul_back(j + 1, back_banks(j + 1))
                     dw_pair(j)
-                    if j == 2:
+                    if j == 1:
                         matmul_back(3, back_banks(3))
                     store_x(j - 1)
                     if j == 1:
                         store_dw(0)
                         interleave_fa1(3)
+                    if j >= 2:
+                        square(j + 2, (0,))
                     if j == 3:
-                        square(5, (0,))
+                        store_dw(2)
                     empty_dw(j)
-                    store_dw(j)
-                    square(j + 2, (1,) if j == 3 else (0, 1))
+                    if j != 2:
+                        store_dw(j)
+                    square(j + 2, (1,) if j >= 2 else (0, 1))
                 if j in SUM_COLS:
                     open_sum(j, 0, rest_cols(j), 5 if j == 1 else 3)
                     close_sum(j, 0, rest_cols(j))
-                elif j == 2:
-                    lay_x(2, 0, vector_cols(2), 3)
                 if j == 0:
                     quant_ec(1)
                     halve_x(0, GP_COLS[0] - GATE, GP_COLS[0])
                 if j in (1, 2):
                     quant_fa(j + 1)
                 if j == 3:
-                    for i in (6, 4):
+                    for i in (6, 5, 4):
                         halve_x(i)
                 if j >= 1:
                     halve_x(j)
@@ -473,7 +473,6 @@ def tile_incrementalpredictivecodingupdate_kernel(tc, x1, x2, w1_bytes, w1_scale
             square(6)
             lay_x(4, 0, vector_cols(4), 3)
             matmul_back(5, back_banks(5))
-            square(7, (0,))
             for j in (4, 5, 6):
                 state_gpsimd(j - 1)
                 slope_back(j, 0)
@@ -484,7 +483,7 @@ def tile_incrementalpredictivecodingupdate_kernel(tc, x1, x2, w1_bytes, w1_scale
                 if j - 1 in SUM_COLS:
                     state_sum_out(j - 1, vector_cols(j - 1), rest_cols(j - 1))
                 if j == 5:
-                    square(7, (1,))
+                    square(7)
                 store_x(j - 1)
                 if j == 4:
                     lay_x(5, 0, vector_cols(5), 4)

@@ -23,7 +23,7 @@ SUM_COLS = {1: 384, 4: 320, 5: 256, 6: 192}
 GATE = 64
 EC_FIRST_COLS = 256
 W1_VECTOR_COLS = 64
-V1_SCALAR_QUADS = 24
+V1_SCALAR_QUADS = 48
 EC_GPSIMD_COLS = 224
 EC_SCALAR_COLS = R - EC_GPSIMD_COLS
 
@@ -336,6 +336,7 @@ def tile_incrementalpredictivecodingupdate_kernel(tc, x1, x2, w1_bytes, w1_scale
             v1_in = v1s[:].rearrange("p t (m w e) -> p w m t e", w=2, e=2)
             for w in (0, 1):
                 gpsimd_copy(v1_out[:, w, V1_SCALAR_QUADS:], v1_in[:, w, V1_SCALAR_QUADS:])
+            halve_x(5, engine=nc.gpsimd)
             fa_planes = work.tile([P, 4, Q], BF16, name="planes")
             nc.scalar.copy(out=v1_out[:, :, :V1_SCALAR_QUADS], in_=v1_in[:, :, :V1_SCALAR_QUADS])
             for t in range(4):
@@ -464,7 +465,7 @@ def tile_incrementalpredictivecodingupdate_kernel(tc, x1, x2, w1_bytes, w1_scale
                 if j in (1, 2):
                     quant_fa(j + 1)
                 if j == 3:
-                    for i in (6, 5, 4):
+                    for i in (6, 4):
                         halve_x(i)
                 if j >= 1:
                     halve_x(j)

from contextlib import ExitStack

import concourse.mybir as mybir
from concourse.masks import make_identity

N, Q, R = 1024, 1024, 512
P = 128
FLOPS = 3 * 2 * N * Q * R

F32 = mybir.dt.float32
BF16 = mybir.dt.bfloat16
U32 = mybir.dt.uint32
U8 = mybir.dt.uint8
FP8 = mybir.dt.float8_e4m3fn
FP8X4 = mybir.dt.float8_e4m3fn_x4
ALU = mybir.AluOpType
ACT = mybir.ActivationFunctionType

HALF = 512
PIECE = 256
GP_COLS = {0: 736, 1: 640, 2: 736, 3: 640, 4: 448, 5: 448, 6: 320}
SUM_COLS = {1: 384, 4: 320, 5: 256, 6: 192}
GATE = 64
EC_FIRST_COLS = 256
W1_VECTOR_COLS = 64
V1_SCALAR_QUADS = 48
EC_GPSIMD_COLS = 224
EC_SCALAR_COLS = R - EC_GPSIMD_COLS


def tile_incrementalpredictivecodingupdate_kernel(tc, x1, x2, w1_bytes, w1_scale, v1, g, pi2, a, c, out_0, out_1):
    nc = tc.nc
    x1_rows = x1.rearrange("(g p t) q -> g p t q", p=P, t=4)
    x2_rows = x2.rearrange("(g p t) r -> g p t r", p=P, t=4)
    w1_rows = w1_bytes.rearrange("(g p t) r -> g p t r", p=P, t=4)
    x_new_rows = out_0.rearrange("(g p t) q -> g p t q", p=P, t=4)
    dw_rows = out_1.rearrange("(g p u) r -> g p u r", g=2, u=4)

    with ExitStack() as ctx:
        keep = ctx.enter_context(tc.tile_pool(name="keep", bufs=1))
        work = ctx.enter_context(tc.tile_pool(name="work", bufs=1))
        psum = ctx.enter_context(tc.psum_pool(name="psum", bufs=1))

        x1s = [keep.tile([P, Q], BF16, name="x1s%d" % i) for i in range(8)]
        x2s = [work.tile([P, 4, R], BF16, name="x2s", bufs=2) for k in (0, 1)]
        w1b = [keep.tile([P, 4, R], U8, name="w1b%d" % k) for k in (0, 1)]
        v1s = keep.tile([P, 4, Q], BF16, name="v1s")
        w1_gain = keep.tile([P, 2, 4], F32, name="w1_gain")
        g_gain = keep.tile([P, 2, 4], BF16, name="g_gain")
        a_gain = keep.tile([P, 2, 4], BF16, name="a_gain")
        c_gain = keep.tile([P, 2, 4], BF16, name="c_gain")
        pi_gain = keep.tile([P, 4], BF16, name="pi_gain")
        a_f32 = keep.tile([P, 2, 4], F32, name="a_f32")
        c_f32 = keep.tile([P, 4], F32, name="c_f32")
        ident = keep.tile([P, P], F32, name="ident")
        minus_half = keep.tile([P, P], BF16, name="minus_half")
        plus_half = keep.tile([P, P], BF16, name="plus_half")

        f = [work.tile([P, Q], F32, name="f", bufs=8) for i in range(8)]
        eps = [keep.tile([P, 4, R], F32, name="eps%d" % k) for k in (0, 1)]
        w1_codes = keep.tile([P, 2 * R], U32, name="w1_codes", align_bytes=256)
        w1_exps = keep.tile([P, 2 * R], U8, name="w1_exps", align_bytes=256)
        v1_codes = keep.tile([P, Q], U32, name="v1_codes", align_bytes=256)
        v1_exps = keep.tile([P, Q], U8, name="v1_exps", align_bytes=256)
        fg_codes = keep.tile([P, 8 * 2 * P], U32, name="fg_codes", align_bytes=256)
        fg_exps = keep.tile([P, 8 * 2 * P], U8, name="fg_exps", align_bytes=256)
        ep_codes = keep.tile([P, 8 * P], U32, name="ep_codes", align_bytes=256)
        ep_exps = keep.tile([P, 8 * P], U8, name="ep_exps", align_bytes=256)
        fa_codes = keep.tile([P, 2 * Q], U32, name="fa_codes", align_bytes=256)
        fa_exps = keep.tile([P, 2 * Q], U8, name="fa_exps", align_bytes=256)
        ec_codes = keep.tile([P, 2 * R], U32, name="ec_codes", align_bytes=256)
        ec_exps = keep.tile([P, 2 * R], U8, name="ec_exps", align_bytes=256)
        a_diag = keep.tile([P, 4, P], F32, name="a_diag")

        def bank(b, shape):
            return psum.tile(shape, F32, name="bank%d" % b)

        def gpsimd_tile(columns):
            return work.tile([P, columns, 4], BF16, name="gpsimd_out", align_bytes=64)

        def quantize(codes, exps, first, inter):
            cols = slice(first, first + inter.shape[1] // 4)
            nc.vector.quantize_mx(out=codes[:, cols].bitcast(FP8X4), scales=exps[:, cols], in_=inter)

        def mx_pass(out, lhs, lhs_first, rhs, rhs_first, start, stop):
            lhs_cols, rhs_cols = slice(lhs_first, lhs_first + P), slice(rhs_first, rhs_first + HALF)
            nc.tensor.matmul_mx(out=out, lhsT=lhs[0][:, lhs_cols].bitcast(FP8X4), lhsT_scale=lhs[1][:, lhs_cols],
                                rhs=rhs[0][:, rhs_cols].bitcast(FP8X4), rhs_scale=rhs[1][:, rhs_cols], start=start, stop=stop)

        def interleave(copy, out, planes):
            copy(out=out.rearrange("p (c i) t -> p c t i", i=4), in_=planes.rearrange("p t (c i) -> p c t i", i=4))

        def gpsimd_copy(out, in_):
            nc.gpsimd.tensor_scalar(out=out, in0=in_, scalar1=1.0, scalar2=0.0, op0=ALU.mult, op1=ALU.add)

        with tc.manual_schedule():
            def load_x1(i):
                nc.sync.dma_start(out=x1s[i][:], in_=x1_rows[i // 4][:, i % 4, :])

            def widen_w1(k, t):
                nc.vector.tensor_scalar(out=w1_planes[:, t, k, :], in0=w1b[k][:, t, :].bitcast(FP8),
                                        scalar1=w1_gain[:, k, t:t + 1], scalar2=None, op0=ALU.mult)

            def tanh(i):
                nc.scalar.activation(out=f[i][:].rearrange("p (u b j) -> p b u j", u=4, j=4),
                                     in_=x1s[i][:].rearrange("p (b j u) -> p b u j", u=4, j=4), func=ACT.Tanh)

            f_turned, fg_inter, mu = {}, {}, {}

            def turn_f(i, b):
                for k in (0, 1):
                    turned = bank(b + k, [P, 4, P])
                    for t in range(4):
                        nc.tensor.transpose(turned[:, t, :], f[i][:, (2 * t + k) * P:(2 * t + k + 1) * P], ident[:])
                    f_turned[i, k] = turned

            def gain_g(i, passes=(0, 1)):
                if i // 4 not in fg_inter:
                    fg_inter[i // 4] = work.tile([P, 4, 2, P, 4], BF16, name="fg_inter", bufs=2, align_bytes=64)
                for k in passes:
                    nc.vector.tensor_tensor(out=fg_inter[i // 4][:, i % 4, k], in0=f_turned[i, k][:].rearrange("p t n -> p n t"),
                                            in1=g_gain[:, k, :].unsqueeze(1).to_broadcast([P, P, 4]), op=ALU.mult)

            def quant_fg(i, tiles):
                quantize(fg_codes, fg_exps, 2 * P * i, fg_inter[i // 4][:, i % 4:i % 4 + tiles].rearrange("p i k n t -> p (i k n t)"))

            def matmul_mu(i, b):
                mu[i] = bank(b, [P, R])
                for k in (0, 1):
                    mx_pass(mu[i][:], (fg_codes, fg_exps), (2 * i + k) * P, (w1_codes, w1_exps), k * R, k == 0, k == 1)

            def error(i):
                nc.vector.tensor_tensor(out=eps[i // 4][:, i % 4, :].rearrange("p (u b j) -> p b u j", u=4, j=4),
                                        in0=x2s[i // 4][:, i % 4, :].rearrange("p (b j u) -> p b u j", u=4, j=4),
                                        in1=mu[i][:].rearrange("p (b j u) -> p b u j", u=4, j=4), op=ALU.subtract)

            eps_turned, back, half_sq, u, half_x, x_new, sums = {}, {}, {}, {}, {}, {}, {}
            ep_inter = work.tile([P, 8, P, 4], BF16, name="ep_inter", align_bytes=64)

            def turn_eps(i, b):
                eps_turned[i] = bank(b, [P, 4, P])
                for t in range(4):
                    nc.tensor.transpose(eps_turned[i][:, t, :], eps[i // 4][:, i % 4, t * P:(t + 1) * P], ident[:])

            def gain_pi(i):
                nc.vector.tensor_tensor(out=ep_inter[:, i], in0=eps_turned[i][:].rearrange("p t n -> p n t"),
                                        in1=pi_gain[:].unsqueeze(1).to_broadcast([P, P, 4]), op=ALU.mult)

            def quant_ep(i, tiles):
                quantize(ep_codes, ep_exps, P * i, ep_inter[:, i:i + tiles].rearrange("p i n t -> p (i n t)"))

            def matmul_back(i, banks):
                for h in (0, 1):
                    back[i, h] = bank(banks[h], [P, HALF])
                    mx_pass(back[i, h][:], (ep_codes, ep_exps), i * P, (v1_codes, v1_exps), h * HALF, True, True)

            def square(i, halves=(0, 1)):
                if i not in half_sq:
                    half_sq[i] = work.tile([P, Q], F32, name="half_sq", bufs=4)
                w = slice(halves[0], halves[-1] + 1)
                nc.scalar.activation(out=half_sq[i][:].rearrange("p (w m e) -> p w m e", w=2, e=2)[:, w],
                                     in_=f[i][:].rearrange("p (w e m) -> p w m e", w=2, e=2)[:, w],
                                     func=ACT.Square, scale=0.5 ** 0.5)

            def units(tile, lo, hi):
                return tile[:].rearrange("p (w m e) -> p m w e", w=2, e=2)[:, lo // 4:hi // 4]

            def quads(plain):
                return plain.rearrange("p (m w e) -> p m w e", w=2, e=2)

            def slope_back(i, h, part=slice(0, HALF)):
                if i not in u:
                    u[i] = work.tile([P, Q], F32, name="u", bufs=4) if i < 6 else work.tile([P, Q], F32, name="x2s", bufs=2)
                cols = slice(h * HALF + part.start, h * HALF + part.stop)
                nc.vector.scalar_tensor_tensor(out=u[i][:, cols], in0=half_sq[i][:, cols], scalar=0.5, in1=back[i, h][:, part],
                                               op0=ALU.subtract, op1=ALU.mult)

            def x_new_tile(i):
                if i not in x_new:
                    x_new[i] = work.tile([P, Q], F32, name="x_new", bufs=4) if i < 4 else work.tile([P, Q], F32, name="f", bufs=8)
                return x_new[i]

            def rest_cols(i):
                return Q - GP_COLS[i]

            def vector_cols(i):
                return rest_cols(i) - SUM_COLS.get(i, 0)

            def halve_x(i, lo=0, hi=None, engine=nc.vector):
                first = rest_cols(i)
                hi = hi or Q - first
                if lo == 0:
                    half_x[i] = work.tile([P, Q - first], BF16, name="half_x%d" % (i % 2 if i < 4 else i))
                add_zero = {} if engine is nc.vector else dict(op1=ALU.add)
                engine.tensor_scalar(out=half_x[i][:, lo:hi], in0=x1s[i][:, first + lo:first + hi],
                                     scalar1=0.5, scalar2=0.0 if add_zero else None, op0=ALU.mult, **add_zero)

            def state_gpsimd(i):
                first = rest_cols(i)
                nc.gpsimd.tensor_tensor(out=quads(x_new_tile(i)[:, first:]), in0=quads(half_x[i][:]), in1=units(u[i], first, Q), op=ALU.subtract)

            def lay_x(i, lo, hi, b):
                sums[i, lo] = bank(b, [P, hi - lo])
                nc.tensor.matmul(sums[i, lo][:], lhsT=plus_half[:], rhs=x1s[i][:, lo:hi], start=True, stop=True)

            def state_from_bank(i, lo, hi):
                nc.vector.tensor_tensor(out=quads(x_new_tile(i)[:, lo:hi]), in0=quads(sums[i, lo][:]), in1=units(u[i], lo, hi), op=ALU.subtract)

            def open_sum(i, lo, hi, b):
                sums[i, lo] = bank(b, [P, hi - lo])
                nc.tensor.matmul(sums[i, lo][:], lhsT=minus_half[:], rhs=x1s[i][:, lo:hi], start=True, stop=False)

            def close_sum(i, lo, hi):
                nc.tensor.matmul(quads(sums[i, lo][:]).rearrange("p m w e -> p w m e"), lhsT=ident[:],
                                 rhs=units(u[i], lo, hi).rearrange("p m w e -> p w m e"), start=False, stop=True)

            def state_sum_out(i, lo, hi):
                nc.scalar.activation(out=x_new_tile(i)[:, lo:hi], in_=sums[i, lo][:], func=ACT.Copy, scale=-1.0)

            def store_x(i, lo=0, hi=Q):
                nc.sync.dma_start(out=x_new_rows[i // 4][:, i % 4, lo:hi], in_=x_new[i][:, lo:hi])

            fa_piece, ec_inter, fa_scaled, dw, dw_out = {}, {}, {}, {}, {}

            def fa_tile(n):
                if n not in fa_piece:
                    fa_piece[n] = work.tile([P, 2, PIECE, 4], BF16, name="fa_piece", bufs=3, align_bytes=64)
                return fa_piece[n]

            def quant_fa(n):
                quantize(fa_codes, fa_exps, 2 * n * PIECE, fa_piece[n][:].rearrange("p k q t -> p (k q t)"))

            def chunk(e):
                n, h = divmod(e, 2)
                return n // 2 * 4 + n % 2 + 2 * h

            def scale_fa0(e, planes=range(4)):
                if e not in fa_scaled:
                    fa_scaled[e] = bank(6 + e % 2, [P, 4, P])
                for t in planes:
                    nc.tensor.matmul(fa_scaled[e][:, t, :], lhsT=a_diag[:, t, :], rhs=f[t][:, chunk(e) * P:(chunk(e) + 1) * P], start=True, stop=True)

            def scale_fa0_out(e):
                nc.scalar.copy(out=fa_tile(e // 2)[:, 0, e % 2 * P:(e % 2 + 1) * P, :], in_=fa_scaled[e][:].rearrange("p t q -> p q t"))

            def plane_fa1(t):
                nc.scalar.activation(out=fa_planes[:, t, :], in_=f[4 + t][:], func=ACT.Copy, scale=a_f32[:, 1, t:t + 1])

            def interleave_fa1(n):
                planes = fa_planes[:].rearrange("p t (w h k c i) -> p w k h c t i", w=2, h=2, k=2, i=4)[:, n // 2, n % 2]
                nc.scalar.copy(out=fa_tile(n)[:, 1].rearrange("p (h c i) t -> p h c t i", h=2, i=4), in_=planes)

            def gain_c(engine, k, lo, hi, gain):
                if engine is nc.gpsimd:
                    ec_inter[k, lo] = gpsimd_tile(R)
                engine.tensor_tensor(out=ec_inter[k, lo if k == 0 else 0][:, lo:hi].rearrange("p (c i) t -> p c t i", i=4),
                                     in0=eps[k][:, :, lo:hi].rearrange("p t (c i) -> p c t i", i=4),
                                     in1=gain.unsqueeze(1).unsqueeze(3).to_broadcast([P, (hi - lo) // 4, 4, 4]), op=ALU.mult)

            def quant_ec_first():
                quantize(ec_codes, ec_exps, 0, ec_inter[0, 0][:, :EC_FIRST_COLS].rearrange("p r t -> p (r t)"))

            def quant_ec(k):
                lo = EC_FIRST_COLS if k == 0 else 0
                quantize(ec_codes, ec_exps, k * R + lo, ec_inter[k, lo][:, lo:].rearrange("p r t -> p (r t)"))

            def matmul_dw(e, b):
                dw[e] = bank(b, [P, R])
                for k in (0, 1):
                    mx_pass(dw[e][:], (fa_codes, fa_exps), (e // 2 * 2 + k) * PIECE + e % 2 * P, (ec_codes, ec_exps), k * R, k == 0, k == 1)

            def empty_dw(n):
                if n % 2 == 0:
                    dw_out[n // 2] = work.tile([P, 2, 2, R], F32, name="fg_inter", bufs=2, align_bytes=64)
                pair = dw_out[n // 2][:, n % 2]
                for h in (0, 1):
                    nc.scalar.activation(out=pair[:, h, :].rearrange("p (m u) -> p m u", u=4),
                                         in_=dw[2 * n + h][:].rearrange("p (u m) -> p m u", u=4), func=ACT.Copy, scale=1.0 / 32.0)

            def store_dw(n):
                nc.sync.dma_start(out=dw_rows[n % 2][:, n // 2 * 2:n // 2 * 2 + 2, :], in_=dw_out[n // 2][:, n % 2])

            def load_gain(gain, values):
                nc.sync.dma_start(out=gain[:], in_=values.rearrange("(g p t) -> p g t", p=P, t=4))

            nc.scalar.dma_start(out=w1_gain[:], in_=w1_scale.rearrange("(g p t) o -> p g (t o)", p=P, t=4))
            for k in (0, 1):
                nc.sync.dma_start(out=w1b[k][:], in_=w1_rows[k])
                load_x1(k)
            load_gain(g_gain, g)
            load_x1(2)
            load_gain(a_gain, a)
            for i in range(3, 8):
                load_x1(i)
            nc.sync.dma_start(out=v1s[:], in_=v1.rearrange("(p t) q -> p t q", t=4))
            nc.sync.dma_start(out=x2s[0][:], in_=x2_rows[0])
            nc.sync.dma_start(out=pi_gain[:], in_=pi2.rearrange("(p t) -> p t", t=4))
            load_gain(c_gain, c)
            nc.sync.dma_start(out=x2s[1][:], in_=x2_rows[1])
            make_identity(nc, ident[:])
            nc.vector.tensor_scalar(out=plus_half[:], in0=ident[:], scalar1=0.5, scalar2=None, op0=ALU.mult)
            nc.vector.tensor_scalar(out=minus_half[:], in0=ident[:], scalar1=-0.5, scalar2=None, op0=ALU.mult)

            w1_planes = work.tile([P, 4, 2, R], BF16, name="planes")
            for k in (0, 1):
                for t in range(4):
                    if (k, t) == (1, 3):
                        halve_x(0, 0, GP_COLS[0] - GATE)
                    widen_w1(k, t)
            w1_inter = gpsimd_tile(2 * R)
            planes = w1_planes[:].rearrange("p t k r -> p t (k r)")
            interleave(nc.vector.tensor_copy, w1_inter[:, :W1_VECTOR_COLS], planes[:, :, :W1_VECTOR_COLS])
            interleave(gpsimd_copy, w1_inter[:, W1_VECTOR_COLS:], planes[:, :, W1_VECTOR_COLS:])
            for i in range(3):
                tanh(i)
            nc.scalar.copy(out=a_f32[:], in_=a_gain[:])
            tanh(3)
            for i in range(4):
                turn_f(i, (6, 0, 2, 4)[i])
                gain_g(i)
            for t in range(4):
                nc.scalar.activation(out=a_diag[:, t, :], in_=ident[:], func=ACT.Copy, scale=a_f32[:, 0, t:t + 1])
            scale_fa0(0)
            for i in range(4, 8):
                tanh(i)
            turn_f(4, 0)
            scale_fa0_out(0)
            quant_fg(0, 2)
            quantize(w1_codes, w1_exps, 0, w1_inter[:].rearrange("p r t -> p (r t)"))
            quant_fg(2, 2)
            for i in range(4):
                matmul_mu(i, 2 + i)

            v1_inter = gpsimd_tile(Q)
            v1_out = v1_inter[:].rearrange("p (w m e) t -> p w m t e", w=2, e=2)
            v1_in = v1s[:].rearrange("p t (m w e) -> p w m t e", w=2, e=2)
            for w in (0, 1):
                gpsimd_copy(v1_out[:, w, V1_SCALAR_QUADS:], v1_in[:, w, V1_SCALAR_QUADS:])
            halve_x(5, engine=nc.gpsimd)
            fa_planes = work.tile([P, 4, Q], BF16, name="planes")
            nc.scalar.copy(out=v1_out[:, :, :V1_SCALAR_QUADS], in_=v1_in[:, :, :V1_SCALAR_QUADS])
            for t in range(4):
                plane_fa1(t)
            gain_g(4)
            turn_f(5, 0)
            for i in range(4):
                error(i)
            turn_f(6, 2)
            scale_fa0(1)
            turn_f(7, 4)
            scale_fa0(2)
            gain_g(5)
            gain_g(6, (0,))
            scale_fa0_out(1)
            quant_fg(4, 1)
            matmul_mu(4, 0)
            turn_eps(0, 2)
            quantize(v1_codes, v1_exps, 0, v1_inter[:].rearrange("p q t -> p (q t)"))
            quant_fg(5, 1)
            matmul_mu(5, 1)
            scale_fa0(3)

            gain_c(nc.gpsimd, 0, 0, EC_FIRST_COLS, c_gain[:, 0, :])
            interleave_fa1(0)
            scale_fa0_out(2)
            interleave_fa1(1)
            nc.scalar.copy(out=c_f32[:], in_=c_gain[:, 1, :])
            square(0)
            scale_fa0_out(3)
            gain_g(6, (1,))
            error(4)
            gain_pi(0)
            turn_eps(1, 3)
            turn_eps(2, 0)
            gain_g(7)
            quant_fg(6, 1)
            matmul_mu(6, 2)
            quant_ec_first()
            quant_fg(7, 1)
            matmul_mu(7, 4)
            scale_fa0(4)
            gain_c(nc.gpsimd, 0, EC_FIRST_COLS, R, c_gain[:, 0, :])
            square(1)
            error(5)
            scale_fa0(5)
            gain_pi(1)
            error(6)
            gain_pi(2)
            error(7)
            interleave_fa1(2)
            scale_fa0_out(4)
            ec_planes = work.tile([P, 4, EC_SCALAR_COLS], BF16, name="ec_planes")
            for t in range(4):
                nc.scalar.activation(out=ec_planes[:, t, :], in_=eps[1][:, t, R - EC_SCALAR_COLS:], func=ACT.Copy, scale=c_f32[:, t:t + 1])
            scale_fa0_out(5)
            turn_eps(3, 4)
            turn_eps(4, 3)
            quant_ep(0, 3)
            matmul_back(0, (5, 0))
            matmul_back(1, (1, 2))
            scale_fa0(6)
            quant_fa(0)
            quant_ec(0)
            quant_fa(1)

            gain_c(nc.gpsimd, 1, 0, EC_GPSIMD_COLS, c_gain[:, 1, :])
            interleave(nc.scalar.copy, ec_inter[1, 0][:, R - EC_SCALAR_COLS:], ec_planes[:])
            gain_pi(3)
            gain_pi(4)
            lay_x(0, 0, vector_cols(0), 3)
            turn_eps(5, 4)
            scale_fa0(7)
            scale_fa0_out(6)
            square(2)
            scale_fa0_out(7)
            def back_banks(i):
                return (0, 3) if i == 2 else ((5, 0), (1, 2))[i % 2]

            def dw_pair(n):
                matmul_dw(2 * n, 6)
                matmul_dw(2 * n + 1, 7 if n else 5)

            for j in range(4):
                if j >= 1:
                    state_gpsimd(j - 1)
                if j >= 1:
                    gain_pi(j + 4)
                if j == 1:
                    dw_pair(0)
                    empty_dw(0)
                if j in (1, 2):
                    turn_eps(j + 5, 4)
                slope_back(j, 0)
                if j >= 1 and vector_cols(j - 1):
                    state_from_bank(j - 1, 0, vector_cols(j - 1))
                slope_back(j, 1)
                if j - 1 in SUM_COLS:
                    state_sum_out(j - 1, 0, rest_cols(j - 1))
                if j >= 1:
                    if j >= 2:
                        lay_x(j, 0, vector_cols(j), j + 1)
                    if j != 2:
                        matmul_back(j + 1, back_banks(j + 1))
                    dw_pair(j)
                    if j == 1:
                        matmul_back(3, back_banks(3))
                    store_x(j - 1)
                    if j == 1:
                        store_dw(0)
                        interleave_fa1(3)
                    if j >= 2:
                        square(j + 2, (0,))
                    if j == 3:
                        store_dw(2)
                    empty_dw(j)
                    if j != 2:
                        store_dw(j)
                    square(j + 2, (1,) if j >= 2 else (0, 1))
                if j in SUM_COLS:
                    open_sum(j, 0, rest_cols(j), 5 if j == 1 else 3)
                    close_sum(j, 0, rest_cols(j))
                if j == 0:
                    quant_ec(1)
                    halve_x(0, GP_COLS[0] - GATE, GP_COLS[0])
                if j in (1, 2):
                    quant_fa(j + 1)
                if j == 3:
                    for i in (6, 4):
                        halve_x(i)
                if j >= 1:
                    halve_x(j)
                quant_ep(*((j + 4, 1) if j else (3, 2)))

            square(6)
            lay_x(4, 0, vector_cols(4), 3)
            matmul_back(5, back_banks(5))
            for j in (4, 5, 6):
                state_gpsimd(j - 1)
                slope_back(j, 0)
                open_sum(j, vector_cols(j), rest_cols(j), {4: 5, 5: 1, 6: 6}[j])
                if vector_cols(j - 1):
                    state_from_bank(j - 1, 0, vector_cols(j - 1))
                slope_back(j, 1)
                if j - 1 in SUM_COLS:
                    state_sum_out(j - 1, vector_cols(j - 1), rest_cols(j - 1))
                if j == 5:
                    square(7)
                store_x(j - 1)
                if j == 4:
                    lay_x(5, 0, vector_cols(5), 4)
                    matmul_back(6, (6, 7))
                if j == 5:
                    matmul_back(7, (0, 3))
                close_sum(j, vector_cols(j), rest_cols(j))
                if j == 5:
                    lay_x(6, 0, vector_cols(6), 2)
            state_gpsimd(6)
            lay_x(7, HALF, Q, 7)
            lay_x(7, 0, HALF, 4)
            state_sum_out(6, vector_cols(6), rest_cols(6))
            parts = [(h, part) for part in (slice(0, HALF // 2), slice(HALF // 2, HALF)) for h in (0, 1)]
            slope_back(7, *parts[0])
            state_from_bank(6, 0, vector_cols(6))
            store_x(6)
            for h, part in parts[1:]:
                slope_back(7, h, part)
            for h in (0, 1):
                state_from_bank(7, h * HALF, (h + 1) * HALF)
                store_x(7, h * HALF, (h + 1) * HALF)
